import numpy as np
import ml_dtypes


def mxq(x, axis, fmt="e4m3"):
    dtype, down = {"e4m3": (ml_dtypes.float8_e4m3fn, 7), "e5m2": (ml_dtypes.float8_e5m2, 14)}[fmt]
    v = np.moveaxis(np.asarray(x, np.float32).astype(ml_dtypes.bfloat16).astype(np.float64), axis, -1)
    blocks = v.reshape(v.shape[:-1] + (-1, 32))
    amax = np.abs(blocks).max(-1, keepdims=True)
    byte = np.maximum(np.where(amax > 0, np.frexp(amax)[1] - 1 + 127, 0) - down, 1)
    scale = np.exp2(byte - 127.0)
    codes = (blocks / scale).astype(np.float32).astype(dtype).astype(np.float64)
    return np.moveaxis((codes * scale).reshape(v.shape), -1, axis)


WIDE = False


def mx_kscale(k):
    if not WIDE:
        return np.ones(k)
    levels = np.array([10, -10, 5, -5, 0])
    if k % 512:
        return np.exp2(np.random.permutation(np.resize(levels, k // 32))).repeat(32)
    a = np.empty((k // 512, 16))
    for p in range(k // 512):
        a[p, :8] = np.random.permutation(np.resize(levels, 8))
        for g in range(8):
            far = levels[np.abs(levels - a[p, g]) >= 10]
            a[p, g + 8] = far[np.random.randint(len(far))]
    return np.exp2(a.ravel()).repeat(32)


def f64(x):
    return np.asarray(x).astype(np.float64)


def striped(idx):
    return np.tile(idx.reshape(-1, 16).T, (8, 1)).astype(np.uint16)


def unstriped(offs):
    return offs[:16].T.reshape(-1).astype(np.int64)


def pack_weight(w):
    k, n = w.shape
    w = f64(np.asarray(w, np.float32).astype(ml_dtypes.bfloat16)).reshape(k // 32, 32, n)
    amax = np.abs(w).max(1)
    byte = np.clip(np.where(amax > 0, np.frexp(amax)[1] - 1 + 127 - 7, 1), 1, 254)
    scaled = (w * np.exp2(127.0 - byte)[:, None, :]).reshape(k, n).astype(np.float32)
    words = np.ascontiguousarray(scaled.reshape(k // 512, 128, 4, n).transpose(0, 1, 3, 2)).astype(ml_dtypes.float8_e4m3fn).view(np.uint8)
    return words, np.ascontiguousarray(byte.astype(np.uint8).reshape(k // 512, 16, n))


def unpack_weight(words, scales):
    g, p, n, _ = words.shape
    vals = np.ascontiguousarray(words).view(ml_dtypes.float8_e4m3fn).astype(np.float64) * np.repeat(np.exp2(scales.astype(np.float64) - 127.0), 8, axis=1)[..., None]
    return vals.transpose(0, 1, 3, 2).reshape(g * 512, n)


def planes(y):
    n, m = y.shape
    v = y.astype(np.float32).astype(ml_dtypes.bfloat16).astype(np.float64).reshape(n // 32, 32, m)
    top = np.abs(v).max(1)
    byte = np.clip(np.where(top > 0, np.frexp(top)[1] - 1 + 127 - 7, 1), 1, 254)
    codes = (v * np.exp2(127.0 - byte)[:, None, :]).reshape(n, m).astype(np.float32).astype(ml_dtypes.float8_e4m3fn).view(np.uint8)
    words = codes.reshape(n // 512, 128, 4, m).transpose(0, 1, 3, 2)
    return np.ascontiguousarray(words), np.ascontiguousarray(byte.astype(np.uint8).reshape(n // 512, 16, m))


K, T, S, H, N, R = 1024, 2048, 1024, 512, 512, 512


def setup_inputs():
    n = np.random.standard_normal
    s = mx_kscale(K)[:, None]
    u = mx_kscale(H)
    packed_xT = pack_weight(n((K, T)) * s)
    return {
        "x_words": packed_xT[0],
        "x_scales": packed_xT[1],
        "w1": (n((K, H)) / np.sqrt(K) / s * u).astype(np.float32),
        "w2": (n((H, N)) / np.sqrt(H) / u[:, None]).astype(np.float32),
        "w3": (n((K, N)) / np.sqrt(K) / s).astype(np.float32),
        "ld": (np.random.uniform(0.2, 1.5, (H, R))).astype(np.float32),
        "lb": (np.random.uniform(0.2, 1.5, (N, R))).astype(np.float32),
        "offs": striped(np.random.permutation(T)[:S]),
        "ad": striped(np.random.permutation(np.concatenate([np.arange(R), np.random.randint(0, R, S - R)]))),
    }


def reference(x_words, x_scales, w1, w2, w3, ld, lb, offs, ad):
    xq = unpack_weight(x_words, x_scales)[:, unstriped(offs)]
    ee = mxq(f64(w3), 0, "e4m3").T @ xq
    y = mxq(f64(w1), 0, "e4m3").T @ xq
    h = f64(ld)[:, unstriped(ad)] * y
    rr = mxq(f64(w2), 0, "e4m3").T @ mxq(h, 0, "e4m3")
    out_0 = ee + f64(lb)[:, unstriped(ad)] * rr
    return (out_0,) + planes(out_0)

@@ -1,0 +1,293 @@
+from contextlib import ExitStack
+
+import concourse.mybir as mybir
+
+K, T, S, H, N, R = 1024, 2048, 1024, 512, 512, 512
+FLOPS = 2 * S * (K * H + K * N + H * N)
+
+F32 = mybir.dt.float32
+BF16 = mybir.dt.bfloat16
+I32 = mybir.dt.int32
+U32 = mybir.dt.uint32
+U16 = mybir.dt.uint16
+U8 = mybir.dt.uint8
+FP8X4 = mybir.dt.float8_e4m3fn_x4
+MULT = mybir.AluOpType.mult
+ADD = mybir.AluOpType.add
+
+P = 128
+PACK = 4
+K_PASS = P * PACK
+PASSES = K // K_PASS
+LIST_ROWS = 16
+BANK = 512
+WINDOW = R + 32
+
+
+def tile_picked_yvera_none_po_kernel(
+    tc, x_words, x_scales, w1, w2, w3, ld, lb, offs, ad, out_0, out_1, out_2
+):
+    nc = tc.nc
+    with ExitStack() as ctx:
+        keep = ctx.enter_context(tc.tile_pool(name="keep", bufs=1))
+        psum = ctx.enter_context(tc.psum_pool(name="psum", bufs=1))
+
+        offs_t = keep.tile([P, S // LIST_ROWS], U16, name="offs_t")
+        ad_t = keep.tile([P, S // LIST_ROWS], U16, name="ad_t")
+
+        def entries(list_tile, lo, hi):
+            return list_tile[:, lo // LIST_ROWS : hi // LIST_ROWS]
+
+        def load_words(g):
+            words = keep.tile([P, T], I32, name="x_in%d" % g)
+            nc.sync.dma_start(words[:], x_words[g].rearrange("p c r -> p (c r)").bitcast(I32))
+            return words
+
+        def load_weight(w, g, name):
+            rows = keep.tile([P, PACK, 512], F32, name=name + "_raw", tag=name + "_raw", align_bytes=64)
+            nc.sync.dma_start(rows[:], w[g * K_PASS : (g + 1) * K_PASS, :].rearrange("(p j) c -> p j c", j=PACK))
+            return rows
+
+        def load_table(table, name):
+            rows = table.rearrange("(p t) r -> t p r", t=PACK)
+            tiles = []
+            for t in range(PACK):
+                plane = keep.tile([P, WINDOW], F32, name="%s%d" % (name, t))
+                nc.gpsimd.memset(plane[:, R:WINDOW], 0.0)
+                nc.sync.dma_start(plane[:, 0:R], rows[t])
+                tiles.append(plane)
+            return tiles
+
+        raw = {}
+        dealt = {}
+        weight = {}
+
+        def round_weight(name, g):
+            dealt[name, g] = keep.tile([P, PACK * 512], BF16, name="%s_%d_bf" % (name, g), tag="%s_%d_bf" % (name, g), align_bytes=64)
+            nc.scalar.copy(
+                dealt[name, g][:].rearrange("p (t m j) -> p m j t", t=PACK, j=PACK),
+                raw[name, g][:].rearrange("p j (m t) -> p m j t", t=PACK),
+            )
+
+        def round_weight_split(name, g):
+            dealt[name, g] = keep.tile([P, PACK * 512], BF16, name="%s_%d_bf" % (name, g), tag="%s_%d_bf" % (name, g), align_bytes=64)
+            dst = dealt[name, g][:].rearrange("p (t m j) -> p m j t", t=PACK, j=PACK)
+            src = raw[name, g][:].rearrange("p j (m t) -> p m j t", t=PACK)
+            nc.scalar.copy(dst[:, 0:64], src[:, 0:64])
+            nc.vector.tensor_copy(dst[:, 64:P], src[:, 64:P])
+
+        def quantize_weight(name, g):
+            codes = keep.tile([P, 512], U32, name="%s_%d_codes" % (name, g), align_bytes=64)
+            scales = keep.tile([P, 512], U8, name="%s_%d_scales" % (name, g), align_bytes=64)
+            nc.vector.quantize_mx(out=codes[:].bitcast(FP8X4), scales=scales[:], in_=dealt[name, g][:])
+            weight[name, g] = (codes, scales)
+
+        xs_in = keep.tile([P, T], U8, name="xs_in")
+        nc.vector.memset(xs_in[:].bitcast(I32), 0)
+        x_in = [None] * PASSES
+        nc.sync.dma_start(ad_t[:], ad)
+        ld_t = load_table(ld, "ld")
+        nc.sync.dma_start(offs_t[:], offs)
+        x_in[0] = load_words(0)
+        for q in range(4):
+            nc.scalar.dma_start(
+                xs_in[32 * q : 32 * q + 4 * PASSES, :].bitcast(I32),
+                x_scales[:, 4 * q : 4 * q + 4, :].bitcast(I32),
+            )
+        raw["w1", 0] = load_weight(w1, 0, "w1_0")
+        raw["w1", 1] = load_weight(w1, 1, "w1_1")
+        x_in[1] = load_words(1)
+        raw["w2", 0] = load_weight(w2, 0, "w2_0")
+        raw["w3", 0] = load_weight(w3, 0, "w3_0")
+        raw["w3", 1] = load_weight(w3, 1, "w3_1")
+        lb_t = load_table(lb, "lb")
+
+        x_sc = keep.tile([P, S], U8, name="x_sc", align_bytes=64)
+
+        def gather_words(g, lo, hi, **more):
+            codes = hold("x%d_codes" % g, lo, hi, [P, hi - lo], U32, **more)
+            nc.vector.tensor_copy(codes[:], x_in[g][:].bitcast(U32).indirect(entries(offs_t, lo, hi)))
+
+        def gather0(lo, hi):
+            gather_words(0, lo, hi)
+
+        def gather1(lo, hi):
+            gather_words(1, lo, hi)
+
+        def gather1_late(lo, hi):
+            gather_words(1, lo, hi, tag="w1_1_bf")
+
+        def product(name, moving, n, tag, bufs):
+            per_bank = BANK // n
+            banks = []
+            for b in range(PACK // per_bank):
+                bank = psum.tile([P, per_bank, n], F32, name=tag, tag=tag, bufs=bufs)
+                for u in range(per_bank):
+                    t = b * per_bank + u
+                    for g, (m_codes, m_scales) in enumerate(moving):
+                        w_codes, w_scales = weight[name, g]
+                        nc.tensor.matmul_mx(
+                            out=bank[:, u, :],
+                            lhsT=w_codes[:, t * P : (t + 1) * P].bitcast(FP8X4),
+                            lhsT_scale=w_scales[:, t * P : (t + 1) * P],
+                            rhs=m_codes.bitcast(FP8X4),
+                            rhs_scale=m_scales,
+                            start=(g == 0),
+                            stop=(g == len(moving) - 1),
+                        )
+                banks.append((slice(b * per_bank, (b + 1) * per_bank), bank))
+            return banks
+
+        def tokens(lo, hi):
+            picked = [find("x%d_codes" % g, lo, hi) for g in range(PASSES)]
+            return [(codes[:, a:b], x_sc[4 * g : P, lo:hi]) for g, (codes, a, b) in enumerate(picked)]
+
+        held = {}
+
+        def hold(kind, lo, hi, shape, dtype, **more):
+            tile = keep.tile(shape, dtype, name="%s%d" % (kind, lo), align_bytes=64, **more)
+            held.setdefault(kind, []).append((lo, hi, tile))
+            return tile
+
+        def find(kind, lo, hi):
+            (found,) = [(a, tile) for a, b, tile in held[kind] if a <= lo and hi <= b]
+            return found[1], lo - found[0], hi - found[0]
+
+        def leave_psum(banks, kind, lo, hi, **more):
+            planes = hold(kind, lo, hi, [P, PACK, hi - lo], F32, **more)
+            for ts, bank in banks:
+                nc.scalar.copy(planes[:, ts, :], bank[:])
+
+        def scale_by_adapter(table, src, dst, lo, hi, **more):
+            planes, a, b = find(src, lo, hi)
+            scaled = hold(dst, lo, hi, [P, PACK, hi - lo], F32, **more)
+            for t in range(PACK):
+                nc.vector.tensor_tensor(
+                    scaled[:, t, :], table[t][:].indirect(entries(ad_t, lo, hi)), planes[:, t, a:b], MULT
+                )
+
+        def weave(copy, src, dst, dtype, lo, hi, **more):
+            planes, a, b = find(src, lo, hi)
+            woven = hold(dst, lo, hi, [P, (hi - lo) * PACK], dtype, **more)
+            copy(
+                woven[:].rearrange("p (a i t) -> p a t i", i=4, t=PACK),
+                planes[:, :, a:b].rearrange("p t (a i) -> p a t i", i=4),
+            )
+
+        out_codes = keep.tile([P, S], U32, name="out_codes", align_bytes=64)
+        out_scales = keep.tile([P, S], U8, name="out_scales", align_bytes=64)
+        out_rows = out_0.rearrange("(p t) s -> p t s", t=PACK)
+        out_words = out_1[0].rearrange("p c r -> p (c r)").bitcast(I32)
+
+        def look_up(lo, hi):
+            planes = hold("ld_picked", lo, hi, [P, PACK, hi - lo], F32)
+            for t in range(PACK):
+                nc.vector.tensor_copy(planes[:, t, :], ld_t[t][:].indirect(entries(ad_t, lo, hi)))
+
+        def weave_ld(lo, hi):
+            weave(nc.scalar.copy, "ld_picked", "ld_woven", F32, lo, hi, tag="w1_%d_raw" % (lo // 256))
+
+        def inner_early(lo, hi):
+            h_bf = hold("h_bf", lo, hi, [P, (hi - lo) * PACK], BF16)
+            for at in range(lo, hi, P):
+                ((ts, bank),) = product("w1", tokens(at, at + P), P, "a_bank", 5)
+                woven, a, b = find("ld_woven", at, at + P)
+                nc.vector.tensor_tensor(
+                    h_bf[:, (at - lo) * PACK : (at - lo + P) * PACK].rearrange("p (n t) -> p n t", t=PACK),
+                    bank[:].rearrange("p t n -> p n t"),
+                    woven[:, a * PACK : b * PACK].rearrange("p (n t) -> p n t", t=PACK),
+                    MULT,
+                )
+
+        def first_product(lo, hi):
+            leave_psum(product("w1", tokens(lo, hi), hi - lo, "a_bank", 5), "y", lo, hi)
+
+        def inner_late(lo, hi):
+            scale_by_adapter(ld_t, "y", "h", lo, hi)
+
+        def round_h(lo, hi):
+            weave(nc.scalar.copy, "h", "h_bf", BF16, lo, hi)
+
+        def second(lo, hi):
+            h_bf, a, b = find("h_bf", lo, hi)
+            h_codes = hold("h_codes", lo, hi, [P, hi - lo], U32)
+            h_scales = hold("h_scales", lo, hi, [P, hi - lo], U8)
+            nc.vector.quantize_mx(out=h_codes[:].bitcast(FP8X4), scales=h_scales[:], in_=h_bf[:, a * PACK : b * PACK])
+            leave_psum(product("w2", [(h_codes[:], h_scales[:])], hi - lo, "a_bank", 5), "rr", lo, hi)
+
+        def outer(lo, hi):
+            scale_by_adapter(lb_t, "rr", "term", lo, hi)
+
+        def total(lo, hi):
+            term, a, b = find("term", lo, hi)
+            result = hold("result", lo, hi, [P, PACK, hi - lo], F32)
+            for ts, bank in product("w3", tokens(lo, hi), hi - lo, "e_bank", 3):
+                nc.vector.tensor_tensor(result[:, ts, :], term[:, ts, a:b], bank[:], ADD)
+            nc.sync.dma_start(out_rows[:, :, lo:hi], result[:])
+
+        def round_out(lo, hi):
+            weave(nc.scalar.copy, "result", "o_bf", BF16, lo, hi)
+
+        def round_out_v(lo, hi):
+            weave(nc.vector.tensor_copy, "result", "o_bf", BF16, lo, hi)
+
+        def planes_out(lo, hi):
+            o_bf, a, b = find("o_bf", lo, hi)
+            nc.vector.quantize_mx(
+                out=out_codes[:, lo:hi].bitcast(FP8X4), scales=out_scales[:, lo:hi], in_=o_bf[:, a * PACK : b * PACK]
+            )
+
+        def store_words(lo, hi):
+            nc.sync.dma_start(out_words[:, lo:hi], out_codes[:, lo:hi].bitcast(I32))
+
+        look_up(0, 512)
+        gather0(0, 1024)
+        nc.vector.tensor_copy(x_sc[:], xs_in[:].indirect(offs_t[:]))
+        round_weight("w1", 0)
+        quantize_weight("w1", 0)
+        round_weight("w1", 1)
+        gather1(0, 512)
+        quantize_weight("w1", 1)
+        gather1_late(512, 1024)
+        weave_ld(0, 256)
+        weave_ld(256, 512)
+        inner_early(0, 512)
+        round_weight("w2", 0)
+        first_product(512, 1024)
+        quantize_weight("w2", 0)
+        second(0, 512)
+        inner_late(512, 1024)
+        round_weight("w3", 0)
+        round_h(512, 768)
+        second(512, 768)
+        round_h(768, 1024)
+        second(768, 1024)
+        round_weight("w3", 1)
+        quantize_weight("w3", 0)
+        quantize_weight("w3", 1)
+        outer(0, 512)
+        total(0, 256)
+        round_out(0, 256)
+        total(256, 512)
+        round_out(256, 512)
+        outer(512, 768)
+        planes_out(0, 256)
+        planes_out(256, 512)
+        store_words(0, 512)
+        total(512, 768)
+        round_out(512, 768)
+        outer(768, 1024)
+        planes_out(512, 768)
+        store_words(512, 768)
+        total(768, 896)
+        round_out(768, 896)
+        total(896, 1024)
+        round_out_v(896, 1024)
+        planes_out(768, 896)
+        planes_out(896, 1024)
+        store_words(768, 1024)
+        for q in range(4):
+            queue = nc.sync if q % 2 == 0 else nc.scalar
+            queue.dma_start(
+                out_2[0, 4 * q : 4 * q + 4, :].bitcast(I32), out_scales[32 * q : 32 * q + 4, :].bitcast(I32)
+            )

@@ -145,6 +145,7 @@ def tile_picked_yvera_none_po_kernel(
         held = {}
 
         def hold(kind, lo, hi, shape, dtype, **more):
+            more.setdefault("tag", "%s%d" % (kind, lo))
             tile = keep.tile(shape, dtype, name="%s%d" % (kind, lo), align_bytes=64, **more)
             held.setdefault(kind, []).append((lo, hi, tile))
             return tile
@@ -209,14 +210,88 @@ def tile_picked_yvera_none_po_kernel(
             weave(nc.scalar.copy, "h", "h_bf", BF16, lo, hi)
 
         def second(lo, hi):
+            quant_h(lo, hi)
+            second_product(lo, hi)
+
+        def quant_h(lo, hi):
             h_bf, a, b = find("h_bf", lo, hi)
             h_codes = hold("h_codes", lo, hi, [P, hi - lo], U32)
             h_scales = hold("h_scales", lo, hi, [P, hi - lo], U8)
             nc.vector.quantize_mx(out=h_codes[:].bitcast(FP8X4), scales=h_scales[:], in_=h_bf[:, a * PACK : b * PACK])
-            leave_psum(product("w2", [(h_codes[:], h_scales[:])], hi - lo, "a_bank", 5), "rr", lo, hi)
+
+        def second_product(lo, hi):
+            h_codes, a, b = find("h_codes", lo, hi)
+            h_scales, a, b = find("h_scales", lo, hi)
+            leave_psum(product("w2", [(h_codes[:, a:b], h_scales[:, a:b])], hi - lo, "a_bank", 5), "rr", lo, hi)
 
         def outer(lo, hi):
             scale_by_adapter(lb_t, "rr", "term", lo, hi)
+
+        def outer_pair(pair, lo, hi, **more):
+            planes, a, b = find("rr", lo, hi)
+            scaled = hold("term%d_" % pair, lo, hi, [P, 2, hi - lo], F32, **more)
+            for u in range(2):
+                t = 2 * pair + u
+                nc.vector.tensor_tensor(
+                    scaled[:, u, :], lb_t[t][:].indirect(entries(ad_t, lo, hi)), planes[:, t, a:b], MULT
+                )
+
+        def outer_a(lo, hi):
+            outer_pair(0, lo, hi)
+
+        def outer_b(lo, hi):
+            outer_pair(1, lo, hi)
+
+        def outer_b_held(lo, hi):
+            outer_pair(1, lo, hi, tag="h512")
+
+        def total_pairs(lo, hi):
+            result = hold("result", lo, hi, [P, PACK, hi - lo], F32)
+            for ts, bank in product("w3", tokens(lo, hi), hi - lo, "e_bank", 3):
+                term, a, b = find("term%d_" % (ts.start // 2), lo, hi)
+                nc.vector.tensor_tensor(result[:, ts, :], term[:, :, a:b], bank[:], ADD)
+            nc.sync.dma_start(out_rows[:, :, lo:hi], result[:])
+
+        def total_pair(pair, lo, hi):
+            if pair == 0:
+                hold("result", lo, hi, [P, PACK, hi - lo], F32)
+                held["ee", lo] = product("w3", tokens(lo, hi), hi - lo, "e_bank", 3)
+            result, a, b = find("result", lo, hi)
+            ts, bank = held["ee", lo][pair]
+            term, a, b = find("term%d_" % pair, lo, hi)
+            nc.vector.tensor_tensor(result[:, ts, :], term[:, :, a:b], bank[:], ADD)
+            nc.sync.dma_start(out_rows[:, ts, lo:hi], result[:, ts, :])
+
+        def total_a(lo, hi):
+            total_pair(0, lo, hi)
+
+        def total_b(lo, hi):
+            total_pair(1, lo, hi)
+
+        def outer_t(t, lo, hi, **more):
+            planes, a, b = find("rr", lo, hi)
+            scaled = hold("plane%d_" % t, lo, hi, [P, hi - lo], F32, **more)
+            nc.vector.tensor_tensor(scaled[:], lb_t[t][:].indirect(entries(ad_t, lo, hi)), planes[:, t, a:b], MULT)
+
+        def total_t(t, lo, hi):
+            if t == 0:
+                hold("result", lo, hi, [P, PACK, hi - lo], F32)
+            result = find("result", lo, hi)[0]
+            bank = psum.tile([P, BANK], F32, name="e_bank", tag="e_bank", bufs=3)
+            for at in range(lo, hi, 256):
+                for g, (m_codes, m_scales) in enumerate(tokens(at, at + 256)):
+                    w_codes, w_scales = weight["w3", g]
+                    nc.tensor.matmul_mx(
+                        out=bank[:, at - lo : at - lo + 256],
+                        lhsT=w_codes[:, t * P : (t + 1) * P].bitcast(FP8X4),
+                        lhsT_scale=w_scales[:, t * P : (t + 1) * P],
+                        rhs=m_codes.bitcast(FP8X4),
+                        rhs_scale=m_scales,
+                        start=(g == 0),
+                        stop=(g == PASSES - 1),
+                    )
+            nc.vector.tensor_tensor(result[:, t, :], find("plane%d_" % t, lo, hi)[0][:], bank[:], ADD)
+            nc.sync.dma_start(out_rows[:, t, lo:hi], result[:, t, :])
 
         def total(lo, hi):
             term, a, b = find("term", lo, hi)
@@ -246,9 +321,9 @@ def tile_picked_yvera_none_po_kernel(
         round_weight("w1", 0)
         quantize_weight("w1", 0)
         round_weight("w1", 1)
-        gather1(0, 512)
+        gather1(0, 256)
         quantize_weight("w1", 1)
-        gather1_late(512, 1024)
+        gather1_late(256, 1024)
         weave_ld(0, 256)
         weave_ld(256, 512)
         inner_early(0, 512)
@@ -258,34 +333,38 @@ def tile_picked_yvera_none_po_kernel(
         second(0, 512)
         inner_late(512, 1024)
         round_weight("w3", 0)
-        round_h(512, 768)
-        second(512, 768)
-        round_h(768, 1024)
-        second(768, 1024)
         round_weight("w3", 1)
+        round_h(512, 1024)
         quantize_weight("w3", 0)
         quantize_weight("w3", 1)
-        outer(0, 512)
-        total(0, 256)
+        quant_h(512, 1024)
+        second_product(512, 768)
+        second_product(768, 1024)
+        outer_t(0, 0, 512)
+        outer_t(1, 0, 512)
+        outer_t(2, 0, 512, tag="w3_1_raw")
+        outer_t(3, 0, 512, tag="h512")
+        total_t(0, 0, 512)
+        total_t(1, 0, 512)
+        total_t(2, 0, 512)
+        total_t(3, 0, 512)
         round_out(0, 256)
-        total(256, 512)
         round_out(256, 512)
-        outer(512, 768)
         planes_out(0, 256)
         planes_out(256, 512)
         store_words(0, 512)
+        outer(512, 768)
         total(512, 768)
         round_out(512, 768)
         outer(768, 1024)
         planes_out(512, 768)
-        store_words(512, 768)
         total(768, 896)
         round_out(768, 896)
         total(896, 1024)
         round_out_v(896, 1024)
         planes_out(768, 896)
         planes_out(896, 1024)
-        store_words(768, 1024)
+        store_words(512, 1024)
         for q in range(4):
             queue = nc.sync if q % 2 == 0 else nc.scalar
             queue.dma_start(

@@ -22,6 +22,7 @@ PASSES = K // K_PASS
 LIST_ROWS = 16
 BANK = 512
 WINDOW = R + 32
+EARLY_WINDOW = 800
 
 
 def tile_picked_yvera_none_po_kernel(
@@ -48,12 +49,12 @@ def tile_picked_yvera_none_po_kernel(
             nc.sync.dma_start(rows[:], w[g * K_PASS : (g + 1) * K_PASS, :].rearrange("(p j) c -> p j c", j=PACK))
             return rows
 
-        def load_table(table, name):
+        def load_table(table, name, window):
             rows = table.rearrange("(p t) r -> t p r", t=PACK)
             tiles = []
             for t in range(PACK):
-                plane = keep.tile([P, WINDOW], F32, name="%s%d" % (name, t))
-                nc.gpsimd.memset(plane[:, R:WINDOW], 0.0)
+                plane = keep.tile([P, window], F32, name="%s%d" % (name, t))
+                nc.gpsimd.memset(plane[:, R:window], 0.0)
                 nc.sync.dma_start(plane[:, 0:R], rows[t])
                 tiles.append(plane)
             return tiles
@@ -76,6 +77,21 @@ def tile_picked_yvera_none_po_kernel(
             nc.scalar.copy(dst[:, 0:64], src[:, 0:64])
             nc.vector.tensor_copy(dst[:, 64:P], src[:, 64:P])
 
+        def round_w3(g):
+            if g == 0:
+                dealt["w3"] = keep.tile([P, PASSES * PACK * 512], BF16, name="w3_bf", align_bytes=64)
+            nc.scalar.copy(
+                dealt["w3"][:, g * PACK * 512 : (g + 1) * PACK * 512].rearrange("p (t m j) -> p m j t", t=PACK, j=PACK),
+                raw["w3", g][:].rearrange("p j (m t) -> p m j t", t=PACK),
+            )
+
+        def quantize_w3():
+            codes = keep.tile([P, PASSES * 512], U32, name="w3_codes", align_bytes=64)
+            scales = keep.tile([P, PASSES * 512], U8, name="w3_scales", align_bytes=64)
+            nc.vector.quantize_mx(out=codes[:].bitcast(FP8X4), scales=scales[:], in_=dealt["w3"][:])
+            for g in range(PASSES):
+                weight["w3", g] = (codes[:, g * 512 : (g + 1) * 512], scales[:, g * 512 : (g + 1) * 512])
+
         def quantize_weight(name, g):
             codes = keep.tile([P, 512], U32, name="%s_%d_codes" % (name, g), align_bytes=64)
             scales = keep.tile([P, 512], U8, name="%s_%d_scales" % (name, g), align_bytes=64)
@@ -86,9 +102,8 @@ def tile_picked_yvera_none_po_kernel(
         nc.vector.memset(xs_in[:].bitcast(I32), 0)
         x_in = [None] * PASSES
         nc.sync.dma_start(ad_t[:], ad)
-        ld_t = load_table(ld, "ld")
+        ld_t = load_table(ld, "ld", EARLY_WINDOW)
         nc.sync.dma_start(offs_t[:], offs)
-        x_in[0] = load_words(0)
         for q in range(4):
             nc.scalar.dma_start(
                 xs_in[32 * q : 32 * q + 4 * PASSES, :].bitcast(I32),
@@ -96,11 +111,12 @@ def tile_picked_yvera_none_po_kernel(
             )
         raw["w1", 0] = load_weight(w1, 0, "w1_0")
         raw["w1", 1] = load_weight(w1, 1, "w1_1")
+        x_in[0] = load_words(0)
         x_in[1] = load_words(1)
         raw["w2", 0] = load_weight(w2, 0, "w2_0")
         raw["w3", 0] = load_weight(w3, 0, "w3_0")
         raw["w3", 1] = load_weight(w3, 1, "w3_1")
-        lb_t = load_table(lb, "lb")
+        lb_t = load_table(lb, "lb", WINDOW)
 
         x_sc = keep.tile([P, S], U8, name="x_sc", align_bytes=64)
 
@@ -268,14 +284,15 @@ def tile_picked_yvera_none_po_kernel(
         def total_b(lo, hi):
             total_pair(1, lo, hi)
 
+        def open_result(lo, hi):
+            hold("result", lo, hi, [P, PACK, hi - lo], F32)
+
         def outer_t(t, lo, hi, **more):
             planes, a, b = find("rr", lo, hi)
             scaled = hold("plane%d_" % t, lo, hi, [P, hi - lo], F32, **more)
             nc.vector.tensor_tensor(scaled[:], lb_t[t][:].indirect(entries(ad_t, lo, hi)), planes[:, t, a:b], MULT)
 
         def total_t(t, lo, hi):
-            if t == 0:
-                hold("result", lo, hi, [P, PACK, hi - lo], F32)
             result = find("result", lo, hi)[0]
             bank = psum.tile([P, BANK], F32, name="e_bank", tag="e_bank", bufs=3)
             for at in range(lo, hi, 256):
@@ -315,35 +332,38 @@ def tile_picked_yvera_none_po_kernel(
         def store_words(lo, hi):
             nc.sync.dma_start(out_words[:, lo:hi], out_codes[:, lo:hi].bitcast(I32))
 
-        look_up(0, 512)
-        gather0(0, 1024)
+        look_up(0, 768)
         nc.vector.tensor_copy(x_sc[:], xs_in[:].indirect(offs_t[:]))
         round_weight("w1", 0)
         quantize_weight("w1", 0)
         round_weight("w1", 1)
-        gather1(0, 256)
+        gather0(0, 1024)
         quantize_weight("w1", 1)
-        gather1_late(256, 1024)
+        gather1(0, 256)
+        gather1(256, 1024)
         weave_ld(0, 256)
-        weave_ld(256, 512)
+        weave_ld(256, 768)
         inner_early(0, 512)
         round_weight("w2", 0)
-        first_product(512, 1024)
+        inner_early(512, 768)
+        first_product(768, 1024)
         quantize_weight("w2", 0)
         second(0, 512)
-        inner_late(512, 1024)
+        inner_late(768, 1024)
+        quant_h(512, 768)
         round_weight("w3", 0)
+        round_h(768, 1024)
+        quant_h(768, 1024)
         round_weight("w3", 1)
-        round_h(512, 1024)
         quantize_weight("w3", 0)
         quantize_weight("w3", 1)
-        quant_h(512, 1024)
         second_product(512, 768)
         second_product(768, 1024)
         outer_t(0, 0, 512)
         outer_t(1, 0, 512)
-        outer_t(2, 0, 512, tag="w3_1_raw")
-        outer_t(3, 0, 512, tag="h512")
+        outer_t(2, 0, 512)
+        outer_t(3, 0, 512)
+        open_result(0, 512)
         total_t(0, 0, 512)
         total_t(1, 0, 512)
         total_t(2, 0, 512)

@@ -285,7 +285,7 @@ def tile_picked_yvera_none_po_kernel(
             total_pair(1, lo, hi)
 
         def open_result(lo, hi):
-            hold("result", lo, hi, [P, PACK, hi - lo], F32)
+            hold("result", lo, hi, [P, PACK, hi - lo], F32, tag="rr%d" % lo)
 
         def outer_t(t, lo, hi, **more):
             planes, a, b = find("rr", lo, hi)
@@ -307,7 +307,12 @@ def tile_picked_yvera_none_po_kernel(
                         start=(g == 0),
                         stop=(g == PASSES - 1),
                     )
-            nc.vector.tensor_tensor(result[:, t, :], find("plane%d_" % t, lo, hi)[0][:], bank[:], ADD)
+            if t == PACK - 1:
+                frozen = hold("frozen", lo, hi, [P, hi - lo], F32)
+                nc.scalar.copy(frozen[:], bank[:])
+                nc.gpsimd.tensor_tensor(result[:, t, :], find("plane%d_" % t, lo, hi)[0][:], frozen[:], ADD)
+            else:
+                nc.vector.tensor_tensor(result[:, t, :], find("plane%d_" % t, lo, hi)[0][:], bank[:], ADD)
             nc.sync.dma_start(out_rows[:, t, lo:hi], result[:, t, :])
 
         def total(lo, hi):
@@ -364,10 +369,10 @@ def tile_picked_yvera_none_po_kernel(
         outer_t(2, 0, 512)
         outer_t(3, 0, 512)
         open_result(0, 512)
+        total_t(3, 0, 512)
         total_t(0, 0, 512)
         total_t(1, 0, 512)
         total_t(2, 0, 512)
-        total_t(3, 0, 512)
         round_out(0, 256)
         round_out(256, 512)
         planes_out(0, 256)

@@ -103,14 +103,14 @@ def tile_picked_yvera_none_po_kernel(
         x_in = [None] * PASSES
         nc.sync.dma_start(ad_t[:], ad)
         ld_t = load_table(ld, "ld", EARLY_WINDOW)
+        raw["w1", 0] = load_weight(w1, 0, "w1_0")
         nc.sync.dma_start(offs_t[:], offs)
+        raw["w1", 1] = load_weight(w1, 1, "w1_1")
         for q in range(4):
             nc.scalar.dma_start(
                 xs_in[32 * q : 32 * q + 4 * PASSES, :].bitcast(I32),
                 x_scales[:, 4 * q : 4 * q + 4, :].bitcast(I32),
             )
-        raw["w1", 0] = load_weight(w1, 0, "w1_0")
-        raw["w1", 1] = load_weight(w1, 1, "w1_1")
         x_in[0] = load_words(0)
         x_in[1] = load_words(1)
         raw["w2", 0] = load_weight(w2, 0, "w2_0")

@@ -138,9 +138,9 @@ def tile_picked_yvera_none_po_kernel(
             banks = []
             for b in range(PACK // per_bank):
                 bank = psum.tile([P, per_bank, n], F32, name=tag, tag=tag, bufs=bufs)
-                for u in range(per_bank):
-                    t = b * per_bank + u
-                    for g, (m_codes, m_scales) in enumerate(moving):
+                for g, (m_codes, m_scales) in enumerate(moving):
+                    for u in range(per_bank):
+                        t = b * per_bank + u
                         w_codes, w_scales = weight[name, g]
                         nc.tensor.matmul_mx(
                             out=bank[:, u, :],
@@ -148,8 +148,8 @@ def tile_picked_yvera_none_po_kernel(
                             lhsT_scale=w_scales[:, t * P : (t + 1) * P],
                             rhs=m_codes.bitcast(FP8X4),
                             rhs_scale=m_scales,
-                            start=(g == 0),
-                            stop=(g == len(moving) - 1),
+                            start=(g == 0 and u == 0),
+                            stop=(g == len(moving) - 1 and u == per_bank - 1),
                         )
                 banks.append((slice(b * per_bank, (b + 1) * per_bank), bank))
             return banks
@@ -209,6 +209,11 @@ def tile_picked_yvera_none_po_kernel(
             for at in range(lo, hi, P):
                 ((ts, bank),) = product("w1", tokens(at, at + P), P, "a_bank", 5)
                 woven, a, b = find("ld_woven", at, at + P)
+                if at == 0:
+                    y_woven = hold("y_woven", at, at + P, [P, P * PACK], F32)
+                    nc.scalar.copy(y_woven[:].rearrange("p (n t) -> p n t", t=PACK), bank[:].rearrange("p t n -> p n t"))
+                    nc.gpsimd.tensor_tensor(h_bf[:, 0 : P * PACK], y_woven[:], woven[:, a * PACK : b * PACK], MULT)
+                    continue
                 nc.vector.tensor_tensor(
                     h_bf[:, (at - lo) * PACK : (at - lo + P) * PACK].rearrange("p (n t) -> p n t", t=PACK),
                     bank[:].rearrange("p t n -> p n t"),
@@ -342,7 +347,8 @@ def tile_picked_yvera_none_po_kernel(
         round_weight("w1", 0)
         quantize_weight("w1", 0)
         round_weight("w1", 1)
-        gather0(0, 1024)
+        gather0(0, 512)
+        gather0(512, 1024)
         quantize_weight("w1", 1)
         gather1(0, 256)
         gather1(256, 1024)

@@ -112,8 +112,11 @@ def tile_picked_yvera_none_po_kernel(
                 x_scales[:, 4 * q : 4 * q + 4, :].bitcast(I32),
             )
         x_in[0] = load_words(0)
+        w2_rows = w2.rearrange("(p j) c -> p j c", j=PACK)
+        w2_halves = [keep.tile([P, PACK, 256], F32, name="w2_half%d" % u, align_bytes=64) for u in range(2)]
+        nc.sync.dma_start(w2_halves[0][:], w2_rows[:, :, 0:256])
         x_in[1] = load_words(1)
-        raw["w2", 0] = load_weight(w2, 0, "w2_0")
+        nc.sync.dma_start(w2_halves[1][:], w2_rows[:, :, 256:512])
         raw["w3", 0] = load_weight(w3, 0, "w3_0")
         raw["w3", 1] = load_weight(w3, 1, "w3_1")
         lb_t = load_table(lb, "lb", WINDOW)
@@ -208,16 +211,17 @@ def tile_picked_yvera_none_po_kernel(
             h_bf = hold("h_bf", lo, hi, [P, (hi - lo) * PACK], BF16)
             for at in range(lo, hi, P):
                 ((ts, bank),) = product("w1", tokens(at, at + P), P, "a_bank", 5)
-                woven, a, b = find("ld_woven", at, at + P)
-                if at == 0:
+                if at < 2 * P:
+                    woven, a, b = find("ld_woven", at, at + P)
                     y_woven = hold("y_woven", at, at + P, [P, P * PACK], F32)
                     nc.scalar.copy(y_woven[:].rearrange("p (n t) -> p n t", t=PACK), bank[:].rearrange("p t n -> p n t"))
-                    nc.gpsimd.tensor_tensor(h_bf[:, 0 : P * PACK], y_woven[:], woven[:, a * PACK : b * PACK], MULT)
+                    nc.gpsimd.tensor_tensor(h_bf[:, at * PACK : (at + P) * PACK], y_woven[:], woven[:, a * PACK : b * PACK], MULT)
                     continue
+                picked, a, b = find("ld_picked", at, at + P)
                 nc.vector.tensor_tensor(
-                    h_bf[:, (at - lo) * PACK : (at - lo + P) * PACK].rearrange("p (n t) -> p n t", t=PACK),
-                    bank[:].rearrange("p t n -> p n t"),
-                    woven[:, a * PACK : b * PACK].rearrange("p (n t) -> p n t", t=PACK),
+                    h_bf[:, (at - lo) * PACK : (at - lo + P) * PACK].rearrange("p (a i t) -> p a t i", i=4, t=PACK),
+                    bank[:].rearrange("p t (a i) -> p a t i", i=4),
+                    picked[:, :, a:b].rearrange("p t (a i) -> p a t i", i=4),
                     MULT,
                 )
 
@@ -236,7 +240,7 @@ def tile_picked_yvera_none_po_kernel(
 
         def quant_h(lo, hi):
             h_bf, a, b = find("h_bf", lo, hi)
-            h_codes = hold("h_codes", lo, hi, [P, hi - lo], U32)
+            h_codes = hold("h_codes", lo, hi, [P, hi - lo], U32, tag="w2_bf" if lo == 0 else "h_codes%d" % lo)
             h_scales = hold("h_scales", lo, hi, [P, hi - lo], U8)
             nc.vector.quantize_mx(out=h_codes[:].bitcast(FP8X4), scales=h_scales[:], in_=h_bf[:, a * PACK : b * PACK])
 
@@ -351,11 +355,16 @@ def tile_picked_yvera_none_po_kernel(
         gather0(512, 1024)
         quantize_weight("w1", 1)
         gather1(0, 256)
-        gather1(256, 1024)
+        gather1(256, 512)
+        gather1(512, 1024)
         weave_ld(0, 256)
-        weave_ld(256, 768)
         inner_early(0, 512)
-        round_weight("w2", 0)
+        dealt["w2", 0] = keep.tile([P, PACK * 512], BF16, name="w2_bf", tag="w2_bf", align_bytes=64)
+        for u in range(2):
+            nc.scalar.copy(
+                dealt["w2", 0][:].rearrange("p (t m j) -> p m j t", t=PACK, j=PACK)[:, 64 * u : 64 * u + 64],
+                w2_halves[u][:].rearrange("p j (m t) -> p m j t", t=PACK),
+            )
         inner_early(512, 768)
         first_product(768, 1024)
         quantize_weight("w2", 0)

@@ -92,8 +92,9 @@ def tile_picked_yvera_none_po_kernel(
             for g in range(PASSES):
                 weight["w3", g] = (codes[:, g * 512 : (g + 1) * 512], scales[:, g * 512 : (g + 1) * 512])
 
-        def quantize_weight(name, g):
-            codes = keep.tile([P, 512], U32, name="%s_%d_codes" % (name, g), align_bytes=64)
+        def quantize_weight(name, g, tag=None):
+            label = "%s_%d_codes" % (name, g)
+            codes = keep.tile([P, 512], U32, name=label, tag=tag or label, align_bytes=64)
             scales = keep.tile([P, 512], U8, name="%s_%d_scales" % (name, g), align_bytes=64)
             nc.vector.quantize_mx(out=codes[:].bitcast(FP8X4), scales=scales[:], in_=dealt[name, g][:])
             weight[name, g] = (codes, scales)
@@ -247,7 +248,12 @@ def tile_picked_yvera_none_po_kernel(
         def second_product(lo, hi):
             h_codes, a, b = find("h_codes", lo, hi)
             h_scales, a, b = find("h_scales", lo, hi)
-            leave_psum(product("w2", [(h_codes[:, a:b], h_scales[:, a:b])], hi - lo, "a_bank", 5), "rr", lo, hi)
+            banks = product("w2", [(h_codes[:, a:b], h_scales[:, a:b])], hi - lo, "a_bank", 5)
+            if lo > 0:
+                leave_psum(banks, "rr", lo, hi)
+                return
+            for ts, bank in banks:
+                nc.scalar.copy(hold("rr_plane%d_" % ts.start, lo, hi, [P, 1, hi - lo], F32)[:], bank[:])
 
         def outer(lo, hi):
             scale_by_adapter(lb_t, "rr", "term", lo, hi)
@@ -294,12 +300,12 @@ def tile_picked_yvera_none_po_kernel(
             total_pair(1, lo, hi)
 
         def open_result(lo, hi):
-            hold("result", lo, hi, [P, PACK, hi - lo], F32, tag="rr%d" % lo)
+            hold("result", lo, hi, [P, PACK, hi - lo], F32, tag="rr512")
 
         def outer_t(t, lo, hi, **more):
-            planes, a, b = find("rr", lo, hi)
+            plane, a, b = find("rr_plane%d_" % t, lo, hi)
             scaled = hold("plane%d_" % t, lo, hi, [P, hi - lo], F32, **more)
-            nc.vector.tensor_tensor(scaled[:], lb_t[t][:].indirect(entries(ad_t, lo, hi)), planes[:, t, a:b], MULT)
+            nc.vector.tensor_tensor(scaled[:], lb_t[t][:].indirect(entries(ad_t, lo, hi)), plane[:, 0, a:b], MULT)
 
         def total_t(t, lo, hi):
             result = find("result", lo, hi)[0]
@@ -376,13 +382,14 @@ def tile_picked_yvera_none_po_kernel(
         quant_h(768, 1024)
         round_weight("w3", 1)
         quantize_weight("w3", 0)
-        quantize_weight("w3", 1)
         second_product(512, 768)
         second_product(768, 1024)
         outer_t(0, 0, 512)
         outer_t(1, 0, 512)
         outer_t(2, 0, 512)
         outer_t(3, 0, 512)
+        quantize_weight("w3", 1, tag="rr_plane3_0")
+        outer(512, 768)
         open_result(0, 512)
         total_t(3, 0, 512)
         total_t(0, 0, 512)
@@ -393,7 +400,6 @@ def tile_picked_yvera_none_po_kernel(
         planes_out(0, 256)
         planes_out(256, 512)
         store_words(0, 512)
-        outer(512, 768)
         total(512, 768)
         round_out(512, 768)
         outer(768, 1024)

@@ -66,8 +66,8 @@ def tile_picked_yvera_none_po_kernel(
         def round_weight(name, g):
             dealt[name, g] = keep.tile([P, PACK * 512], BF16, name="%s_%d_bf" % (name, g), tag="%s_%d_bf" % (name, g), align_bytes=64)
             nc.scalar.copy(
-                dealt[name, g][:].rearrange("p (t m j) -> p m j t", t=PACK, j=PACK),
-                raw[name, g][:].rearrange("p j (m t) -> p m j t", t=PACK),
+                dealt[name, g][:].rearrange("p (h u m j) -> p h m j u", h=2, u=2, j=PACK),
+                raw[name, g][:].rearrange("p j (m h u) -> p h m j u", h=2, u=2),
             )
 
         def round_weight_split(name, g):
@@ -368,8 +368,8 @@ def tile_picked_yvera_none_po_kernel(
         dealt["w2", 0] = keep.tile([P, PACK * 512], BF16, name="w2_bf", tag="w2_bf", align_bytes=64)
         for u in range(2):
             nc.scalar.copy(
-                dealt["w2", 0][:].rearrange("p (t m j) -> p m j t", t=PACK, j=PACK)[:, 64 * u : 64 * u + 64],
-                w2_halves[u][:].rearrange("p j (m t) -> p m j t", t=PACK),
+                dealt["w2", 0][:].rearrange("p (h u m j) -> p h m j u", h=2, u=2, j=PACK)[:, :, 64 * u : 64 * u + 64],
+                w2_halves[u][:].rearrange("p j (m h u) -> p h m j u", h=2, u=2),
             )
         inner_early(512, 768)
         first_product(768, 1024)

@@ -310,8 +310,9 @@ def tile_picked_yvera_none_po_kernel(
         def total_t(t, lo, hi):
             result = find("result", lo, hi)[0]
             bank = psum.tile([P, BANK], F32, name="e_bank", tag="e_bank", bufs=3)
-            for at in range(lo, hi, 256):
-                for g, (m_codes, m_scales) in enumerate(tokens(at, at + 256)):
+            for g in range(PASSES):
+                for at in range(lo, hi, 256):
+                    m_codes, m_scales = tokens(at, at + 256)[g]
                     w_codes, w_scales = weight["w3", g]
                     nc.tensor.matmul_mx(
                         out=bank[:, at - lo : at - lo + 256],
@@ -319,8 +320,8 @@ def tile_picked_yvera_none_po_kernel(
                         lhsT_scale=w_scales[:, t * P : (t + 1) * P],
                         rhs=m_codes.bitcast(FP8X4),
                         rhs_scale=m_scales,
-                        start=(g == 0),
-                        stop=(g == PASSES - 1),
+                        start=(g == 0 and at == lo),
+                        stop=(g == PASSES - 1 and at == hi - 256),
                     )
             if t == PACK - 1:
                 frozen = hold("frozen", lo, hi, [P, hi - lo], F32)
@@ -335,6 +336,17 @@ def tile_picked_yvera_none_po_kernel(
             result = hold("result", lo, hi, [P, PACK, hi - lo], F32)
             for ts, bank in product("w3", tokens(lo, hi), hi - lo, "e_bank", 3):
                 nc.vector.tensor_tensor(result[:, ts, :], term[:, ts, a:b], bank[:], ADD)
+                nc.sync.dma_start(out_rows[:, ts, lo:hi], result[:, ts, :])
+
+        def total_shared(lo, hi):
+            term, a, b = find("term", lo, hi)
+            result = hold("result", lo, hi, [P, PACK, hi - lo], F32)
+            (ts, lower), (ts, upper) = product("w3", tokens(lo, hi), hi - lo, "a_bank", 5)
+            frozen = hold("frozen", lo, hi, [P, hi - lo], F32)
+            nc.scalar.copy(frozen[:], upper[:, 1, :])
+            nc.gpsimd.tensor_tensor(result[:, 3, :], term[:, 3, a:b], frozen[:], ADD)
+            nc.vector.tensor_tensor(result[:, 0:2, :], term[:, 0:2, a:b], lower[:], ADD)
+            nc.vector.tensor_tensor(result[:, 2, :], term[:, 2, a:b], upper[:, 0, :], ADD)
             nc.sync.dma_start(out_rows[:, :, lo:hi], result[:])
 
         def round_out(lo, hi):
@@ -395,22 +407,22 @@ def tile_picked_yvera_none_po_kernel(
         total_t(0, 0, 512)
         total_t(1, 0, 512)
         total_t(2, 0, 512)
+        total_shared(512, 768)
         round_out(0, 256)
         round_out(256, 512)
         planes_out(0, 256)
         planes_out(256, 512)
         store_words(0, 512)
-        total(512, 768)
         round_out(512, 768)
         outer(768, 1024)
         planes_out(512, 768)
-        total(768, 896)
+        store_words(512, 768)
+        total(768, 1024)
         round_out(768, 896)
-        total(896, 1024)
         round_out_v(896, 1024)
         planes_out(768, 896)
         planes_out(896, 1024)
-        store_words(512, 1024)
+        store_words(768, 1024)
         for q in range(4):
             queue = nc.sync if q % 2 == 0 else nc.scalar
             queue.dma_start(

@@ -21,8 +21,12 @@ K_PASS = P * PACK
 PASSES = K // K_PASS
 LIST_ROWS = 16
 BANK = 512
-WINDOW = R + 32
-EARLY_WINDOW = 800
+HALF = S // 2
+LB_WINDOW = R + 32
+HEAD = 768
+LD_WINDOW = HEAD + 32
+PLAIN = 768
+H_ON_GPSIMD = 256
 
 
 def tile_picked_yvera_none_po_kernel(
@@ -31,6 +35,7 @@ def tile_picked_yvera_none_po_kernel(
     nc = tc.nc
     with ExitStack() as ctx:
         keep = ctx.enter_context(tc.tile_pool(name="keep", bufs=1))
+        reused = ctx.enter_context(tc.tile_pool(name="reused", bufs=1))
         psum = ctx.enter_context(tc.psum_pool(name="psum", bufs=1))
 
         offs_t = keep.tile([P, S // LIST_ROWS], U16, name="offs_t")
@@ -39,8 +44,20 @@ def tile_picked_yvera_none_po_kernel(
         def entries(list_tile, lo, hi):
             return list_tile[:, lo // LIST_ROWS : hi // LIST_ROWS]
 
-        def load_words(g):
-            words = keep.tile([P, T], I32, name="x_in%d" % g)
+        held = {}
+
+        def hold(kind, lo, hi, shape, dtype, pool=keep, **more):
+            more.setdefault("tag", "%s%d" % (kind, lo))
+            tile = pool.tile(shape, dtype, name="%s%d" % (kind, lo), align_bytes=64, **more)
+            held.setdefault(kind, []).append((lo, hi, tile))
+            return tile
+
+        def find(kind, lo, hi):
+            (found,) = [(a, tile) for a, b, tile in held[kind] if a <= lo and hi <= b]
+            return found[1], lo - found[0], hi - found[0]
+
+        def load_words(g, pool=keep, **more):
+            words = pool.tile([P, T], I32, name="x_in%d" % g, align_bytes=64, **more)
             nc.sync.dma_start(words[:], x_words[g].rearrange("p c r -> p (c r)").bitcast(I32))
             return words
 
@@ -70,31 +87,10 @@ def tile_picked_yvera_none_po_kernel(
                 raw[name, g][:].rearrange("p j (m h u) -> p h m j u", h=2, u=2),
             )
 
-        def round_weight_split(name, g):
-            dealt[name, g] = keep.tile([P, PACK * 512], BF16, name="%s_%d_bf" % (name, g), tag="%s_%d_bf" % (name, g), align_bytes=64)
-            dst = dealt[name, g][:].rearrange("p (t m j) -> p m j t", t=PACK, j=PACK)
-            src = raw[name, g][:].rearrange("p j (m t) -> p m j t", t=PACK)
-            nc.scalar.copy(dst[:, 0:64], src[:, 0:64])
-            nc.vector.tensor_copy(dst[:, 64:P], src[:, 64:P])
-
-        def round_w3(g):
-            if g == 0:
-                dealt["w3"] = keep.tile([P, PASSES * PACK * 512], BF16, name="w3_bf", align_bytes=64)
-            nc.scalar.copy(
-                dealt["w3"][:, g * PACK * 512 : (g + 1) * PACK * 512].rearrange("p (t m j) -> p m j t", t=PACK, j=PACK),
-                raw["w3", g][:].rearrange("p j (m t) -> p m j t", t=PACK),
-            )
-
-        def quantize_w3():
-            codes = keep.tile([P, PASSES * 512], U32, name="w3_codes", align_bytes=64)
-            scales = keep.tile([P, PASSES * 512], U8, name="w3_scales", align_bytes=64)
-            nc.vector.quantize_mx(out=codes[:].bitcast(FP8X4), scales=scales[:], in_=dealt["w3"][:])
-            for g in range(PASSES):
-                weight["w3", g] = (codes[:, g * 512 : (g + 1) * 512], scales[:, g * 512 : (g + 1) * 512])
-
-        def quantize_weight(name, g, tag=None):
+        def quantize_weight(name, g, pool=keep, **more):
             label = "%s_%d_codes" % (name, g)
-            codes = keep.tile([P, 512], U32, name=label, tag=tag or label, align_bytes=64)
+            more.setdefault("tag", label)
+            codes = pool.tile([P, 512], U32, name=label, align_bytes=64, **more)
             scales = keep.tile([P, 512], U8, name="%s_%d_scales" % (name, g), align_bytes=64)
             nc.vector.quantize_mx(out=codes[:].bitcast(FP8X4), scales=scales[:], in_=dealt[name, g][:])
             weight[name, g] = (codes, scales)
@@ -103,7 +99,7 @@ def tile_picked_yvera_none_po_kernel(
         nc.vector.memset(xs_in[:].bitcast(I32), 0)
         x_in = [None] * PASSES
         nc.sync.dma_start(ad_t[:], ad)
-        ld_t = load_table(ld, "ld", EARLY_WINDOW)
+        ld_t = load_table(ld, "ld", LD_WINDOW)
         raw["w1", 0] = load_weight(w1, 0, "w1_0")
         nc.sync.dma_start(offs_t[:], offs)
         raw["w1", 1] = load_weight(w1, 1, "w1_1")
@@ -115,27 +111,18 @@ def tile_picked_yvera_none_po_kernel(
         x_in[0] = load_words(0)
         w2_rows = w2.rearrange("(p j) c -> p j c", j=PACK)
         w2_halves = [keep.tile([P, PACK, 256], F32, name="w2_half%d" % u, align_bytes=64) for u in range(2)]
-        nc.sync.dma_start(w2_halves[0][:], w2_rows[:, :, 0:256])
         x_in[1] = load_words(1)
+        nc.sync.dma_start(w2_halves[0][:], w2_rows[:, :, 0:256])
         nc.sync.dma_start(w2_halves[1][:], w2_rows[:, :, 256:512])
         raw["w3", 0] = load_weight(w3, 0, "w3_0")
         raw["w3", 1] = load_weight(w3, 1, "w3_1")
-        lb_t = load_table(lb, "lb", WINDOW)
+        lb_t = load_table(lb, "lb", LB_WINDOW)
 
         x_sc = keep.tile([P, S], U8, name="x_sc", align_bytes=64)
 
-        def gather_words(g, lo, hi, **more):
-            codes = hold("x%d_codes" % g, lo, hi, [P, hi - lo], U32, **more)
+        def gather_words(g, lo, hi):
+            codes = hold("x%d_codes" % g, lo, hi, [P, hi - lo], U32)
             nc.vector.tensor_copy(codes[:], x_in[g][:].bitcast(U32).indirect(entries(offs_t, lo, hi)))
-
-        def gather0(lo, hi):
-            gather_words(0, lo, hi)
-
-        def gather1(lo, hi):
-            gather_words(1, lo, hi)
-
-        def gather1_late(lo, hi):
-            gather_words(1, lo, hi, tag="w1_1_bf")
 
         def product(name, moving, n, tag, bufs):
             per_bank = BANK // n
@@ -162,30 +149,10 @@ def tile_picked_yvera_none_po_kernel(
             picked = [find("x%d_codes" % g, lo, hi) for g in range(PASSES)]
             return [(codes[:, a:b], x_sc[4 * g : P, lo:hi]) for g, (codes, a, b) in enumerate(picked)]
 
-        held = {}
-
-        def hold(kind, lo, hi, shape, dtype, **more):
-            more.setdefault("tag", "%s%d" % (kind, lo))
-            tile = keep.tile(shape, dtype, name="%s%d" % (kind, lo), align_bytes=64, **more)
-            held.setdefault(kind, []).append((lo, hi, tile))
-            return tile
-
-        def find(kind, lo, hi):
-            (found,) = [(a, tile) for a, b, tile in held[kind] if a <= lo and hi <= b]
-            return found[1], lo - found[0], hi - found[0]
-
         def leave_psum(banks, kind, lo, hi, **more):
             planes = hold(kind, lo, hi, [P, PACK, hi - lo], F32, **more)
             for ts, bank in banks:
                 nc.scalar.copy(planes[:, ts, :], bank[:])
-
-        def scale_by_adapter(table, src, dst, lo, hi, **more):
-            planes, a, b = find(src, lo, hi)
-            scaled = hold(dst, lo, hi, [P, PACK, hi - lo], F32, **more)
-            for t in range(PACK):
-                nc.vector.tensor_tensor(
-                    scaled[:, t, :], table[t][:].indirect(entries(ad_t, lo, hi)), planes[:, t, a:b], MULT
-                )
 
         def weave(copy, src, dst, dtype, lo, hi, **more):
             planes, a, b = find(src, lo, hi)
@@ -200,44 +167,37 @@ def tile_picked_yvera_none_po_kernel(
         out_rows = out_0.rearrange("(p t) s -> p t s", t=PACK)
         out_words = out_1[0].rearrange("p c r -> p (c r)").bitcast(I32)
 
-        def look_up(lo, hi):
-            planes = hold("ld_picked", lo, hi, [P, PACK, hi - lo], F32)
+        def look_up(lo, hi, **more):
+            planes = hold("ld_picked", lo, hi, [P, PACK, hi - lo], F32, **more)
             for t in range(PACK):
                 nc.vector.tensor_copy(planes[:, t, :], ld_t[t][:].indirect(entries(ad_t, lo, hi)))
 
-        def weave_ld(lo, hi):
-            weave(nc.scalar.copy, "ld_picked", "ld_woven", F32, lo, hi, tag="w1_%d_raw" % (lo // 256))
-
-        def inner_early(lo, hi):
-            h_bf = hold("h_bf", lo, hi, [P, (hi - lo) * PACK], BF16)
-            for at in range(lo, hi, P):
-                ((ts, bank),) = product("w1", tokens(at, at + P), P, "a_bank", 5)
-                if at < 2 * P:
-                    woven, a, b = find("ld_woven", at, at + P)
-                    y_woven = hold("y_woven", at, at + P, [P, P * PACK], F32)
-                    nc.scalar.copy(y_woven[:].rearrange("p (n t) -> p n t", t=PACK), bank[:].rearrange("p t n -> p n t"))
-                    nc.gpsimd.tensor_tensor(h_bf[:, at * PACK : (at + P) * PACK], y_woven[:], woven[:, a * PACK : b * PACK], MULT)
-                    continue
-                picked, a, b = find("ld_picked", at, at + P)
-                nc.vector.tensor_tensor(
-                    h_bf[:, (at - lo) * PACK : (at - lo + P) * PACK].rearrange("p (a i t) -> p a t i", i=4, t=PACK),
-                    bank[:].rearrange("p t (a i) -> p a t i", i=4),
-                    picked[:, :, a:b].rearrange("p t (a i) -> p a t i", i=4),
-                    MULT,
+        def weave_ld(lo, hi, tag):
+            picked, a, b = find("ld_picked", lo, hi)
+            woven = hold("ld_woven", lo, hi, [P, (hi - lo) * PACK], F32, tag=tag)
+            for at in range(0, hi - lo, 256):
+                end = min(at + 256, hi - lo)
+                nc.scalar.copy(
+                    woven[:, at * PACK : end * PACK].rearrange("p (a i t) -> p a t i", i=4, t=PACK),
+                    picked[:, :, a + at : a + end].rearrange("p t (a i) -> p a t i", i=4),
                 )
 
-        def first_product(lo, hi):
-            leave_psum(product("w1", tokens(lo, hi), hi - lo, "a_bank", 5), "y", lo, hi)
-
-        def inner_late(lo, hi):
-            scale_by_adapter(ld_t, "y", "h", lo, hi)
-
-        def round_h(lo, hi):
-            weave(nc.scalar.copy, "h", "h_bf", BF16, lo, hi)
-
-        def second(lo, hi):
-            quant_h(lo, hi)
-            second_product(lo, hi)
+        def inner(at):
+            h_bf, c, d = find("h_bf", at, at + P)
+            ((ts, bank),) = product("w1", tokens(at, at + P), P, "a_bank", 5)
+            if at < H_ON_GPSIMD:
+                woven, a, b = find("ld_woven", at, at + P)
+                y_woven = hold("y_woven", at, at + P, [P, P * PACK], F32)
+                nc.scalar.copy(y_woven[:].rearrange("p (n t) -> p n t", t=PACK), bank[:].rearrange("p t n -> p n t"))
+                nc.gpsimd.tensor_tensor(h_bf[:, c * PACK : d * PACK], y_woven[:], woven[:, a * PACK : b * PACK], MULT)
+                return
+            picked, a, b = find("ld_picked", at, at + P)
+            nc.vector.tensor_tensor(
+                h_bf[:, c * PACK : d * PACK].rearrange("p (a i t) -> p a t i", i=4, t=PACK),
+                bank[:].rearrange("p t (a i) -> p a t i", i=4),
+                picked[:, :, a:b].rearrange("p t (a i) -> p a t i", i=4),
+                MULT,
+            )
 
         def quant_h(lo, hi):
             h_bf, a, b = find("h_bf", lo, hi)
@@ -255,56 +215,20 @@ def tile_picked_yvera_none_po_kernel(
             for ts, bank in banks:
                 nc.scalar.copy(hold("rr_plane%d_" % ts.start, lo, hi, [P, 1, hi - lo], F32)[:], bank[:])
 
+        def scale_by_adapter(table, src, dst, lo, hi):
+            planes, a, b = find(src, lo, hi)
+            scaled = hold(dst, lo, hi, [P, PACK, hi - lo], F32)
+            for t in range(PACK):
+                nc.vector.tensor_tensor(
+                    scaled[:, t, :], table[t][:].indirect(entries(ad_t, lo, hi)), planes[:, t, a:b], MULT
+                )
+
         def outer(lo, hi):
             scale_by_adapter(lb_t, "rr", "term", lo, hi)
 
-        def outer_pair(pair, lo, hi, **more):
-            planes, a, b = find("rr", lo, hi)
-            scaled = hold("term%d_" % pair, lo, hi, [P, 2, hi - lo], F32, **more)
-            for u in range(2):
-                t = 2 * pair + u
-                nc.vector.tensor_tensor(
-                    scaled[:, u, :], lb_t[t][:].indirect(entries(ad_t, lo, hi)), planes[:, t, a:b], MULT
-                )
-
-        def outer_a(lo, hi):
-            outer_pair(0, lo, hi)
-
-        def outer_b(lo, hi):
-            outer_pair(1, lo, hi)
-
-        def outer_b_held(lo, hi):
-            outer_pair(1, lo, hi, tag="h512")
-
-        def total_pairs(lo, hi):
-            result = hold("result", lo, hi, [P, PACK, hi - lo], F32)
-            for ts, bank in product("w3", tokens(lo, hi), hi - lo, "e_bank", 3):
-                term, a, b = find("term%d_" % (ts.start // 2), lo, hi)
-                nc.vector.tensor_tensor(result[:, ts, :], term[:, :, a:b], bank[:], ADD)
-            nc.sync.dma_start(out_rows[:, :, lo:hi], result[:])
-
-        def total_pair(pair, lo, hi):
-            if pair == 0:
-                hold("result", lo, hi, [P, PACK, hi - lo], F32)
-                held["ee", lo] = product("w3", tokens(lo, hi), hi - lo, "e_bank", 3)
-            result, a, b = find("result", lo, hi)
-            ts, bank = held["ee", lo][pair]
-            term, a, b = find("term%d_" % pair, lo, hi)
-            nc.vector.tensor_tensor(result[:, ts, :], term[:, :, a:b], bank[:], ADD)
-            nc.sync.dma_start(out_rows[:, ts, lo:hi], result[:, ts, :])
-
-        def total_a(lo, hi):
-            total_pair(0, lo, hi)
-
-        def total_b(lo, hi):
-            total_pair(1, lo, hi)
-
-        def open_result(lo, hi):
-            hold("result", lo, hi, [P, PACK, hi - lo], F32, tag="rr512")
-
-        def outer_t(t, lo, hi, **more):
+        def outer_t(t, lo, hi):
             plane, a, b = find("rr_plane%d_" % t, lo, hi)
-            scaled = hold("plane%d_" % t, lo, hi, [P, hi - lo], F32, **more)
+            scaled = hold("plane%d_" % t, lo, hi, [P, hi - lo], F32)
             nc.vector.tensor_tensor(scaled[:], lb_t[t][:].indirect(entries(ad_t, lo, hi)), plane[:, 0, a:b], MULT)
 
         def total_t(t, lo, hi):
@@ -349,11 +273,8 @@ def tile_picked_yvera_none_po_kernel(
             nc.vector.tensor_tensor(result[:, 2, :], term[:, 2, a:b], upper[:, 0, :], ADD)
             nc.sync.dma_start(out_rows[:, :, lo:hi], result[:])
 
-        def round_out(lo, hi):
-            weave(nc.scalar.copy, "result", "o_bf", BF16, lo, hi)
-
-        def round_out_v(lo, hi):
-            weave(nc.vector.tensor_copy, "result", "o_bf", BF16, lo, hi)
+        def round_out(copy, lo, hi):
+            weave(copy, "result", "o_bf", BF16, lo, hi)
 
         def planes_out(lo, hi):
             o_bf, a, b = find("o_bf", lo, hi)
@@ -364,62 +285,63 @@ def tile_picked_yvera_none_po_kernel(
         def store_words(lo, hi):
             nc.sync.dma_start(out_words[:, lo:hi], out_codes[:, lo:hi].bitcast(I32))
 
-        look_up(0, 768)
+        look_up(0, HEAD)
         nc.vector.tensor_copy(x_sc[:], xs_in[:].indirect(offs_t[:]))
         round_weight("w1", 0)
         quantize_weight("w1", 0)
         round_weight("w1", 1)
-        gather0(0, 512)
-        gather0(512, 1024)
+        gather_words(0, 0, 512)
+        gather_words(0, 512, 1024)
         quantize_weight("w1", 1)
-        gather1(0, 256)
-        gather1(256, 512)
-        gather1(512, 1024)
-        weave_ld(0, 256)
-        inner_early(0, 512)
+        gather_words(1, 0, 256)
+        gather_words(1, 256, 512)
+        gather_words(1, 512, 1024)
+        weave_ld(0, 256, "w1_0_raw")
+        hold("h_bf", 0, HALF, [P, HALF * PACK], BF16)
+        hold("h_bf", HALF, PLAIN, [P, (PLAIN - HALF) * PACK], BF16)
+        for at in range(0, HALF, P):
+            inner(at)
         dealt["w2", 0] = keep.tile([P, PACK * 512], BF16, name="w2_bf", tag="w2_bf", align_bytes=64)
         for u in range(2):
             nc.scalar.copy(
                 dealt["w2", 0][:].rearrange("p (h u m j) -> p h m j u", h=2, u=2, j=PACK)[:, :, 64 * u : 64 * u + 64],
                 w2_halves[u][:].rearrange("p j (m h u) -> p h m j u", h=2, u=2),
             )
-        inner_early(512, 768)
-        first_product(768, 1024)
+        for at in range(HALF, PLAIN, P):
+            inner(at)
+        leave_psum(product("w1", tokens(PLAIN, S), S - PLAIN, "a_bank", 5), "y", PLAIN, S)
         quantize_weight("w2", 0)
-        second(0, 512)
-        inner_late(768, 1024)
-        quant_h(512, 768)
+        quant_h(0, HALF)
+        second_product(0, HALF)
+        scale_by_adapter(ld_t, "y", "h", PLAIN, S)
+        quant_h(HALF, PLAIN)
         round_weight("w3", 0)
-        round_h(768, 1024)
-        quant_h(768, 1024)
+        weave(nc.scalar.copy, "h", "h_bf", BF16, PLAIN, S)
+        quant_h(PLAIN, S)
         round_weight("w3", 1)
         quantize_weight("w3", 0)
         second_product(512, 768)
         second_product(768, 1024)
-        outer_t(0, 0, 512)
-        outer_t(1, 0, 512)
-        outer_t(2, 0, 512)
-        outer_t(3, 0, 512)
+        for t in range(PACK):
+            outer_t(t, 0, HALF)
         quantize_weight("w3", 1, tag="rr_plane3_0")
         outer(512, 768)
-        open_result(0, 512)
-        total_t(3, 0, 512)
-        total_t(0, 0, 512)
-        total_t(1, 0, 512)
-        total_t(2, 0, 512)
+        hold("result", 0, HALF, [P, PACK, HALF], F32, tag="rr512")
+        for t in (3, 0, 1, 2):
+            total_t(t, 0, HALF)
         total_shared(512, 768)
-        round_out(0, 256)
-        round_out(256, 512)
+        round_out(nc.scalar.copy, 0, 256)
+        round_out(nc.scalar.copy, 256, 512)
         planes_out(0, 256)
         planes_out(256, 512)
         store_words(0, 512)
-        round_out(512, 768)
+        round_out(nc.scalar.copy, 512, 768)
         outer(768, 1024)
         planes_out(512, 768)
         store_words(512, 768)
         total(768, 1024)
-        round_out(768, 896)
-        round_out_v(896, 1024)
+        round_out(nc.scalar.copy, 768, 896)
+        round_out(nc.vector.tensor_copy, 896, 1024)
         planes_out(768, 896)
         planes_out(896, 1024)
         store_words(768, 1024)

@@ -23,10 +23,11 @@ LIST_ROWS = 16
 BANK = 512
 HALF = S // 2
 LB_WINDOW = R + 32
-HEAD = 768
+HEAD = 832
 LD_WINDOW = HEAD + 32
-PLAIN = 768
+PLAIN = HEAD
 H_ON_GPSIMD = 256
+AT_H = 0
 
 
 def tile_picked_yvera_none_po_kernel(
@@ -124,11 +125,14 @@ def tile_picked_yvera_none_po_kernel(
             codes = hold("x%d_codes" % g, lo, hi, [P, hi - lo], U32)
             nc.vector.tensor_copy(codes[:], x_in[g][:].bitcast(U32).indirect(entries(offs_t, lo, hi)))
 
-        def product(name, moving, n, tag, bufs):
+        def take_bank(number, shape):
+            return psum.tile(shape, F32, name="bank%d" % number, tag="bank%d" % number, offset=number * BANK * 4)
+
+        def product(name, moving, n, numbers):
             per_bank = BANK // n
             banks = []
-            for b in range(PACK // per_bank):
-                bank = psum.tile([P, per_bank, n], F32, name=tag, tag=tag, bufs=bufs)
+            for b, number in enumerate(numbers):
+                bank = take_bank(number, [P, per_bank, n])
                 for g, (m_codes, m_scales) in enumerate(moving):
                     for u in range(per_bank):
                         t = b * per_bank + u
@@ -184,31 +188,43 @@ def tile_picked_yvera_none_po_kernel(
 
         def inner(at):
             h_bf, c, d = find("h_bf", at, at + P)
-            ((ts, bank),) = product("w1", tokens(at, at + P), P, "a_bank", 5)
+            ((ts, bank),) = product("w1", tokens(at, at + P), P, [(0, 1, 2, 3, 0, 1, 2, 4)[at // P]])
             if at < H_ON_GPSIMD:
                 woven, a, b = find("ld_woven", at, at + P)
                 y_woven = hold("y_woven", at, at + P, [P, P * PACK], F32)
                 nc.scalar.copy(y_woven[:].rearrange("p (n t) -> p n t", t=PACK), bank[:].rearrange("p t n -> p n t"))
                 nc.gpsimd.tensor_tensor(h_bf[:, c * PACK : d * PACK], y_woven[:], woven[:, a * PACK : b * PACK], MULT)
                 return
-            picked, a, b = find("ld_picked", at, at + P)
-            nc.vector.tensor_tensor(
-                h_bf[:, c * PACK : d * PACK].rearrange("p (a i t) -> p a t i", i=4, t=PACK),
-                bank[:].rearrange("p t (a i) -> p a t i", i=4),
-                picked[:, :, a:b].rearrange("p t (a i) -> p a t i", i=4),
-                MULT,
+            direct = max(0, min(P, PLAIN - at))
+            if direct > 0:
+                picked, a, b = find("ld_picked", at, at + direct)
+                nc.vector.tensor_tensor(
+                    h_bf[:, c * PACK : (c + direct) * PACK].rearrange("p (a i t) -> p a t i", i=4, t=PACK),
+                    bank[:, :, 0:direct].rearrange("p t (a i) -> p a t i", i=4),
+                    picked[:, :, a:b].rearrange("p t (a i) -> p a t i", i=4),
+                    MULT,
+                )
+            if direct < P:
+                y, a, b = find("y", at + direct, at + P)
+                nc.scalar.copy(y[:, :, a:b], bank[:, :, direct:P])
+
+        def round_late_h():
+            h_bf, a, b = find("h_bf", PLAIN, S)
+            nc.scalar.copy(
+                h_bf[:, a * PACK : b * PACK].rearrange("p (a i t) -> p a t i", i=4, t=PACK),
+                find("h", PLAIN, S)[0][:].rearrange("p t (a i) -> p a t i", i=4),
             )
 
-        def quant_h(lo, hi):
+        def quant_h(lo, hi, **more):
             h_bf, a, b = find("h_bf", lo, hi)
-            h_codes = hold("h_codes", lo, hi, [P, hi - lo], U32, tag="w2_bf" if lo == 0 else "h_codes%d" % lo)
+            h_codes = hold("h_codes", lo, hi, [P, hi - lo], U32, **more)
             h_scales = hold("h_scales", lo, hi, [P, hi - lo], U8)
             nc.vector.quantize_mx(out=h_codes[:].bitcast(FP8X4), scales=h_scales[:], in_=h_bf[:, a * PACK : b * PACK])
 
-        def second_product(lo, hi):
+        def second_product(lo, hi, numbers):
             h_codes, a, b = find("h_codes", lo, hi)
             h_scales, a, b = find("h_scales", lo, hi)
-            banks = product("w2", [(h_codes[:, a:b], h_scales[:, a:b])], hi - lo, "a_bank", 5)
+            banks = product("w2", [(h_codes[:, a:b], h_scales[:, a:b])], hi - lo, numbers)
             if lo > 0:
                 leave_psum(banks, "rr", lo, hi)
                 return
@@ -231,9 +247,9 @@ def tile_picked_yvera_none_po_kernel(
             scaled = hold("plane%d_" % t, lo, hi, [P, hi - lo], F32)
             nc.vector.tensor_tensor(scaled[:], lb_t[t][:].indirect(entries(ad_t, lo, hi)), plane[:, 0, a:b], MULT)
 
-        def total_t(t, lo, hi):
+        def total_t(t, lo, hi, number):
             result = find("result", lo, hi)[0]
-            bank = psum.tile([P, BANK], F32, name="e_bank", tag="e_bank", bufs=3)
+            bank = take_bank(number, [P, BANK])
             for g in range(PASSES):
                 for at in range(lo, hi, 256):
                     m_codes, m_scales = tokens(at, at + 256)[g]
@@ -258,14 +274,14 @@ def tile_picked_yvera_none_po_kernel(
         def total(lo, hi):
             term, a, b = find("term", lo, hi)
             result = hold("result", lo, hi, [P, PACK, hi - lo], F32)
-            for ts, bank in product("w3", tokens(lo, hi), hi - lo, "e_bank", 3):
+            for ts, bank in product("w3", tokens(lo, hi), hi - lo, [4, 0]):
                 nc.vector.tensor_tensor(result[:, ts, :], term[:, ts, a:b], bank[:], ADD)
                 nc.sync.dma_start(out_rows[:, ts, lo:hi], result[:, ts, :])
 
         def total_shared(lo, hi):
             term, a, b = find("term", lo, hi)
             result = hold("result", lo, hi, [P, PACK, hi - lo], F32)
-            (ts, lower), (ts, upper) = product("w3", tokens(lo, hi), hi - lo, "a_bank", 5)
+            (ts, lower), (ts, upper) = product("w3", tokens(lo, hi), hi - lo, [7, 3])
             frozen = hold("frozen", lo, hi, [P, hi - lo], F32)
             nc.scalar.copy(frozen[:], upper[:, 1, :])
             nc.gpsimd.tensor_tensor(result[:, 3, :], term[:, 3, a:b], frozen[:], ADD)
@@ -297,8 +313,9 @@ def tile_picked_yvera_none_po_kernel(
         gather_words(1, 256, 512)
         gather_words(1, 512, 1024)
         weave_ld(0, 256, "w1_0_raw")
-        hold("h_bf", 0, HALF, [P, HALF * PACK], BF16)
-        hold("h_bf", HALF, PLAIN, [P, (PLAIN - HALF) * PACK], BF16)
+        hold("h_bf", 0, HALF, [P, HALF * PACK], BF16, pool=reused, offset=AT_H)
+        hold("h_bf", HALF, 768, [P, 256 * PACK], BF16)
+        hold("h_bf", 768, S, [P, 256 * PACK], BF16)
         for at in range(0, HALF, P):
             inner(at)
         dealt["w2", 0] = keep.tile([P, PACK * 512], BF16, name="w2_bf", tag="w2_bf", align_bytes=64)
@@ -307,41 +324,40 @@ def tile_picked_yvera_none_po_kernel(
                 dealt["w2", 0][:].rearrange("p (h u m j) -> p h m j u", h=2, u=2, j=PACK)[:, :, 64 * u : 64 * u + 64],
                 w2_halves[u][:].rearrange("p j (m h u) -> p h m j u", h=2, u=2),
             )
-        for at in range(HALF, PLAIN, P):
+        hold("y", PLAIN, S, [P, PACK, S - PLAIN], F32)
+        for at in range(HALF, S, P):
             inner(at)
-        leave_psum(product("w1", tokens(PLAIN, S), S - PLAIN, "a_bank", 5), "y", PLAIN, S)
         quantize_weight("w2", 0)
-        quant_h(0, HALF)
-        second_product(0, HALF)
+        quant_h(0, HALF, tag="w2_bf")
+        second_product(0, HALF, [5, 6, 7, 3])
         scale_by_adapter(ld_t, "y", "h", PLAIN, S)
-        quant_h(HALF, PLAIN)
+        quant_h(HALF, 768, pool=reused, offset=AT_H)
         round_weight("w3", 0)
-        weave(nc.scalar.copy, "h", "h_bf", BF16, PLAIN, S)
-        quant_h(PLAIN, S)
+        round_late_h()
+        quant_h(768, S)
         round_weight("w3", 1)
         quantize_weight("w3", 0)
-        second_product(512, 768)
-        second_product(768, 1024)
+        second_product(512, 768, [4, 0])
+        second_product(768, 1024, [4, 0])
         for t in range(PACK):
             outer_t(t, 0, HALF)
         quantize_weight("w3", 1, tag="rr_plane3_0")
         outer(512, 768)
         hold("result", 0, HALF, [P, PACK, HALF], F32, tag="rr512")
-        for t in (3, 0, 1, 2):
-            total_t(t, 0, HALF)
+        for t, number in ((3, 1), (0, 2), (1, 5), (2, 6)):
+            total_t(t, 0, HALF, number)
         total_shared(512, 768)
-        round_out(nc.scalar.copy, 0, 256)
-        round_out(nc.scalar.copy, 256, 512)
+        for lo in range(0, 768, 256):
+            round_out(nc.scalar.copy, lo, lo + 256)
         planes_out(0, 256)
-        planes_out(256, 512)
-        store_words(0, 512)
-        round_out(nc.scalar.copy, 512, 768)
+        store_words(0, 256)
         outer(768, 1024)
-        planes_out(512, 768)
-        store_words(512, 768)
         total(768, 1024)
         round_out(nc.scalar.copy, 768, 896)
         round_out(nc.vector.tensor_copy, 896, 1024)
+        planes_out(256, 512)
+        planes_out(512, 768)
+        store_words(256, 768)
         planes_out(768, 896)
         planes_out(896, 1024)
         store_words(768, 1024)

@@ -112,8 +112,8 @@ def tile_picked_yvera_none_po_kernel(
         x_in[0] = load_words(0)
         w2_rows = w2.rearrange("(p j) c -> p j c", j=PACK)
         w2_halves = [keep.tile([P, PACK, 256], F32, name="w2_half%d" % u, align_bytes=64) for u in range(2)]
-        x_in[1] = load_words(1)
         nc.sync.dma_start(w2_halves[0][:], w2_rows[:, :, 0:256])
+        x_in[1] = load_words(1)
         nc.sync.dma_start(w2_halves[1][:], w2_rows[:, :, 256:512])
         raw["w3", 0] = load_weight(w3, 0, "w3_0")
         raw["w3", 1] = load_weight(w3, 1, "w3_1")

@@ -1,6 +1,7 @@
 from contextlib import ExitStack
 
 import concourse.mybir as mybir
+from concourse.masks import make_identity
 
 K, T, S, H, N, R = 1024, 2048, 1024, 512, 512, 512
 FLOPS = 2 * S * (K * H + K * N + H * N)
@@ -67,7 +68,7 @@ def tile_picked_yvera_none_po_kernel(
             nc.sync.dma_start(rows[:], w[g * K_PASS : (g + 1) * K_PASS, :].rearrange("(p j) c -> p j c", j=PACK))
             return rows
 
-        def load_table(table, name, window):
+        def load_table(table, name, window, after_first=None):
             rows = table.rearrange("(p t) r -> t p r", t=PACK)
             tiles = []
             for t in range(PACK):
@@ -75,6 +76,8 @@ def tile_picked_yvera_none_po_kernel(
                 nc.gpsimd.memset(plane[:, R:window], 0.0)
                 nc.sync.dma_start(plane[:, 0:R], rows[t])
                 tiles.append(plane)
+                if t == 0 and after_first is not None:
+                    nc.sync.dma_start(*after_first)
             return tiles
 
         raw = {}
@@ -99,8 +102,7 @@ def tile_picked_yvera_none_po_kernel(
         xs_in = keep.tile([P, T], U8, name="xs_in")
         nc.vector.memset(xs_in[:].bitcast(I32), 0)
         x_in = [None] * PASSES
-        nc.sync.dma_start(ad_t[:], ad)
-        ld_t = load_table(ld, "ld", LD_WINDOW)
+        ld_t = load_table(ld, "ld", LD_WINDOW, (ad_t[:], ad))
         raw["w1", 0] = load_weight(w1, 0, "w1_0")
         nc.sync.dma_start(offs_t[:], offs)
         raw["w1", 1] = load_weight(w1, 1, "w1_1")
@@ -119,6 +121,8 @@ def tile_picked_yvera_none_po_kernel(
         raw["w3", 1] = load_weight(w3, 1, "w3_1")
         lb_t = load_table(lb, "lb", LB_WINDOW)
 
+        identity = keep.tile([P, P], F32, name="identity")
+        make_identity(nc, identity[:])
         x_sc = keep.tile([P, S], U8, name="x_sc", align_bytes=64)
 
         def gather_words(g, lo, hi):
@@ -128,10 +132,10 @@ def tile_picked_yvera_none_po_kernel(
         def take_bank(number, shape):
             return psum.tile(shape, F32, name="bank%d" % number, tag="bank%d" % number, offset=number * BANK * 4)
 
-        def product(name, moving, n, numbers):
+        def product(name, moving, n, numbers, first=0):
             per_bank = BANK // n
             banks = []
-            for b, number in enumerate(numbers):
+            for b, number in enumerate(numbers, first):
                 bank = take_bank(number, [P, per_bank, n])
                 for g, (m_codes, m_scales) in enumerate(moving):
                     for u in range(per_bank):
@@ -231,16 +235,21 @@ def tile_picked_yvera_none_po_kernel(
             for ts, bank in banks:
                 nc.scalar.copy(hold("rr_plane%d_" % ts.start, lo, hi, [P, 1, hi - lo], F32)[:], bank[:])
 
-        def scale_by_adapter(table, src, dst, lo, hi):
+        def last_product(pair, number):
+            moving = (find("h_codes", 768, S)[0][:], find("h_scales", 768, S)[0][:])
+            ((ts, bank),) = product("w2", [moving], 256, [number], pair)
+            nc.scalar.copy(find("rr", 768, S)[0][:, ts, :], bank[:])
+
+        def scale_by_adapter(table, src, dst, lo, hi, order=range(PACK), **more):
             planes, a, b = find(src, lo, hi)
-            scaled = hold(dst, lo, hi, [P, PACK, hi - lo], F32)
-            for t in range(PACK):
+            scaled = hold(dst, lo, hi, [P, PACK, hi - lo], F32, **more)
+            for t in order:
                 nc.vector.tensor_tensor(
                     scaled[:, t, :], table[t][:].indirect(entries(ad_t, lo, hi)), planes[:, t, a:b], MULT
                 )
 
-        def outer(lo, hi):
-            scale_by_adapter(lb_t, "rr", "term", lo, hi)
+        def outer(lo, hi, **more):
+            scale_by_adapter(lb_t, "rr", "term", lo, hi, **more)
 
         def outer_t(t, lo, hi):
             plane, a, b = find("rr_plane%d_" % t, lo, hi)
@@ -271,6 +280,43 @@ def tile_picked_yvera_none_po_kernel(
                 nc.vector.tensor_tensor(result[:, t, :], find("plane%d_" % t, lo, hi)[0][:], bank[:], ADD)
             nc.sync.dma_start(out_rows[:, t, lo:hi], result[:, t, :])
 
+        def turn_term(t, number):
+            plane = find("plane%d_" % t, 0, HALF)[0]
+            bank = take_bank(number, [P, BANK])
+            for at in range(0, HALF, P):
+                nc.tensor.transpose(bank[:, at : at + P], plane[:, at : at + P], identity[:])
+            nc.scalar.copy(hold("term_turned", 0, HALF, [P, HALF], F32, tag="w3_1_raw")[:], bank[:])
+
+        def frozen_turned(t, number):
+            bank = take_bank(number, [P, BANK])
+            for g in range(PASSES):
+                w_codes, w_scales = weight["w3", g]
+                for at in range(0, HALF, P):
+                    x_codes, x_scale = tokens(at, at + P)[g]
+                    nc.tensor.matmul_mx(
+                        out=bank[:, at : at + P],
+                        lhsT=x_codes.bitcast(FP8X4),
+                        lhsT_scale=x_scale,
+                        rhs=w_codes[:, t * P : (t + 1) * P].bitcast(FP8X4),
+                        rhs_scale=w_scales[:, t * P : (t + 1) * P],
+                        start=(g == 0 and at == 0),
+                        stop=(g == PASSES - 1 and at == HALF - P),
+                    )
+            frozen = hold("frozen_turned", 0, HALF, [P, HALF], F32)
+            nc.scalar.copy(frozen[:], bank[:])
+
+        def sum_on_tensor(t, number):
+            bank = take_bank(number, [P, BANK])
+            for n, turned in enumerate((find("term_turned", 0, HALF)[0], find("frozen_turned", 0, HALF)[0])):
+                for at in range(0, HALF, P):
+                    nc.tensor.matmul(
+                        bank[:, at : at + P], turned[:, at : at + P], identity[:],
+                        start=(n == 0 and at == 0), stop=(n == 1 and at == HALF - P), is_transpose=True,
+                    )
+            result = find("result", 0, HALF)[0]
+            nc.scalar.copy(result[:, t, :], bank[:])
+            nc.sync.dma_start(out_rows[:, t, 0:HALF], result[:, t, :])
+
         def total(lo, hi):
             term, a, b = find("term", lo, hi)
             result = hold("result", lo, hi, [P, PACK, hi - lo], F32)
@@ -289,8 +335,8 @@ def tile_picked_yvera_none_po_kernel(
             nc.vector.tensor_tensor(result[:, 2, :], term[:, 2, a:b], upper[:, 0, :], ADD)
             nc.sync.dma_start(out_rows[:, :, lo:hi], result[:])
 
-        def round_out(copy, lo, hi):
-            weave(copy, "result", "o_bf", BF16, lo, hi)
+        def round_out(copy, lo, hi, **more):
+            weave(copy, "result", "o_bf", BF16, lo, hi, **more)
 
         def planes_out(lo, hi):
             o_bf, a, b = find("o_bf", lo, hi)
@@ -338,26 +384,32 @@ def tile_picked_yvera_none_po_kernel(
         round_weight("w3", 1)
         quantize_weight("w3", 0)
         second_product(512, 768, [4, 0])
-        second_product(768, 1024, [4, 0])
         for t in range(PACK):
             outer_t(t, 0, HALF)
+        turn_term(0, 6)
+        hold("rr", 768, S, [P, PACK, 256], F32)
+        last_product(0, 4)
         quantize_weight("w3", 1, tag="rr_plane3_0")
-        outer(512, 768)
-        hold("result", 0, HALF, [P, PACK, HALF], F32, tag="rr512")
-        for t, number in ((3, 1), (0, 2), (1, 5), (2, 6)):
-            total_t(t, 0, HALF, number)
+        outer(512, 768, order=(0, 1, 3, 2))
         total_shared(512, 768)
-        for lo in range(0, 768, 256):
+        hold("result", 0, HALF, [P, PACK, HALF], F32, tag="rr512")
+        total_t(3, 0, HALF, 1)
+        frozen_turned(0, 2)
+        last_product(1, 0)
+        total_t(1, 0, HALF, 5)
+        total_t(2, 0, HALF, 6)
+        sum_on_tensor(0, 2)
+        for lo in (512, 0, 256):
             round_out(nc.scalar.copy, lo, lo + 256)
-        planes_out(0, 256)
-        store_words(0, 256)
-        outer(768, 1024)
+        planes_out(512, 768)
+        store_words(512, 768)
+        outer(768, 1024, tag="plane1_0")
         total(768, 1024)
         round_out(nc.scalar.copy, 768, 896)
-        round_out(nc.vector.tensor_copy, 896, 1024)
+        planes_out(0, 256)
         planes_out(256, 512)
-        planes_out(512, 768)
-        store_words(256, 768)
+        store_words(0, 512)
+        round_out(nc.vector.tensor_copy, 896, 1024, tag="o_bf256")
         planes_out(768, 896)
         planes_out(896, 1024)
         store_words(768, 1024)

@@ -20,15 +20,27 @@ P = 128
 PACK = 4
 K_PASS = P * PACK
 PASSES = K // K_PASS
+COLUMNS = 512
 LIST_ROWS = 16
 BANK = 512
 HALF = S // 2
-LB_WINDOW = R + 32
-HEAD = 832
-LD_WINDOW = HEAD + 32
-PLAIN = HEAD
+QUARTER = S // 4
+LAST = S - QUARTER
+SPARE = 32
+HEAD = 896
+LD_WINDOW = HEAD + SPARE
+LB_WINDOW = HALF + SPARE
 H_ON_GPSIMD = 256
-AT_H = 0
+SPLIT = LAST + P
+
+Y_BANKS = (0, 1, 2, 3, 0, 1, 2, 4)
+RR_FIRST_HALF = (5, 6, 7, 3)
+RR_THIRD_QUARTER = (4, 0)
+RR_LAST_QUARTER = (4, 0)
+EE_FIRST_HALF = {3: 1, 0: 2, 1: 5, 2: 6}
+EE_THIRD_QUARTER = (7, 3)
+EE_LAST_QUARTER = (4, 0)
+TURNED_TERM = 6
 
 
 def tile_picked_yvera_none_po_kernel(
@@ -48,9 +60,9 @@ def tile_picked_yvera_none_po_kernel(
 
         held = {}
 
-        def hold(kind, lo, hi, shape, dtype, pool=keep, **more):
-            more.setdefault("tag", "%s%d" % (kind, lo))
-            tile = pool.tile(shape, dtype, name="%s%d" % (kind, lo), align_bytes=64, **more)
+        def hold(kind, lo, hi, shape, dtype, pool=keep, **place):
+            place.setdefault("tag", "%s%d" % (kind, lo))
+            tile = pool.tile(shape, dtype, name="%s%d" % (kind, lo), align_bytes=64, **place)
             held.setdefault(kind, []).append((lo, hi, tile))
             return tile
 
@@ -58,51 +70,45 @@ def tile_picked_yvera_none_po_kernel(
             (found,) = [(a, tile) for a, b, tile in held[kind] if a <= lo and hi <= b]
             return found[1], lo - found[0], hi - found[0]
 
-        def load_words(g, pool=keep, **more):
-            words = pool.tile([P, T], I32, name="x_in%d" % g, align_bytes=64, **more)
+        def load_words(g):
+            words = keep.tile([P, T], I32, name="x_in%d" % g, align_bytes=64)
             nc.sync.dma_start(words[:], x_words[g].rearrange("p c r -> p (c r)").bitcast(I32))
             return words
 
         def load_weight(w, g, name):
-            rows = keep.tile([P, PACK, 512], F32, name=name + "_raw", tag=name + "_raw", align_bytes=64)
+            rows = keep.tile([P, PACK, COLUMNS], F32, name=name + "_raw", tag=name + "_raw", align_bytes=64)
             nc.sync.dma_start(rows[:], w[g * K_PASS : (g + 1) * K_PASS, :].rearrange("(p j) c -> p j c", j=PACK))
             return rows
 
-        def load_table(table, name, window, after_first=None):
-            rows = table.rearrange("(p t) r -> t p r", t=PACK)
-            tiles = []
-            for t in range(PACK):
-                plane = keep.tile([P, window], F32, name="%s%d" % (name, t))
-                nc.gpsimd.memset(plane[:, R:window], 0.0)
-                nc.sync.dma_start(plane[:, 0:R], rows[t])
-                tiles.append(plane)
-                if t == 0 and after_first is not None:
-                    nc.sync.dma_start(*after_first)
-            return tiles
+        def load_plane(table, name, window, t):
+            plane = keep.tile([P, window], F32, name="%s%d" % (name, t))
+            nc.gpsimd.memset(plane[:, R:window], 0.0)
+            nc.sync.dma_start(plane[:, 0:R], table.rearrange("(p t) r -> t p r", t=PACK)[t])
+            return plane
 
         raw = {}
         dealt = {}
         weight = {}
 
         def round_weight(name, g):
-            dealt[name, g] = keep.tile([P, PACK * 512], BF16, name="%s_%d_bf" % (name, g), tag="%s_%d_bf" % (name, g), align_bytes=64)
+            label = "%s_%d_bf" % (name, g)
+            dealt[name, g] = keep.tile([P, PACK * COLUMNS], BF16, name=label, tag=label, align_bytes=64)
             nc.scalar.copy(
                 dealt[name, g][:].rearrange("p (h u m j) -> p h m j u", h=2, u=2, j=PACK),
                 raw[name, g][:].rearrange("p j (m h u) -> p h m j u", h=2, u=2),
             )
 
-        def quantize_weight(name, g, pool=keep, **more):
-            label = "%s_%d_codes" % (name, g)
-            more.setdefault("tag", label)
-            codes = pool.tile([P, 512], U32, name=label, align_bytes=64, **more)
-            scales = keep.tile([P, 512], U8, name="%s_%d_scales" % (name, g), align_bytes=64)
+        def quantize_weight(name, g):
+            codes = keep.tile([P, COLUMNS], U32, name="%s_%d_codes" % (name, g), align_bytes=64)
+            scales = keep.tile([P, COLUMNS], U8, name="%s_%d_scales" % (name, g), align_bytes=64)
             nc.vector.quantize_mx(out=codes[:].bitcast(FP8X4), scales=scales[:], in_=dealt[name, g][:])
             weight[name, g] = (codes, scales)
 
         xs_in = keep.tile([P, T], U8, name="xs_in")
         nc.vector.memset(xs_in[:].bitcast(I32), 0)
-        x_in = [None] * PASSES
-        ld_t = load_table(ld, "ld", LD_WINDOW, (ad_t[:], ad))
+        ld_t = [load_plane(ld, "ld", LD_WINDOW, 0)]
+        nc.sync.dma_start(ad_t[:], ad)
+        ld_t += [load_plane(ld, "ld", LD_WINDOW, t) for t in range(1, PACK)]
         raw["w1", 0] = load_weight(w1, 0, "w1_0")
         nc.sync.dma_start(offs_t[:], offs)
         raw["w1", 1] = load_weight(w1, 1, "w1_1")
@@ -111,15 +117,16 @@ def tile_picked_yvera_none_po_kernel(
                 xs_in[32 * q : 32 * q + 4 * PASSES, :].bitcast(I32),
                 x_scales[:, 4 * q : 4 * q + 4, :].bitcast(I32),
             )
-        x_in[0] = load_words(0)
+        x_in = [load_words(0)]
         w2_rows = w2.rearrange("(p j) c -> p j c", j=PACK)
-        w2_halves = [keep.tile([P, PACK, 256], F32, name="w2_half%d" % u, align_bytes=64) for u in range(2)]
-        nc.sync.dma_start(w2_halves[0][:], w2_rows[:, :, 0:256])
-        x_in[1] = load_words(1)
-        nc.sync.dma_start(w2_halves[1][:], w2_rows[:, :, 256:512])
+        half = COLUMNS // 2
+        w2_halves = [keep.tile([P, PACK, half], F32, name="w2_half%d" % u, align_bytes=64) for u in range(2)]
+        nc.sync.dma_start(w2_halves[0][:], w2_rows[:, :, 0:half])
+        x_in.append(load_words(1))
+        nc.sync.dma_start(w2_halves[1][:], w2_rows[:, :, half:COLUMNS])
         raw["w3", 0] = load_weight(w3, 0, "w3_0")
         raw["w3", 1] = load_weight(w3, 1, "w3_1")
-        lb_t = load_table(lb, "lb", LB_WINDOW)
+        lb_t = [load_plane(lb, "lb", LB_WINDOW, t) for t in range(PACK)]
 
         identity = keep.tile([P, P], F32, name="identity")
         make_identity(nc, identity[:])
@@ -157,262 +164,230 @@ def tile_picked_yvera_none_po_kernel(
             picked = [find("x%d_codes" % g, lo, hi) for g in range(PASSES)]
             return [(codes[:, a:b], x_sc[4 * g : P, lo:hi]) for g, (codes, a, b) in enumerate(picked)]
 
-        def leave_psum(banks, kind, lo, hi, **more):
-            planes = hold(kind, lo, hi, [P, PACK, hi - lo], F32, **more)
-            for ts, bank in banks:
-                nc.scalar.copy(planes[:, ts, :], bank[:])
+        def as_woven(ap):
+            return ap.rearrange("p (a i t) -> p a t i", i=4, t=PACK)
 
-        def weave(copy, src, dst, dtype, lo, hi, **more):
-            planes, a, b = find(src, lo, hi)
-            woven = hold(dst, lo, hi, [P, (hi - lo) * PACK], dtype, **more)
-            copy(
-                woven[:].rearrange("p (a i t) -> p a t i", i=4, t=PACK),
-                planes[:, :, a:b].rearrange("p t (a i) -> p a t i", i=4),
-            )
+        def as_planes(ap):
+            return ap.rearrange("p t (a i) -> p a t i", i=4)
 
         out_codes = keep.tile([P, S], U32, name="out_codes", align_bytes=64)
         out_scales = keep.tile([P, S], U8, name="out_scales", align_bytes=64)
         out_rows = out_0.rearrange("(p t) s -> p t s", t=PACK)
         out_words = out_1[0].rearrange("p c r -> p (c r)").bitcast(I32)
 
-        def look_up(lo, hi, **more):
-            planes = hold("ld_picked", lo, hi, [P, PACK, hi - lo], F32, **more)
-            for t in range(PACK):
-                nc.vector.tensor_copy(planes[:, t, :], ld_t[t][:].indirect(entries(ad_t, lo, hi)))
-
-        def weave_ld(lo, hi, tag):
-            picked, a, b = find("ld_picked", lo, hi)
-            woven = hold("ld_woven", lo, hi, [P, (hi - lo) * PACK], F32, tag=tag)
-            for at in range(0, hi - lo, 256):
-                end = min(at + 256, hi - lo)
-                nc.scalar.copy(
-                    woven[:, at * PACK : end * PACK].rearrange("p (a i t) -> p a t i", i=4, t=PACK),
-                    picked[:, :, a + at : a + end].rearrange("p t (a i) -> p a t i", i=4),
-                )
-
-        def inner(at):
+        def form_h(at):
             h_bf, c, d = find("h_bf", at, at + P)
-            ((ts, bank),) = product("w1", tokens(at, at + P), P, [(0, 1, 2, 3, 0, 1, 2, 4)[at // P]])
+            ((ts, bank),) = product("w1", tokens(at, at + P), P, [Y_BANKS[at // P]])
             if at < H_ON_GPSIMD:
-                woven, a, b = find("ld_woven", at, at + P)
                 y_woven = hold("y_woven", at, at + P, [P, P * PACK], F32)
                 nc.scalar.copy(y_woven[:].rearrange("p (n t) -> p n t", t=PACK), bank[:].rearrange("p t n -> p n t"))
-                nc.gpsimd.tensor_tensor(h_bf[:, c * PACK : d * PACK], y_woven[:], woven[:, a * PACK : b * PACK], MULT)
+                nc.gpsimd.tensor_tensor(
+                    h_bf[:, c * PACK : d * PACK], y_woven[:], ld_woven[:, at * PACK : (at + P) * PACK], MULT
+                )
                 return
-            direct = max(0, min(P, PLAIN - at))
+            direct = max(0, min(P, HEAD - at))
             if direct > 0:
-                picked, a, b = find("ld_picked", at, at + direct)
                 nc.vector.tensor_tensor(
-                    h_bf[:, c * PACK : (c + direct) * PACK].rearrange("p (a i t) -> p a t i", i=4, t=PACK),
-                    bank[:, :, 0:direct].rearrange("p t (a i) -> p a t i", i=4),
-                    picked[:, :, a:b].rearrange("p t (a i) -> p a t i", i=4),
+                    as_woven(h_bf[:, c * PACK : (c + direct) * PACK]),
+                    as_planes(bank[:, :, 0:direct]),
+                    as_planes(ld_picked[:, :, at : at + direct]),
                     MULT,
                 )
             if direct < P:
                 y, a, b = find("y", at + direct, at + P)
                 nc.scalar.copy(y[:, :, a:b], bank[:, :, direct:P])
 
-        def round_late_h():
-            h_bf, a, b = find("h_bf", PLAIN, S)
-            nc.scalar.copy(
-                h_bf[:, a * PACK : b * PACK].rearrange("p (a i t) -> p a t i", i=4, t=PACK),
-                find("h", PLAIN, S)[0][:].rearrange("p t (a i) -> p a t i", i=4),
-            )
-
-        def quant_h(lo, hi, **more):
-            h_bf, a, b = find("h_bf", lo, hi)
-            h_codes = hold("h_codes", lo, hi, [P, hi - lo], U32, **more)
+        def quantize_h(lo, hi, **place):
+            h_codes = hold("h_codes", lo, hi, [P, hi - lo], U32, **place)
             h_scales = hold("h_scales", lo, hi, [P, hi - lo], U8)
-            nc.vector.quantize_mx(out=h_codes[:].bitcast(FP8X4), scales=h_scales[:], in_=h_bf[:, a * PACK : b * PACK])
+            nc.vector.quantize_mx(out=h_codes[:].bitcast(FP8X4), scales=h_scales[:], in_=find("h_bf", lo, hi)[0][:])
 
-        def second_product(lo, hi, numbers):
-            h_codes, a, b = find("h_codes", lo, hi)
-            h_scales, a, b = find("h_scales", lo, hi)
-            banks = product("w2", [(h_codes[:, a:b], h_scales[:, a:b])], hi - lo, numbers)
-            if lo > 0:
-                leave_psum(banks, "rr", lo, hi)
-                return
-            for ts, bank in banks:
-                nc.scalar.copy(hold("rr_plane%d_" % ts.start, lo, hi, [P, 1, hi - lo], F32)[:], bank[:])
+        def rr_banks(lo, hi, numbers, first=0):
+            moving = (find("h_codes", lo, hi)[0][:], find("h_scales", lo, hi)[0][:])
+            return product("w2", [moving], hi - lo, numbers, first)
 
-        def last_product(pair, number):
-            moving = (find("h_codes", 768, S)[0][:], find("h_scales", 768, S)[0][:])
-            ((ts, bank),) = product("w2", [moving], 256, [number], pair)
-            nc.scalar.copy(find("rr", 768, S)[0][:, ts, :], bank[:])
+        def rr_last_quarter(pair):
+            ((ts, bank),) = rr_banks(LAST, S, [RR_LAST_QUARTER[pair]], pair)
+            nc.scalar.copy(find("rr", LAST, S)[0][:, ts, :], bank[:])
 
-        def scale_by_adapter(table, src, dst, lo, hi, order=range(PACK), **more):
-            planes, a, b = find(src, lo, hi)
-            scaled = hold(dst, lo, hi, [P, PACK, hi - lo], F32, **more)
+        def scale_by_adapter(table, src, dst, lo, hi, order=range(PACK), **place):
+            planes = find(src, lo, hi)[0]
+            scaled = hold(dst, lo, hi, [P, PACK, hi - lo], F32, **place)
             for t in order:
                 nc.vector.tensor_tensor(
-                    scaled[:, t, :], table[t][:].indirect(entries(ad_t, lo, hi)), planes[:, t, a:b], MULT
+                    scaled[:, t, :], table[t][:].indirect(entries(ad_t, lo, hi)), planes[:, t, :], MULT
                 )
 
-        def outer(lo, hi, **more):
-            scale_by_adapter(lb_t, "rr", "term", lo, hi, **more)
-
-        def outer_t(t, lo, hi):
-            plane, a, b = find("rr_plane%d_" % t, lo, hi)
-            scaled = hold("plane%d_" % t, lo, hi, [P, hi - lo], F32)
-            nc.vector.tensor_tensor(scaled[:], lb_t[t][:].indirect(entries(ad_t, lo, hi)), plane[:, 0, a:b], MULT)
-
-        def total_t(t, lo, hi, number):
-            result = find("result", lo, hi)[0]
-            bank = take_bank(number, [P, BANK])
+        def total_plane(t):
+            result = find("result", 0, HALF)[0]
+            bank = take_bank(EE_FIRST_HALF[t], [P, BANK])
             for g in range(PASSES):
-                for at in range(lo, hi, 256):
-                    m_codes, m_scales = tokens(at, at + 256)[g]
+                for at in range(0, HALF, QUARTER):
+                    m_codes, m_scales = tokens(at, at + QUARTER)[g]
                     w_codes, w_scales = weight["w3", g]
                     nc.tensor.matmul_mx(
-                        out=bank[:, at - lo : at - lo + 256],
+                        out=bank[:, at : at + QUARTER],
                         lhsT=w_codes[:, t * P : (t + 1) * P].bitcast(FP8X4),
                         lhsT_scale=w_scales[:, t * P : (t + 1) * P],
                         rhs=m_codes.bitcast(FP8X4),
                         rhs_scale=m_scales,
-                        start=(g == 0 and at == lo),
-                        stop=(g == PASSES - 1 and at == hi - 256),
+                        start=(g == 0 and at == 0),
+                        stop=(g == PASSES - 1 and at == HALF - QUARTER),
                     )
             if t == PACK - 1:
-                frozen = hold("frozen", lo, hi, [P, hi - lo], F32)
-                nc.scalar.copy(frozen[:], bank[:])
-                nc.gpsimd.tensor_tensor(result[:, t, :], find("plane%d_" % t, lo, hi)[0][:], frozen[:], ADD)
+                ee = hold("ee", 0, HALF, [P, HALF], F32)
+                nc.scalar.copy(ee[:], bank[:])
+                nc.gpsimd.tensor_tensor(result[:, t, :], term_plane[t][:], ee[:], ADD)
             else:
-                nc.vector.tensor_tensor(result[:, t, :], find("plane%d_" % t, lo, hi)[0][:], bank[:], ADD)
-            nc.sync.dma_start(out_rows[:, t, lo:hi], result[:, t, :])
-
-        def turn_term(t, number):
-            plane = find("plane%d_" % t, 0, HALF)[0]
-            bank = take_bank(number, [P, BANK])
-            for at in range(0, HALF, P):
-                nc.tensor.transpose(bank[:, at : at + P], plane[:, at : at + P], identity[:])
-            nc.scalar.copy(hold("term_turned", 0, HALF, [P, HALF], F32, tag="w3_1_raw")[:], bank[:])
-
-        def frozen_turned(t, number):
-            bank = take_bank(number, [P, BANK])
-            for g in range(PASSES):
-                w_codes, w_scales = weight["w3", g]
-                for at in range(0, HALF, P):
-                    x_codes, x_scale = tokens(at, at + P)[g]
-                    nc.tensor.matmul_mx(
-                        out=bank[:, at : at + P],
-                        lhsT=x_codes.bitcast(FP8X4),
-                        lhsT_scale=x_scale,
-                        rhs=w_codes[:, t * P : (t + 1) * P].bitcast(FP8X4),
-                        rhs_scale=w_scales[:, t * P : (t + 1) * P],
-                        start=(g == 0 and at == 0),
-                        stop=(g == PASSES - 1 and at == HALF - P),
-                    )
-            frozen = hold("frozen_turned", 0, HALF, [P, HALF], F32)
-            nc.scalar.copy(frozen[:], bank[:])
-
-        def sum_on_tensor(t, number):
-            bank = take_bank(number, [P, BANK])
-            for n, turned in enumerate((find("term_turned", 0, HALF)[0], find("frozen_turned", 0, HALF)[0])):
-                for at in range(0, HALF, P):
-                    nc.tensor.matmul(
-                        bank[:, at : at + P], turned[:, at : at + P], identity[:],
-                        start=(n == 0 and at == 0), stop=(n == 1 and at == HALF - P), is_transpose=True,
-                    )
-            result = find("result", 0, HALF)[0]
-            nc.scalar.copy(result[:, t, :], bank[:])
+                nc.vector.tensor_tensor(result[:, t, :], term_plane[t][:], bank[:], ADD)
             nc.sync.dma_start(out_rows[:, t, 0:HALF], result[:, t, :])
 
-        def total(lo, hi):
-            term, a, b = find("term", lo, hi)
-            result = hold("result", lo, hi, [P, PACK, hi - lo], F32)
-            for ts, bank in product("w3", tokens(lo, hi), hi - lo, [4, 0]):
-                nc.vector.tensor_tensor(result[:, ts, :], term[:, ts, a:b], bank[:], ADD)
-                nc.sync.dma_start(out_rows[:, ts, lo:hi], result[:, ts, :])
+        def round_out(copy, lo, hi, **place):
+            result, a, b = find("result", lo, hi)
+            woven = hold("o_bf", lo, hi, [P, (hi - lo) * PACK], BF16, **place)
+            copy(as_woven(woven[:]), as_planes(result[:, :, a:b]))
 
-        def total_shared(lo, hi):
-            term, a, b = find("term", lo, hi)
-            result = hold("result", lo, hi, [P, PACK, hi - lo], F32)
-            (ts, lower), (ts, upper) = product("w3", tokens(lo, hi), hi - lo, [7, 3])
-            frozen = hold("frozen", lo, hi, [P, hi - lo], F32)
-            nc.scalar.copy(frozen[:], upper[:, 1, :])
-            nc.gpsimd.tensor_tensor(result[:, 3, :], term[:, 3, a:b], frozen[:], ADD)
-            nc.vector.tensor_tensor(result[:, 0:2, :], term[:, 0:2, a:b], lower[:], ADD)
-            nc.vector.tensor_tensor(result[:, 2, :], term[:, 2, a:b], upper[:, 0, :], ADD)
-            nc.sync.dma_start(out_rows[:, :, lo:hi], result[:])
-
-        def round_out(copy, lo, hi, **more):
-            weave(copy, "result", "o_bf", BF16, lo, hi, **more)
-
-        def planes_out(lo, hi):
-            o_bf, a, b = find("o_bf", lo, hi)
+        def quantize_out(lo, hi):
             nc.vector.quantize_mx(
-                out=out_codes[:, lo:hi].bitcast(FP8X4), scales=out_scales[:, lo:hi], in_=o_bf[:, a * PACK : b * PACK]
+                out=out_codes[:, lo:hi].bitcast(FP8X4), scales=out_scales[:, lo:hi], in_=find("o_bf", lo, hi)[0][:]
             )
 
         def store_words(lo, hi):
             nc.sync.dma_start(out_words[:, lo:hi], out_codes[:, lo:hi].bitcast(I32))
 
-        look_up(0, HEAD)
+        ld_picked = hold("ld_picked", 0, HEAD, [P, PACK, HEAD], F32)
+        for t in range(PACK):
+            nc.vector.tensor_copy(ld_picked[:, t, :], ld_t[t][:].indirect(entries(ad_t, 0, HEAD)))
         nc.vector.tensor_copy(x_sc[:], xs_in[:].indirect(offs_t[:]))
         round_weight("w1", 0)
         quantize_weight("w1", 0)
         round_weight("w1", 1)
-        gather_words(0, 0, 512)
-        gather_words(0, 512, 1024)
+        gather_words(0, 0, HALF)
+        gather_words(0, HALF, S)
         quantize_weight("w1", 1)
-        gather_words(1, 0, 256)
-        gather_words(1, 256, 512)
-        gather_words(1, 512, 1024)
-        weave_ld(0, 256, "w1_0_raw")
-        hold("h_bf", 0, HALF, [P, HALF * PACK], BF16, pool=reused, offset=AT_H)
-        hold("h_bf", HALF, 768, [P, 256 * PACK], BF16)
-        hold("h_bf", 768, S, [P, 256 * PACK], BF16)
+        gather_words(1, 0, QUARTER)
+        gather_words(1, QUARTER, HALF)
+        gather_words(1, HALF, S)
+        ld_woven = hold("ld_woven", 0, H_ON_GPSIMD, [P, H_ON_GPSIMD * PACK], F32, tag="w1_0_raw")
+        nc.scalar.copy(as_woven(ld_woven[:]), as_planes(ld_picked[:, :, 0:H_ON_GPSIMD]))
+
+        hold("h_bf", 0, HALF, [P, HALF * PACK], BF16, pool=reused, offset=0)
+        hold("h_bf", HALF, LAST, [P, QUARTER * PACK], BF16)
+        hold("h_bf", LAST, S, [P, QUARTER * PACK], BF16)
         for at in range(0, HALF, P):
-            inner(at)
-        dealt["w2", 0] = keep.tile([P, PACK * 512], BF16, name="w2_bf", tag="w2_bf", align_bytes=64)
+            form_h(at)
+        dealt["w2", 0] = keep.tile([P, PACK * COLUMNS], BF16, name="w2_bf", tag="w2_bf", align_bytes=64)
         for u in range(2):
             nc.scalar.copy(
-                dealt["w2", 0][:].rearrange("p (h u m j) -> p h m j u", h=2, u=2, j=PACK)[:, :, 64 * u : 64 * u + 64],
+                dealt["w2", 0][:].rearrange("p (h u m j) -> p h m j u", h=2, u=2, j=PACK)[
+                    :, :, u * half // PACK : (u + 1) * half // PACK
+                ],
                 w2_halves[u][:].rearrange("p j (m h u) -> p h m j u", h=2, u=2),
             )
-        hold("y", PLAIN, S, [P, PACK, S - PLAIN], F32)
+        hold("y", HEAD, S, [P, PACK, S - HEAD], F32)
         for at in range(HALF, S, P):
-            inner(at)
+            form_h(at)
+
         quantize_weight("w2", 0)
-        quant_h(0, HALF, tag="w2_bf")
-        second_product(0, HALF, [5, 6, 7, 3])
-        scale_by_adapter(ld_t, "y", "h", PLAIN, S)
-        quant_h(HALF, 768, pool=reused, offset=AT_H)
+        quantize_h(0, HALF, tag="w2_bf")
+        rr_plane = [None] * PACK
+        for ts, bank in rr_banks(0, HALF, RR_FIRST_HALF):
+            rr_plane[ts.start] = hold("rr_plane%d_" % ts.start, 0, HALF, [P, 1, HALF], F32)
+            nc.scalar.copy(rr_plane[ts.start][:], bank[:])
+        scale_by_adapter(ld_t, "y", "h", HEAD, S)
+        quantize_h(HALF, LAST, pool=reused, offset=0)
         round_weight("w3", 0)
-        round_late_h()
-        quant_h(768, S)
+        h_bf, a, b = find("h_bf", HEAD, S)
+        nc.scalar.copy(as_woven(h_bf[:, a * PACK : b * PACK]), as_planes(find("h", HEAD, S)[0][:]))
+        quantize_h(LAST, S)
         round_weight("w3", 1)
         quantize_weight("w3", 0)
-        second_product(512, 768, [4, 0])
+        banks = rr_banks(HALF, LAST, RR_THIRD_QUARTER)
+        rr_third = hold("rr", HALF, LAST, [P, PACK, QUARTER], F32)
+        for ts, bank in banks:
+            nc.scalar.copy(rr_third[:, ts, :], bank[:])
+
+        term_plane = []
         for t in range(PACK):
-            outer_t(t, 0, HALF)
-        turn_term(0, 6)
-        hold("rr", 768, S, [P, PACK, 256], F32)
-        last_product(0, 4)
-        quantize_weight("w3", 1, tag="rr_plane3_0")
-        outer(512, 768, order=(0, 1, 3, 2))
-        total_shared(512, 768)
-        hold("result", 0, HALF, [P, PACK, HALF], F32, tag="rr512")
-        total_t(3, 0, HALF, 1)
-        frozen_turned(0, 2)
-        last_product(1, 0)
-        total_t(1, 0, HALF, 5)
-        total_t(2, 0, HALF, 6)
-        sum_on_tensor(0, 2)
-        for lo in (512, 0, 256):
-            round_out(nc.scalar.copy, lo, lo + 256)
-        planes_out(512, 768)
-        store_words(512, 768)
-        outer(768, 1024, tag="plane1_0")
-        total(768, 1024)
-        round_out(nc.scalar.copy, 768, 896)
-        planes_out(0, 256)
-        planes_out(256, 512)
-        store_words(0, 512)
-        round_out(nc.vector.tensor_copy, 896, 1024, tag="o_bf256")
-        planes_out(768, 896)
-        planes_out(896, 1024)
-        store_words(768, 1024)
+            place = {}
+            if t == PACK - 1:
+                quantize_weight("w3", 1)
+                place = {"tag": "w3_1_bf"}
+            term_plane.append(hold("term_plane%d_" % t, 0, HALF, [P, HALF], F32, **place))
+            nc.vector.tensor_tensor(
+                term_plane[t][:], lb_t[t][:].indirect(entries(ad_t, 0, HALF)), rr_plane[t][:, 0, :], MULT
+            )
+        bank = take_bank(TURNED_TERM, [P, BANK])
+        for at in range(0, HALF, P):
+            nc.tensor.transpose(bank[:, at : at + P], term_plane[0][:, at : at + P], identity[:])
+        term_turned = hold("term_turned", 0, HALF, [P, HALF], F32, tag="w3_1_raw")
+        nc.scalar.copy(term_turned[:], bank[:])
+        hold("rr", LAST, S, [P, PACK, QUARTER], F32)
+        rr_last_quarter(0)
+        scale_by_adapter(lb_t, "rr", "term", HALF, LAST, order=(0, 1, 3, 2))
+
+        term = find("term", HALF, LAST)[0]
+        result = hold("result", HALF, LAST, [P, PACK, QUARTER], F32)
+        (ts, lower), (ts, upper) = product("w3", tokens(HALF, LAST), QUARTER, EE_THIRD_QUARTER)
+        ee = hold("ee", HALF, LAST, [P, QUARTER], F32)
+        nc.scalar.copy(ee[:], upper[:, 1, :])
+        nc.gpsimd.tensor_tensor(result[:, 3, :], term[:, 3, :], ee[:], ADD)
+        nc.vector.tensor_tensor(result[:, 0:2, :], term[:, 0:2, :], lower[:], ADD)
+        nc.vector.tensor_tensor(result[:, 2, :], term[:, 2, :], upper[:, 0, :], ADD)
+        nc.sync.dma_start(out_rows[:, :, HALF:LAST], result[:])
+        result = hold("result", 0, HALF, [P, PACK, HALF], F32, tag="rr%d" % HALF)
+        total_plane(3)
+        bank = take_bank(EE_FIRST_HALF[0], [P, BANK])
+        for g in range(PASSES):
+            w_codes, w_scales = weight["w3", g]
+            for at in range(0, HALF, P):
+                x_codes, x_scale = tokens(at, at + P)[g]
+                nc.tensor.matmul_mx(
+                    out=bank[:, at : at + P],
+                    lhsT=x_codes.bitcast(FP8X4),
+                    lhsT_scale=x_scale,
+                    rhs=w_codes[:, 0:P].bitcast(FP8X4),
+                    rhs_scale=w_scales[:, 0:P],
+                    start=(g == 0 and at == 0),
+                    stop=(g == PASSES - 1 and at == HALF - P),
+                )
+        ee_turned = hold("ee_turned", 0, HALF, [P, HALF], F32)
+        nc.scalar.copy(ee_turned[:], bank[:])
+        rr_last_quarter(1)
+        total_plane(1)
+        total_plane(2)
+        bank = take_bank(EE_FIRST_HALF[0], [P, BANK])
+        for n, turned in enumerate((term_turned, ee_turned)):
+            for at in range(0, HALF, P):
+                nc.tensor.matmul(
+                    bank[:, at : at + P],
+                    turned[:, at : at + P],
+                    identity[:],
+                    start=(n == 0 and at == 0),
+                    stop=(n == 1 and at == HALF - P),
+                    is_transpose=True,
+                )
+        nc.scalar.copy(result[:, 0, :], bank[:])
+        nc.sync.dma_start(out_rows[:, 0, 0:HALF], result[:, 0, :])
+
+        for lo in (HALF, 0, QUARTER):
+            round_out(nc.scalar.copy, lo, lo + QUARTER)
+        quantize_out(HALF, LAST)
+        store_words(HALF, LAST)
+        scale_by_adapter(lb_t, "rr", "term", LAST, S, tag="term_plane1_0")
+        term = find("term", LAST, S)[0]
+        result = hold("result", LAST, S, [P, PACK, QUARTER], F32)
+        for ts, bank in product("w3", tokens(LAST, S), QUARTER, EE_LAST_QUARTER):
+            nc.vector.tensor_tensor(result[:, ts, :], term[:, ts, :], bank[:], ADD)
+            nc.sync.dma_start(out_rows[:, ts, LAST:S], result[:, ts, :])
+        round_out(nc.scalar.copy, LAST, SPLIT)
+        quantize_out(0, QUARTER)
+        quantize_out(QUARTER, HALF)
+        store_words(0, HALF)
+        round_out(nc.vector.tensor_copy, SPLIT, S, tag="o_bf%d" % QUARTER)
+        quantize_out(LAST, SPLIT)
+        quantize_out(SPLIT, S)
+        store_words(LAST, S)
         for q in range(4):
             queue = nc.sync if q % 2 == 0 else nc.scalar
             queue.dma_start(

@@ -1,7 +1,6 @@
 from contextlib import ExitStack
 
 import concourse.mybir as mybir
-from concourse.masks import make_identity
 
 K, T, S, H, N, R = 1024, 2048, 1024, 512, 512, 512
 FLOPS = 2 * S * (K * H + K * N + H * N)
@@ -15,6 +14,7 @@ U8 = mybir.dt.uint8
 FP8X4 = mybir.dt.float8_e4m3fn_x4
 MULT = mybir.AluOpType.mult
 ADD = mybir.AluOpType.add
+COPY = mybir.ActivationFunctionType.Copy
 
 P = 128
 PACK = 4
@@ -25,22 +25,8 @@ LIST_ROWS = 16
 BANK = 512
 HALF = S // 2
 QUARTER = S // 4
-LAST = S - QUARTER
 SPARE = 32
-HEAD = 896
-LD_WINDOW = HEAD + SPARE
-LB_WINDOW = HALF + SPARE
-H_ON_GPSIMD = 256
-SPLIT = LAST + P
-
-Y_BANKS = (0, 1, 2, 3, 0, 1, 2, 4)
-RR_FIRST_HALF = (5, 6, 7, 3)
-RR_THIRD_QUARTER = (4, 0)
-RR_LAST_QUARTER = (4, 0)
-EE_FIRST_HALF = {3: 1, 0: 2, 1: 5, 2: 6}
-EE_THIRD_QUARTER = (7, 3)
-EE_LAST_QUARTER = (4, 0)
-TURNED_TERM = 6
+WINDOW = R + SPARE
 
 
 def tile_picked_yvera_none_po_kernel(
@@ -49,7 +35,6 @@ def tile_picked_yvera_none_po_kernel(
     nc = tc.nc
     with ExitStack() as ctx:
         keep = ctx.enter_context(tc.tile_pool(name="keep", bufs=1))
-        reused = ctx.enter_context(tc.tile_pool(name="reused", bufs=1))
         psum = ctx.enter_context(tc.psum_pool(name="psum", bufs=1))
 
         offs_t = keep.tile([P, S // LIST_ROWS], U16, name="offs_t")
@@ -58,111 +43,103 @@ def tile_picked_yvera_none_po_kernel(
         def entries(list_tile, lo, hi):
             return list_tile[:, lo // LIST_ROWS : hi // LIST_ROWS]
 
-        held = {}
-
-        def hold(kind, lo, hi, shape, dtype, pool=keep, **place):
-            place.setdefault("tag", "%s%d" % (kind, lo))
-            tile = pool.tile(shape, dtype, name="%s%d" % (kind, lo), align_bytes=64, **place)
-            held.setdefault(kind, []).append((lo, hi, tile))
-            return tile
-
-        def find(kind, lo, hi):
-            (found,) = [(a, tile) for a, b, tile in held[kind] if a <= lo and hi <= b]
-            return found[1], lo - found[0], hi - found[0]
+        def tile(name, shape, dtype, **place):
+            return keep.tile(shape, dtype, name=name, align_bytes=64, **place)
 
         def load_words(g):
-            words = keep.tile([P, T], I32, name="x_in%d" % g, align_bytes=64)
+            words = tile("x_in%d" % g, [P, T], I32)
             nc.sync.dma_start(words[:], x_words[g].rearrange("p c r -> p (c r)").bitcast(I32))
             return words
 
         def load_weight(w, g, name):
-            rows = keep.tile([P, PACK, COLUMNS], F32, name=name + "_raw", tag=name + "_raw", align_bytes=64)
+            rows = tile("%s_%d_raw" % (name, g), [P, PACK, COLUMNS], F32)
             nc.sync.dma_start(rows[:], w[g * K_PASS : (g + 1) * K_PASS, :].rearrange("(p j) c -> p j c", j=PACK))
-            return rows
+            raw[name, g] = rows
 
-        def load_plane(table, name, window, t):
-            plane = keep.tile([P, window], F32, name="%s%d" % (name, t))
-            nc.gpsimd.memset(plane[:, R:window], 0.0)
+        def load_plane(table, name, t):
+            plane = tile("%s%d" % (name, t), [P, WINDOW], F32)
+            nc.gpsimd.memset(plane[:, R:WINDOW], 0.0)
             nc.sync.dma_start(plane[:, 0:R], table.rearrange("(p t) r -> t p r", t=PACK)[t])
-            return plane
+            planes[name, t] = plane
 
         raw = {}
         dealt = {}
         weight = {}
+        planes = {}
 
-        def round_weight(name, g):
-            label = "%s_%d_bf" % (name, g)
-            dealt[name, g] = keep.tile([P, PACK * COLUMNS], BF16, name=label, tag=label, align_bytes=64)
-            nc.scalar.copy(
+        def round_weight(copy, name, g):
+            dealt[name, g] = tile("%s_%d_bf" % (name, g), [P, PACK * COLUMNS], BF16)
+            copy(
                 dealt[name, g][:].rearrange("p (h u m j) -> p h m j u", h=2, u=2, j=PACK),
                 raw[name, g][:].rearrange("p j (m h u) -> p h m j u", h=2, u=2),
             )
 
         def quantize_weight(name, g):
-            codes = keep.tile([P, COLUMNS], U32, name="%s_%d_codes" % (name, g), align_bytes=64)
-            scales = keep.tile([P, COLUMNS], U8, name="%s_%d_scales" % (name, g), align_bytes=64)
+            codes = tile("%s_%d_codes" % (name, g), [P, COLUMNS], U32)
+            scales = tile("%s_%d_scales" % (name, g), [P, COLUMNS], U8)
             nc.vector.quantize_mx(out=codes[:].bitcast(FP8X4), scales=scales[:], in_=dealt[name, g][:])
             weight[name, g] = (codes, scales)
 
-        xs_in = keep.tile([P, T], U8, name="xs_in")
+        xs_in = tile("xs_in", [P, T], U8)
         nc.vector.memset(xs_in[:].bitcast(I32), 0)
-        ld_t = [load_plane(ld, "ld", LD_WINDOW, 0)]
+        load_plane(ld, "ld", 0)
         nc.sync.dma_start(ad_t[:], ad)
-        ld_t += [load_plane(ld, "ld", LD_WINDOW, t) for t in range(1, PACK)]
-        raw["w1", 0] = load_weight(w1, 0, "w1_0")
-        nc.sync.dma_start(offs_t[:], offs)
-        raw["w1", 1] = load_weight(w1, 1, "w1_1")
+        load_plane(ld, "ld", 1)
         for q in range(4):
-            nc.scalar.dma_start(
+            nc.sync.dma_start(
                 xs_in[32 * q : 32 * q + 4 * PASSES, :].bitcast(I32),
                 x_scales[:, 4 * q : 4 * q + 4, :].bitcast(I32),
             )
+        nc.sync.dma_start(offs_t[:], offs)
+        load_plane(ld, "ld", 2)
+        load_weight(w1, 0, "w1")
+        load_plane(ld, "ld", 3)
         x_in = [load_words(0)]
-        w2_rows = w2.rearrange("(p j) c -> p j c", j=PACK)
-        half = COLUMNS // 2
-        w2_halves = [keep.tile([P, PACK, half], F32, name="w2_half%d" % u, align_bytes=64) for u in range(2)]
-        nc.sync.dma_start(w2_halves[0][:], w2_rows[:, :, 0:half])
+        load_plane(lb, "lb", 0)
+        load_weight(w1, 1, "w1")
+        load_plane(lb, "lb", 1)
         x_in.append(load_words(1))
-        nc.sync.dma_start(w2_halves[1][:], w2_rows[:, :, half:COLUMNS])
-        raw["w3", 0] = load_weight(w3, 0, "w3_0")
-        raw["w3", 1] = load_weight(w3, 1, "w3_1")
-        lb_t = [load_plane(lb, "lb", LB_WINDOW, t) for t in range(PACK)]
+        load_weight(w2, 0, "w2")
+        load_plane(lb, "lb", 2)
+        load_plane(lb, "lb", 3)
+        load_weight(w3, 0, "w3")
+        load_weight(w3, 1, "w3")
 
-        identity = keep.tile([P, P], F32, name="identity")
-        make_identity(nc, identity[:])
-        x_sc = keep.tile([P, S], U8, name="x_sc", align_bytes=64)
+        picked = {name: tile(name + "_picked", [P, PACK, S], F32) for name in ("ld", "lb")}
+
+        def look_up(name, t, lo, hi):
+            nc.scalar.activation(picked[name][:, t, lo:hi], planes[name, t][:].indirect(entries(ad_t, lo, hi)), COPY)
+
+        x_sc = tile("x_sc", [P, S], U8)
+        x_codes = {}
 
         def gather_words(g, lo, hi):
-            codes = hold("x%d_codes" % g, lo, hi, [P, hi - lo], U32)
+            codes = tile("x%d_codes%d" % (g, lo), [P, hi - lo], U32)
             nc.vector.tensor_copy(codes[:], x_in[g][:].bitcast(U32).indirect(entries(offs_t, lo, hi)))
+            for at in range(lo, hi, P):
+                x_codes[g, at] = (codes, lo)
+
+        def tokens(g, lo, hi):
+            codes, first = x_codes[g, lo]
+            return codes[:, lo - first : hi - first], x_sc[4 * g : P, lo:hi]
 
         def take_bank(number, shape):
             return psum.tile(shape, F32, name="bank%d" % number, tag="bank%d" % number, offset=number * BANK * 4)
 
-        def product(name, moving, n, numbers, first=0):
-            per_bank = BANK // n
-            banks = []
-            for b, number in enumerate(numbers, first):
-                bank = take_bank(number, [P, per_bank, n])
-                for g, (m_codes, m_scales) in enumerate(moving):
-                    for u in range(per_bank):
-                        t = b * per_bank + u
-                        w_codes, w_scales = weight[name, g]
-                        nc.tensor.matmul_mx(
-                            out=bank[:, u, :],
-                            lhsT=w_codes[:, t * P : (t + 1) * P].bitcast(FP8X4),
-                            lhsT_scale=w_scales[:, t * P : (t + 1) * P],
-                            rhs=m_codes.bitcast(FP8X4),
-                            rhs_scale=m_scales,
-                            start=(g == 0 and u == 0),
-                            stop=(g == len(moving) - 1 and u == per_bank - 1),
-                        )
-                banks.append((slice(b * per_bank, (b + 1) * per_bank), bank))
-            return banks
-
-        def tokens(lo, hi):
-            picked = [find("x%d_codes" % g, lo, hi) for g in range(PASSES)]
-            return [(codes[:, a:b], x_sc[4 * g : P, lo:hi]) for g, (codes, a, b) in enumerate(picked)]
+        def product(name, moving, bank, first, count):
+            for g, (m_codes, m_scales) in enumerate(moving):
+                w_codes, w_scales = weight[name, g]
+                for u in range(count):
+                    t = first + u
+                    nc.tensor.matmul_mx(
+                        out=bank[:, u, :],
+                        lhsT=w_codes[:, t * P : (t + 1) * P].bitcast(FP8X4),
+                        lhsT_scale=w_scales[:, t * P : (t + 1) * P],
+                        rhs=m_codes.bitcast(FP8X4),
+                        rhs_scale=m_scales,
+                        start=(g == 0 and u == 0),
+                        stop=(g == len(moving) - 1 and u == count - 1),
+                    )
 
         def as_woven(ap):
             return ap.rearrange("p (a i t) -> p a t i", i=4, t=PACK)
@@ -170,224 +147,115 @@ def tile_picked_yvera_none_po_kernel(
         def as_planes(ap):
             return ap.rearrange("p t (a i) -> p a t i", i=4)
 
-        out_codes = keep.tile([P, S], U32, name="out_codes", align_bytes=64)
-        out_scales = keep.tile([P, S], U8, name="out_scales", align_bytes=64)
+        out_codes = tile("out_codes", [P, S], U32)
+        out_scales = tile("out_scales", [P, S], U8)
         out_rows = out_0.rearrange("(p t) s -> p t s", t=PACK)
         out_words = out_1[0].rearrange("p c r -> p (c r)").bitcast(I32)
 
+        for t in range(PACK):
+            for lo in (0, HALF):
+                look_up("ld", t, lo, lo + HALF)
+        nc.vector.tensor_copy(x_sc[:], xs_in[:].indirect(offs_t[:]))
+        round_weight(nc.vector.tensor_copy, "w1", 0)
+        quantize_weight("w1", 0)
+        gather_words(0, 0, HALF)
+        gather_words(0, HALF, S)
+        round_weight(nc.vector.tensor_copy, "w1", 1)
+        quantize_weight("w1", 1)
+        for t in range(2):
+            for lo in (0, HALF):
+                look_up("lb", t, lo, lo + HALF)
+        gather_words(1, 0, QUARTER)
+        gather_words(1, QUARTER, HALF)
+        gather_words(1, HALF, S)
+
+        h_bf = [tile("h_bf%d" % u, [P, HALF * PACK], BF16) for u in range(2)]
+        h_codes = [tile("h_codes%d" % u, [P, HALF], U32) for u in range(2)]
+        h_scales = [tile("h_scales%d" % u, [P, HALF], U8) for u in range(2)]
+
         def form_h(at):
-            h_bf, c, d = find("h_bf", at, at + P)
-            ((ts, bank),) = product("w1", tokens(at, at + P), P, [Y_BANKS[at // P]])
-            if at < H_ON_GPSIMD:
-                y_woven = hold("y_woven", at, at + P, [P, P * PACK], F32)
-                nc.scalar.copy(y_woven[:].rearrange("p (n t) -> p n t", t=PACK), bank[:].rearrange("p t n -> p n t"))
-                nc.gpsimd.tensor_tensor(
-                    h_bf[:, c * PACK : d * PACK], y_woven[:], ld_woven[:, at * PACK : (at + P) * PACK], MULT
-                )
-                return
-            direct = max(0, min(P, HEAD - at))
-            if direct > 0:
-                nc.vector.tensor_tensor(
-                    as_woven(h_bf[:, c * PACK : (c + direct) * PACK]),
-                    as_planes(bank[:, :, 0:direct]),
-                    as_planes(ld_picked[:, :, at : at + direct]),
-                    MULT,
-                )
-            if direct < P:
-                y, a, b = find("y", at + direct, at + P)
-                nc.scalar.copy(y[:, :, a:b], bank[:, :, direct:P])
+            bank = take_bank(at // P, [P, PACK, P])
+            product("w1", [tokens(g, at, at + P) for g in range(PASSES)], bank, 0, PACK)
+            c = at % HALF
+            nc.vector.tensor_tensor(
+                as_woven(h_bf[at // HALF][:, c * PACK : (c + P) * PACK]),
+                as_planes(bank[:]),
+                as_planes(picked["ld"][:, :, at : at + P]),
+                MULT,
+            )
 
-        def quantize_h(lo, hi, **place):
-            h_codes = hold("h_codes", lo, hi, [P, hi - lo], U32, **place)
-            h_scales = hold("h_scales", lo, hi, [P, hi - lo], U8)
-            nc.vector.quantize_mx(out=h_codes[:].bitcast(FP8X4), scales=h_scales[:], in_=find("h_bf", lo, hi)[0][:])
+        def quantize_h(u):
+            nc.vector.quantize_mx(out=h_codes[u][:].bitcast(FP8X4), scales=h_scales[u][:], in_=h_bf[u][:])
 
-        def rr_banks(lo, hi, numbers, first=0):
-            moving = (find("h_codes", lo, hi)[0][:], find("h_scales", lo, hi)[0][:])
-            return product("w2", [moving], hi - lo, numbers, first)
+        term = tile("term", [P, PACK, S], F32)
 
-        def rr_last_quarter(pair):
-            ((ts, bank),) = rr_banks(LAST, S, [RR_LAST_QUARTER[pair]], pair)
-            nc.scalar.copy(find("rr", LAST, S)[0][:, ts, :], bank[:])
+        def form_term(u, t):
+            bank = take_bank(PACK * u + t, [P, 1, HALF])
+            product("w2", [(h_codes[u][:], h_scales[u][:])], bank, t, 1)
+            lo = u * HALF
+            nc.vector.tensor_tensor(term[:, t, lo : lo + HALF], bank[:, 0, :], picked["lb"][:, t, lo : lo + HALF], MULT)
 
-        def scale_by_adapter(table, src, dst, lo, hi, order=range(PACK), **place):
-            planes = find(src, lo, hi)[0]
-            scaled = hold(dst, lo, hi, [P, PACK, hi - lo], F32, **place)
-            for t in order:
-                nc.vector.tensor_tensor(
-                    scaled[:, t, :], table[t][:].indirect(entries(ad_t, lo, hi)), planes[:, t, :], MULT
-                )
+        round_weight(nc.scalar.copy, "w2", 0)
+        for at in range(0, HALF, P):
+            form_h(at)
+        quantize_weight("w2", 0)
+        quantize_h(0)
+        for at in range(HALF, S, P):
+            form_h(at)
+        quantize_h(1)
+        look_up("lb", 2, 0, HALF)
+        look_up("lb", 3, 0, HALF)
+        round_weight(nc.scalar.copy, "w3", 0)
+        round_weight(nc.scalar.copy, "w3", 1)
+        look_up("lb", 2, HALF, S)
+        look_up("lb", 3, HALF, S)
+        for t in range(PACK):
+            form_term(0, t)
+        quantize_weight("w3", 0)
+        quantize_weight("w3", 1)
+        for t in range(PACK):
+            form_term(1, t)
 
-        def total_plane(t):
-            result = find("result", 0, HALF)[0]
-            bank = take_bank(EE_FIRST_HALF[t], [P, BANK])
-            for g in range(PASSES):
-                for at in range(0, HALF, QUARTER):
-                    m_codes, m_scales = tokens(at, at + QUARTER)[g]
-                    w_codes, w_scales = weight["w3", g]
-                    nc.tensor.matmul_mx(
-                        out=bank[:, at : at + QUARTER],
-                        lhsT=w_codes[:, t * P : (t + 1) * P].bitcast(FP8X4),
-                        lhsT_scale=w_scales[:, t * P : (t + 1) * P],
-                        rhs=m_codes.bitcast(FP8X4),
-                        rhs_scale=m_scales,
-                        start=(g == 0 and at == 0),
-                        stop=(g == PASSES - 1 and at == HALF - QUARTER),
-                    )
-            if t == PACK - 1:
-                ee = hold("ee", 0, HALF, [P, HALF], F32)
-                nc.scalar.copy(ee[:], bank[:])
-                nc.gpsimd.tensor_tensor(result[:, t, :], term_plane[t][:], ee[:], ADD)
-            else:
-                nc.vector.tensor_tensor(result[:, t, :], term_plane[t][:], bank[:], ADD)
-            nc.sync.dma_start(out_rows[:, t, 0:HALF], result[:, t, :])
+        result = {}
 
-        def round_out(copy, lo, hi, **place):
-            result, a, b = find("result", lo, hi)
-            woven = hold("o_bf", lo, hi, [P, (hi - lo) * PACK], BF16, **place)
-            copy(as_woven(woven[:]), as_planes(result[:, :, a:b]))
+        def total(lo):
+            result[lo] = tile("result%d" % lo, [P, PACK, QUARTER], F32)
+            for pair in range(2):
+                bank = take_bank(2 * (lo // QUARTER) + pair, [P, 2, QUARTER])
+                moving = []
+                for g in range(PASSES):
+                    moving.append(tokens(g, lo, lo + QUARTER))
+                product("w3", moving, bank, 2 * pair, 2)
+                ts = slice(2 * pair, 2 * pair + 2)
+                nc.vector.tensor_tensor(result[lo][:, ts, :], bank[:], term[:, ts, lo : lo + QUARTER], ADD)
+            nc.sync.dma_start(out_rows[:, :, lo : lo + QUARTER], result[lo][:])
+
+        woven = {}
+
+        def round_out(copy, lo, hi):
+            first = lo - lo % QUARTER
+            woven[lo] = tile("o_bf%d" % lo, [P, (hi - lo) * PACK], BF16)
+            copy(as_woven(woven[lo][:]), as_planes(result[first][:, :, lo - first : hi - first]))
 
         def quantize_out(lo, hi):
-            nc.vector.quantize_mx(
-                out=out_codes[:, lo:hi].bitcast(FP8X4), scales=out_scales[:, lo:hi], in_=find("o_bf", lo, hi)[0][:]
-            )
+            nc.vector.quantize_mx(out=out_codes[:, lo:hi].bitcast(FP8X4), scales=out_scales[:, lo:hi], in_=woven[lo][:])
 
         def store_words(lo, hi):
             nc.sync.dma_start(out_words[:, lo:hi], out_codes[:, lo:hi].bitcast(I32))
 
-        ld_picked = hold("ld_picked", 0, HEAD, [P, PACK, HEAD], F32)
-        for t in range(PACK):
-            nc.vector.tensor_copy(ld_picked[:, t, :], ld_t[t][:].indirect(entries(ad_t, 0, HEAD)))
-        nc.vector.tensor_copy(x_sc[:], xs_in[:].indirect(offs_t[:]))
-        round_weight("w1", 0)
-        quantize_weight("w1", 0)
-        round_weight("w1", 1)
-        gather_words(0, 0, HALF)
-        gather_words(0, HALF, S)
-        quantize_weight("w1", 1)
-        gather_words(1, 0, QUARTER)
-        gather_words(1, QUARTER, HALF)
-        gather_words(1, HALF, S)
-        ld_woven = hold("ld_woven", 0, H_ON_GPSIMD, [P, H_ON_GPSIMD * PACK], F32, tag="w1_0_raw")
-        nc.scalar.copy(as_woven(ld_woven[:]), as_planes(ld_picked[:, :, 0:H_ON_GPSIMD]))
-
-        hold("h_bf", 0, HALF, [P, HALF * PACK], BF16, pool=reused, offset=0)
-        hold("h_bf", HALF, LAST, [P, QUARTER * PACK], BF16)
-        hold("h_bf", LAST, S, [P, QUARTER * PACK], BF16)
-        for at in range(0, HALF, P):
-            form_h(at)
-        dealt["w2", 0] = keep.tile([P, PACK * COLUMNS], BF16, name="w2_bf", tag="w2_bf", align_bytes=64)
-        for u in range(2):
-            nc.scalar.copy(
-                dealt["w2", 0][:].rearrange("p (h u m j) -> p h m j u", h=2, u=2, j=PACK)[
-                    :, :, u * half // PACK : (u + 1) * half // PACK
-                ],
-                w2_halves[u][:].rearrange("p j (m h u) -> p h m j u", h=2, u=2),
-            )
-        hold("y", HEAD, S, [P, PACK, S - HEAD], F32)
-        for at in range(HALF, S, P):
-            form_h(at)
-
-        quantize_weight("w2", 0)
-        quantize_h(0, HALF, tag="w2_bf")
-        rr_plane = [None] * PACK
-        for ts, bank in rr_banks(0, HALF, RR_FIRST_HALF):
-            rr_plane[ts.start] = hold("rr_plane%d_" % ts.start, 0, HALF, [P, 1, HALF], F32)
-            nc.scalar.copy(rr_plane[ts.start][:], bank[:])
-        scale_by_adapter(ld_t, "y", "h", HEAD, S)
-        quantize_h(HALF, LAST, pool=reused, offset=0)
-        round_weight("w3", 0)
-        h_bf, a, b = find("h_bf", HEAD, S)
-        nc.scalar.copy(as_woven(h_bf[:, a * PACK : b * PACK]), as_planes(find("h", HEAD, S)[0][:]))
-        quantize_h(LAST, S)
-        round_weight("w3", 1)
-        quantize_weight("w3", 0)
-        banks = rr_banks(HALF, LAST, RR_THIRD_QUARTER)
-        rr_third = hold("rr", HALF, LAST, [P, PACK, QUARTER], F32)
-        for ts, bank in banks:
-            nc.scalar.copy(rr_third[:, ts, :], bank[:])
-
-        term_plane = []
-        for t in range(PACK):
-            place = {}
-            if t == PACK - 1:
-                quantize_weight("w3", 1)
-                place = {"tag": "w3_1_bf"}
-            term_plane.append(hold("term_plane%d_" % t, 0, HALF, [P, HALF], F32, **place))
-            nc.vector.tensor_tensor(
-                term_plane[t][:], lb_t[t][:].indirect(entries(ad_t, 0, HALF)), rr_plane[t][:, 0, :], MULT
-            )
-        bank = take_bank(TURNED_TERM, [P, BANK])
-        for at in range(0, HALF, P):
-            nc.tensor.transpose(bank[:, at : at + P], term_plane[0][:, at : at + P], identity[:])
-        term_turned = hold("term_turned", 0, HALF, [P, HALF], F32, tag="w3_1_raw")
-        nc.scalar.copy(term_turned[:], bank[:])
-        hold("rr", LAST, S, [P, PACK, QUARTER], F32)
-        rr_last_quarter(0)
-        scale_by_adapter(lb_t, "rr", "term", HALF, LAST, order=(0, 1, 3, 2))
-
-        term = find("term", HALF, LAST)[0]
-        result = hold("result", HALF, LAST, [P, PACK, QUARTER], F32)
-        (ts, lower), (ts, upper) = product("w3", tokens(HALF, LAST), QUARTER, EE_THIRD_QUARTER)
-        ee = hold("ee", HALF, LAST, [P, QUARTER], F32)
-        nc.scalar.copy(ee[:], upper[:, 1, :])
-        nc.gpsimd.tensor_tensor(result[:, 3, :], term[:, 3, :], ee[:], ADD)
-        nc.vector.tensor_tensor(result[:, 0:2, :], term[:, 0:2, :], lower[:], ADD)
-        nc.vector.tensor_tensor(result[:, 2, :], term[:, 2, :], upper[:, 0, :], ADD)
-        nc.sync.dma_start(out_rows[:, :, HALF:LAST], result[:])
-        result = hold("result", 0, HALF, [P, PACK, HALF], F32, tag="rr%d" % HALF)
-        total_plane(3)
-        bank = take_bank(EE_FIRST_HALF[0], [P, BANK])
-        for g in range(PASSES):
-            w_codes, w_scales = weight["w3", g]
-            for at in range(0, HALF, P):
-                x_codes, x_scale = tokens(at, at + P)[g]
-                nc.tensor.matmul_mx(
-                    out=bank[:, at : at + P],
-                    lhsT=x_codes.bitcast(FP8X4),
-                    lhsT_scale=x_scale,
-                    rhs=w_codes[:, 0:P].bitcast(FP8X4),
-                    rhs_scale=w_scales[:, 0:P],
-                    start=(g == 0 and at == 0),
-                    stop=(g == PASSES - 1 and at == HALF - P),
-                )
-        ee_turned = hold("ee_turned", 0, HALF, [P, HALF], F32)
-        nc.scalar.copy(ee_turned[:], bank[:])
-        rr_last_quarter(1)
-        total_plane(1)
-        total_plane(2)
-        bank = take_bank(EE_FIRST_HALF[0], [P, BANK])
-        for n, turned in enumerate((term_turned, ee_turned)):
-            for at in range(0, HALF, P):
-                nc.tensor.matmul(
-                    bank[:, at : at + P],
-                    turned[:, at : at + P],
-                    identity[:],
-                    start=(n == 0 and at == 0),
-                    stop=(n == 1 and at == HALF - P),
-                    is_transpose=True,
-                )
-        nc.scalar.copy(result[:, 0, :], bank[:])
-        nc.sync.dma_start(out_rows[:, 0, 0:HALF], result[:, 0, :])
-
-        for lo in (HALF, 0, QUARTER):
-            round_out(nc.scalar.copy, lo, lo + QUARTER)
-        quantize_out(HALF, LAST)
-        store_words(HALF, LAST)
-        scale_by_adapter(lb_t, "rr", "term", LAST, S, tag="term_plane1_0")
-        term = find("term", LAST, S)[0]
-        result = hold("result", LAST, S, [P, PACK, QUARTER], F32)
-        for ts, bank in product("w3", tokens(LAST, S), QUARTER, EE_LAST_QUARTER):
-            nc.vector.tensor_tensor(result[:, ts, :], term[:, ts, :], bank[:], ADD)
-            nc.sync.dma_start(out_rows[:, ts, LAST:S], result[:, ts, :])
-        round_out(nc.scalar.copy, LAST, SPLIT)
-        quantize_out(0, QUARTER)
-        quantize_out(QUARTER, HALF)
-        store_words(0, HALF)
-        round_out(nc.vector.tensor_copy, SPLIT, S, tag="o_bf%d" % QUARTER)
-        quantize_out(LAST, SPLIT)
-        quantize_out(SPLIT, S)
-        store_words(LAST, S)
+        last = S - QUARTER
+        for lo in range(0, S, QUARTER):
+            total(lo)
+            if lo < last:
+                round_out(nc.scalar.copy, lo, lo + QUARTER)
+            if lo > 0:
+                quantize_out(lo - QUARTER, lo)
+        store_words(0, last)
+        round_out(nc.scalar.copy, last, last + P)
+        round_out(nc.vector.tensor_copy, last + P, S)
+        quantize_out(last, last + P)
+        quantize_out(last + P, S)
+        store_words(last, S)
         for q in range(4):
             queue = nc.sync if q % 2 == 0 else nc.scalar
             queue.dma_start(

@@ -27,6 +27,8 @@ HALF = S // 2
 QUARTER = S // 4
 SPARE = 32
 WINDOW = R + SPARE
+H_ON_GPSIMD = 384
+EE_BANKS = (0, 1, 2, 3, 6, 7, 4, 5)
 
 
 def tile_picked_yvera_none_po_kernel(
@@ -52,13 +54,17 @@ def tile_picked_yvera_none_po_kernel(
             return words
 
         def load_weight(w, g, name):
-            rows = tile("%s_%d_raw" % (name, g), [P, PACK, COLUMNS], F32)
+            label = "%s_%d_raw" % (name, g)
+            rows = tile(label, [P, PACK, COLUMNS], F32, tag=label)
             nc.sync.dma_start(rows[:], w[g * K_PASS : (g + 1) * K_PASS, :].rearrange("(p j) c -> p j c", j=PACK))
             raw[name, g] = rows
 
         def load_plane(table, name, t):
             plane = tile("%s%d" % (name, t), [P, WINDOW], F32)
-            nc.gpsimd.memset(plane[:, R:WINDOW], 0.0)
+            if (name, t) == ("lb", PACK - 1):
+                nc.scalar.activation(plane[:, R:WINDOW], planes["ld", 0][:, R:WINDOW], COPY)
+            else:
+                nc.gpsimd.memset(plane[:, R:WINDOW], 0.0)
             nc.sync.dma_start(plane[:, 0:R], table.rearrange("(p t) r -> t p r", t=PACK)[t])
             planes[name, t] = plane
 
@@ -68,14 +74,15 @@ def tile_picked_yvera_none_po_kernel(
         planes = {}
 
         def round_weight(copy, name, g):
-            dealt[name, g] = tile("%s_%d_bf" % (name, g), [P, PACK * COLUMNS], BF16)
+            label = "%s_%d_bf" % (name, g)
+            dealt[name, g] = tile(label, [P, PACK * COLUMNS], BF16, tag=label)
             copy(
                 dealt[name, g][:].rearrange("p (h u m j) -> p h m j u", h=2, u=2, j=PACK),
                 raw[name, g][:].rearrange("p j (m h u) -> p h m j u", h=2, u=2),
             )
 
-        def quantize_weight(name, g):
-            codes = tile("%s_%d_codes" % (name, g), [P, COLUMNS], U32)
+        def quantize_weight(name, g, **place):
+            codes = tile("%s_%d_codes" % (name, g), [P, COLUMNS], U32, **place)
             scales = tile("%s_%d_scales" % (name, g), [P, COLUMNS], U8)
             nc.vector.quantize_mx(out=codes[:].bitcast(FP8X4), scales=scales[:], in_=dealt[name, g][:])
             weight[name, g] = (codes, scales)
@@ -84,31 +91,34 @@ def tile_picked_yvera_none_po_kernel(
         nc.vector.memset(xs_in[:].bitcast(I32), 0)
         load_plane(ld, "ld", 0)
         nc.sync.dma_start(ad_t[:], ad)
-        load_plane(ld, "ld", 1)
+        for t in range(1, PACK):
+            load_plane(ld, "ld", t)
         for q in range(4):
             nc.sync.dma_start(
                 xs_in[32 * q : 32 * q + 4 * PASSES, :].bitcast(I32),
                 x_scales[:, 4 * q : 4 * q + 4, :].bitcast(I32),
             )
         nc.sync.dma_start(offs_t[:], offs)
-        load_plane(ld, "ld", 2)
         load_weight(w1, 0, "w1")
-        load_plane(ld, "ld", 3)
-        x_in = [load_words(0)]
         load_plane(lb, "lb", 0)
-        load_weight(w1, 1, "w1")
         load_plane(lb, "lb", 1)
+        x_in = [load_words(0)]
+        load_plane(lb, "lb", 2)
+        load_weight(w1, 1, "w1")
+        load_plane(lb, "lb", 3)
         x_in.append(load_words(1))
         load_weight(w2, 0, "w2")
-        load_plane(lb, "lb", 2)
-        load_plane(lb, "lb", 3)
         load_weight(w3, 0, "w3")
         load_weight(w3, 1, "w3")
 
         picked = {name: tile(name + "_picked", [P, PACK, S], F32) for name in ("ld", "lb")}
 
         def look_up(name, t, lo, hi):
-            nc.scalar.activation(picked[name][:, t, lo:hi], planes[name, t][:].indirect(entries(ad_t, lo, hi)), COPY)
+            columns = planes[name, t][:].indirect(entries(ad_t, lo, hi))
+            if name == "ld" and t % 2 == 1:
+                nc.vector.tensor_copy(picked[name][:, t, lo:hi], columns)
+            else:
+                nc.scalar.activation(picked[name][:, t, lo:hi], columns, COPY)
 
         x_sc = tile("x_sc", [P, S], U8)
         x_codes = {}
@@ -155,6 +165,16 @@ def tile_picked_yvera_none_po_kernel(
         for t in range(PACK):
             for lo in (0, HALF):
                 look_up("ld", t, lo, lo + HALF)
+        ld_woven = tile("ld_woven", [P, H_ON_GPSIMD * PACK], F32)
+        for at in range(0, H_ON_GPSIMD, P):
+            nc.gpsimd.tensor_scalar(
+                ld_woven[:, at * PACK : (at + P) * PACK].rearrange("p (n t) -> p n t", t=PACK),
+                picked["ld"][:, :, at : at + P].rearrange("p t n -> p n t"),
+                1.0,
+                0.0,
+                MULT,
+                ADD,
+            )
         nc.vector.tensor_copy(x_sc[:], xs_in[:].indirect(offs_t[:]))
         round_weight(nc.vector.tensor_copy, "w1", 0)
         quantize_weight("w1", 0)
@@ -162,7 +182,7 @@ def tile_picked_yvera_none_po_kernel(
         gather_words(0, HALF, S)
         round_weight(nc.vector.tensor_copy, "w1", 1)
         quantize_weight("w1", 1)
-        for t in range(2):
+        for t in range(PACK):
             for lo in (0, HALF):
                 look_up("lb", t, lo, lo + HALF)
         gather_words(1, 0, QUARTER)
@@ -177,6 +197,13 @@ def tile_picked_yvera_none_po_kernel(
             bank = take_bank(at // P, [P, PACK, P])
             product("w1", [tokens(g, at, at + P) for g in range(PASSES)], bank, 0, PACK)
             c = at % HALF
+            if at < H_ON_GPSIMD:
+                y_woven = tile("y_woven%d" % at, [P, P * PACK], F32, tag="y_woven%d" % at)
+                nc.scalar.copy(y_woven[:].rearrange("p (n t) -> p n t", t=PACK), bank[:].rearrange("p t n -> p n t"))
+                nc.gpsimd.tensor_tensor(
+                    h_bf[0][:, c * PACK : (c + P) * PACK], y_woven[:], ld_woven[:, c * PACK : (c + P) * PACK], MULT
+                )
+                return
             nc.vector.tensor_tensor(
                 as_woven(h_bf[at // HALF][:, c * PACK : (c + P) * PACK]),
                 as_planes(bank[:]),
@@ -187,33 +214,37 @@ def tile_picked_yvera_none_po_kernel(
         def quantize_h(u):
             nc.vector.quantize_mx(out=h_codes[u][:].bitcast(FP8X4), scales=h_scales[u][:], in_=h_bf[u][:])
 
-        term = tile("term", [P, PACK, S], F32)
+        term = {}
 
         def form_term(u, t):
             bank = take_bank(PACK * u + t, [P, 1, HALF])
             product("w2", [(h_codes[u][:], h_scales[u][:])], bank, t, 1)
             lo = u * HALF
-            nc.vector.tensor_tensor(term[:, t, lo : lo + HALF], bank[:, 0, :], picked["lb"][:, t, lo : lo + HALF], MULT)
+            scaled = term[u][:, t, :]
+            if u == 1 and t >= 2:
+                nc.scalar.copy(rr[:, t % 2, :], bank[:, 0, :])
+                nc.gpsimd.tensor_tensor(scaled, rr[:, t % 2, :], picked["lb"][:, t, lo : lo + HALF], MULT)
+            else:
+                nc.vector.tensor_tensor(scaled, bank[:, 0, :], picked["lb"][:, t, lo : lo + HALF], MULT)
 
+        for at in range(0, H_ON_GPSIMD, P):
+            form_h(at)
         round_weight(nc.scalar.copy, "w2", 0)
-        for at in range(0, HALF, P):
+        for at in range(H_ON_GPSIMD, S, P):
             form_h(at)
-        quantize_weight("w2", 0)
+        quantize_weight("w2", 0, tag="y_woven%d" % (H_ON_GPSIMD - P))
         quantize_h(0)
-        for at in range(HALF, S, P):
-            form_h(at)
         quantize_h(1)
-        look_up("lb", 2, 0, HALF)
-        look_up("lb", 3, 0, HALF)
         round_weight(nc.scalar.copy, "w3", 0)
         round_weight(nc.scalar.copy, "w3", 1)
-        look_up("lb", 2, HALF, S)
-        look_up("lb", 3, HALF, S)
+        quantize_weight("w3", 0)
+        term[0] = tile("term0", [P, PACK, HALF], F32)
         for t in range(PACK):
             form_term(0, t)
-        quantize_weight("w3", 0)
         quantize_weight("w3", 1)
-        for t in range(PACK):
+        rr = tile("rr", [P, 2, HALF], F32, tag="w3_1_raw")
+        term[1] = tile("term1", [P, PACK, HALF], F32, tag="w3_1_bf")
+        for t in (2, 3, 0, 1):
             form_term(1, t)
 
         result = {}
@@ -221,14 +252,20 @@ def tile_picked_yvera_none_po_kernel(
         def total(lo):
             result[lo] = tile("result%d" % lo, [P, PACK, QUARTER], F32)
             for pair in range(2):
-                bank = take_bank(2 * (lo // QUARTER) + pair, [P, 2, QUARTER])
+                bank = take_bank(EE_BANKS[2 * (lo // QUARTER) + pair], [P, 2, QUARTER])
                 moving = []
                 for g in range(PASSES):
                     moving.append(tokens(g, lo, lo + QUARTER))
                 product("w3", moving, bank, 2 * pair, 2)
                 ts = slice(2 * pair, 2 * pair + 2)
-                nc.vector.tensor_tensor(result[lo][:, ts, :], bank[:], term[:, ts, lo : lo + QUARTER], ADD)
-            nc.sync.dma_start(out_rows[:, :, lo : lo + QUARTER], result[lo][:])
+                scaled = term[lo // HALF][:, ts, lo % HALF : lo % HALF + QUARTER]
+                if lo == 0 and pair == 1:
+                    ee = tile("ee%d" % lo, [P, 2, QUARTER], F32)
+                    nc.scalar.copy(ee[:], bank[:])
+                    nc.gpsimd.tensor_tensor(result[lo][:, ts, :], ee[:], scaled, ADD)
+                else:
+                    nc.vector.tensor_tensor(result[lo][:, ts, :], bank[:], scaled, ADD)
+                nc.sync.dma_start(out_rows[:, ts, lo : lo + QUARTER], result[lo][:, ts, :])
 
         woven = {}
 
@@ -246,16 +283,15 @@ def tile_picked_yvera_none_po_kernel(
         last = S - QUARTER
         for lo in range(0, S, QUARTER):
             total(lo)
-            if lo < last:
-                round_out(nc.scalar.copy, lo, lo + QUARTER)
-            if lo > 0:
-                quantize_out(lo - QUARTER, lo)
-        store_words(0, last)
-        round_out(nc.scalar.copy, last, last + P)
-        round_out(nc.vector.tensor_copy, last + P, S)
-        quantize_out(last, last + P)
-        quantize_out(last + P, S)
-        store_words(last, S)
+        for lo in (QUARTER, 0, HALF):
+            round_out(nc.scalar.copy, lo, lo + QUARTER)
+        round_out(nc.vector.tensor_copy, last, S)
+        quantize_out(QUARTER, HALF)
+        quantize_out(0, QUARTER)
+        store_words(0, HALF)
+        quantize_out(last, S)
+        quantize_out(HALF, last)
+        store_words(HALF, S)
         for q in range(4):
             queue = nc.sync if q % 2 == 0 else nc.scalar
             queue.dma_start(

@@ -111,14 +111,18 @@ def tile_picked_yvera_none_po_kernel(
         load_weight(w3, 0, "w3")
         load_weight(w3, 1, "w3")
 
-        picked = {name: tile(name + "_picked", [P, PACK, S], F32) for name in ("ld", "lb")}
+        picked = {}
+        for name in ("ld", "lb"):
+            for u in range(2):
+                label = "%s_picked%d" % (name, u)
+                picked[name, u] = tile(label, [P, PACK, HALF], F32, tag=label)
 
         def look_up(name, t, lo, hi):
             columns = planes[name, t][:].indirect(entries(ad_t, lo, hi))
             if name == "ld" and t % 2 == 1:
-                nc.vector.tensor_copy(picked[name][:, t, lo:hi], columns)
+                nc.vector.tensor_copy(picked[name, lo // HALF][:, t, :], columns)
             else:
-                nc.scalar.activation(picked[name][:, t, lo:hi], columns, COPY)
+                nc.scalar.activation(picked[name, lo // HALF][:, t, :], columns, COPY)
 
         x_sc = tile("x_sc", [P, S], U8)
         x_codes = {}
@@ -169,7 +173,7 @@ def tile_picked_yvera_none_po_kernel(
         for at in range(0, H_ON_GPSIMD, P):
             nc.gpsimd.tensor_scalar(
                 ld_woven[:, at * PACK : (at + P) * PACK].rearrange("p (n t) -> p n t", t=PACK),
-                picked["ld"][:, :, at : at + P].rearrange("p t n -> p n t"),
+                picked["ld", 0][:, :, at : at + P].rearrange("p t n -> p n t"),
                 1.0,
                 0.0,
                 MULT,
@@ -189,7 +193,7 @@ def tile_picked_yvera_none_po_kernel(
         gather_words(1, QUARTER, HALF)
         gather_words(1, HALF, S)
 
-        h_bf = [tile("h_bf%d" % u, [P, HALF * PACK], BF16) for u in range(2)]
+        h_bf = [tile("h_bf%d" % u, [P, HALF * PACK], BF16, tag="h_bf%d" % u) for u in range(2)]
         h_codes = [tile("h_codes%d" % u, [P, HALF], U32) for u in range(2)]
         h_scales = [tile("h_scales%d" % u, [P, HALF], U8) for u in range(2)]
 
@@ -207,7 +211,7 @@ def tile_picked_yvera_none_po_kernel(
             nc.vector.tensor_tensor(
                 as_woven(h_bf[at // HALF][:, c * PACK : (c + P) * PACK]),
                 as_planes(bank[:]),
-                as_planes(picked["ld"][:, :, at : at + P]),
+                as_planes(picked["ld", at // HALF][:, :, c : c + P]),
                 MULT,
             )
 
@@ -219,13 +223,12 @@ def tile_picked_yvera_none_po_kernel(
         def form_term(u, t):
             bank = take_bank(PACK * u + t, [P, 1, HALF])
             product("w2", [(h_codes[u][:], h_scales[u][:])], bank, t, 1)
-            lo = u * HALF
             scaled = term[u][:, t, :]
             if u == 1 and t >= 2:
                 nc.scalar.copy(rr[:, t % 2, :], bank[:, 0, :])
-                nc.gpsimd.tensor_tensor(scaled, rr[:, t % 2, :], picked["lb"][:, t, lo : lo + HALF], MULT)
+                nc.gpsimd.tensor_tensor(scaled, rr[:, t % 2, :], picked["lb", u][:, t, :], MULT)
             else:
-                nc.vector.tensor_tensor(scaled, bank[:, 0, :], picked["lb"][:, t, lo : lo + HALF], MULT)
+                nc.vector.tensor_tensor(scaled, bank[:, 0, :], picked["lb", u][:, t, :], MULT)
 
         for at in range(0, H_ON_GPSIMD, P):
             form_h(at)
@@ -236,14 +239,32 @@ def tile_picked_yvera_none_po_kernel(
         quantize_h(0)
         quantize_h(1)
         round_weight(nc.scalar.copy, "w3", 0)
-        round_weight(nc.scalar.copy, "w3", 1)
-        quantize_weight("w3", 0)
+        pairs = [tile("w3_1_low", [P, 2 * COLUMNS], BF16), tile("w3_1_bf", [P, 2 * COLUMNS], BF16, tag="h_bf1")]
+        nc.scalar.copy(
+            pairs[0][:].rearrange("p (u m j) -> p m j u", u=2, j=PACK),
+            raw["w3", 1][:].rearrange("p j (m h u) -> p h m j u", h=2, u=2)[:, 0],
+        )
+        for u in range(2):
+            nc.gpsimd.tensor_scalar(
+                pairs[1][:, u * COLUMNS : (u + 1) * COLUMNS].rearrange("p (m j) -> p m j", j=PACK),
+                raw["w3", 1][:].rearrange("p j (m t) -> p t m j", t=PACK)[:, 2 + u],
+                1.0,
+                0.0,
+                MULT,
+                ADD,
+            )
         term[0] = tile("term0", [P, PACK, HALF], F32)
         for t in range(PACK):
             form_term(0, t)
-        quantize_weight("w3", 1)
+        quantize_weight("w3", 0, tag="lb_picked0")
+        codes = tile("w3_1_codes", [P, COLUMNS], U32)
+        scales = tile("w3_1_scales", [P, COLUMNS], U8)
+        for h in range(2):
+            columns = slice(h * 2 * P, (h + 1) * 2 * P)
+            nc.vector.quantize_mx(out=codes[:, columns].bitcast(FP8X4), scales=scales[:, columns], in_=pairs[h][:])
+        weight["w3", 1] = (codes, scales)
         rr = tile("rr", [P, 2, HALF], F32, tag="w3_1_raw")
-        term[1] = tile("term1", [P, PACK, HALF], F32, tag="w3_1_bf")
+        term[1] = tile("term1", [P, PACK, HALF], F32, tag="h_bf1")
         for t in (2, 3, 0, 1):
             form_term(1, t)
 

@@ -28,7 +28,6 @@ QUARTER = S // 4
 SPARE = 32
 WINDOW = R + SPARE
 H_ON_GPSIMD = 384
-EE_BANKS = (0, 1, 2, 3, 6, 7, 4, 5)
 
 
 def tile_picked_yvera_none_po_kernel(
@@ -89,17 +88,22 @@ def tile_picked_yvera_none_po_kernel(
 
         xs_in = tile("xs_in", [P, T], U8)
         nc.vector.memset(xs_in[:].bitcast(I32), 0)
+        scale_rows = [(g, i) for i in range(4) for g in range(PASSES)]
+
+        def load_scales(lo, hi):
+            for g, i in scale_rows[lo:hi]:
+                nc.sync.dma_start(xs_in[4 * g + i : P : 32, :].bitcast(I32), x_scales[g, i:16:4, :].bitcast(I32))
+
         load_plane(ld, "ld", 0)
         nc.sync.dma_start(ad_t[:], ad)
-        for t in range(1, PACK):
-            load_plane(ld, "ld", t)
-        for q in range(4):
-            nc.sync.dma_start(
-                xs_in[32 * q : 32 * q + 4 * PASSES, :].bitcast(I32),
-                x_scales[:, 4 * q : 4 * q + 4, :].bitcast(I32),
-            )
-        nc.sync.dma_start(offs_t[:], offs)
+        load_plane(ld, "ld", 1)
+        load_scales(0, 2)
+        load_plane(ld, "ld", 2)
+        load_scales(2, 4)
+        load_plane(ld, "ld", 3)
+        load_scales(4, 8)
         load_weight(w1, 0, "w1")
+        nc.sync.dma_start(offs_t[:], offs)
         load_plane(lb, "lb", 0)
         load_plane(lb, "lb", 1)
         x_in = [load_words(0)]
@@ -112,30 +116,32 @@ def tile_picked_yvera_none_po_kernel(
         load_weight(w3, 1, "w3")
 
         picked = {}
-        for name in ("ld", "lb"):
-            for u in range(2):
-                label = "%s_picked%d" % (name, u)
-                picked[name, u] = tile(label, [P, PACK, HALF], F32, tag=label)
+        for u in range(2):
+            whole = tile("ld_picked%d" % u, [P, PACK, HALF], F32)
+            picked["ld", u] = whole
+            for t in range(PACK):
+                picked["ld", u, t] = whole[:, t, :]
+                label = "lb_picked%d_%d" % (u, t)
+                picked["lb", u, t] = tile(label, [P, HALF], F32, tag=label)[:]
 
         def look_up(name, t, lo, hi):
             columns = planes[name, t][:].indirect(entries(ad_t, lo, hi))
             if name == "ld" and t % 2 == 1:
-                nc.vector.tensor_copy(picked[name, lo // HALF][:, t, :], columns)
+                nc.vector.tensor_copy(picked[name, lo // HALF, t], columns)
             else:
-                nc.scalar.activation(picked[name, lo // HALF][:, t, :], columns, COPY)
+                nc.scalar.activation(picked[name, lo // HALF, t], columns, COPY)
 
         x_sc = tile("x_sc", [P, S], U8)
         x_codes = {}
 
+        for g in range(PASSES):
+            x_codes[g] = tile("x%d_codes" % g, [P, S], U32)
+
         def gather_words(g, lo, hi):
-            codes = tile("x%d_codes%d" % (g, lo), [P, hi - lo], U32)
-            nc.vector.tensor_copy(codes[:], x_in[g][:].bitcast(U32).indirect(entries(offs_t, lo, hi)))
-            for at in range(lo, hi, P):
-                x_codes[g, at] = (codes, lo)
+            nc.vector.tensor_copy(x_codes[g][:, lo:hi], x_in[g][:].bitcast(U32).indirect(entries(offs_t, lo, hi)))
 
         def tokens(g, lo, hi):
-            codes, first = x_codes[g, lo]
-            return codes[:, lo - first : hi - first], x_sc[4 * g : P, lo:hi]
+            return x_codes[g][:, lo:hi], x_sc[4 * g : P, lo:hi]
 
         def take_bank(number, shape):
             return psum.tile(shape, F32, name="bank%d" % number, tag="bank%d" % number, offset=number * BANK * 4)
@@ -223,12 +229,12 @@ def tile_picked_yvera_none_po_kernel(
         def form_term(u, t):
             bank = take_bank(PACK * u + t, [P, 1, HALF])
             product("w2", [(h_codes[u][:], h_scales[u][:])], bank, t, 1)
-            scaled = term[u][:, t, :]
+            scaled = term[u, t // 2][:, t % 2, :]
             if u == 1 and t >= 2:
                 nc.scalar.copy(rr[:, t % 2, :], bank[:, 0, :])
-                nc.gpsimd.tensor_tensor(scaled, rr[:, t % 2, :], picked["lb", u][:, t, :], MULT)
+                nc.gpsimd.tensor_tensor(scaled, rr[:, t % 2, :], picked["lb", u, t], MULT)
             else:
-                nc.vector.tensor_tensor(scaled, bank[:, 0, :], picked["lb", u][:, t, :], MULT)
+                nc.vector.tensor_tensor(scaled, bank[:, 0, :], picked["lb", u, t], MULT)
 
         for at in range(0, H_ON_GPSIMD, P):
             form_h(at)
@@ -253,47 +259,47 @@ def tile_picked_yvera_none_po_kernel(
                 MULT,
                 ADD,
             )
-        term[0] = tile("term0", [P, PACK, HALF], F32)
-        for t in range(PACK):
+        term[0, 0] = tile("term0_0", [P, 2, HALF], F32)
+        for t in range(2):
             form_term(0, t)
-        quantize_weight("w3", 0, tag="lb_picked0")
+        quantize_weight("w3", 0, tag="lb_picked0_1")
         codes = tile("w3_1_codes", [P, COLUMNS], U32)
         scales = tile("w3_1_scales", [P, COLUMNS], U8)
         for h in range(2):
             columns = slice(h * 2 * P, (h + 1) * 2 * P)
             nc.vector.quantize_mx(out=codes[:, columns].bitcast(FP8X4), scales=scales[:, columns], in_=pairs[h][:])
         weight["w3", 1] = (codes, scales)
+        term[0, 1] = tile("term0_1", [P, 2, HALF], F32, tag="w3_0_bf")
+        for t in range(2, PACK):
+            form_term(0, t)
         rr = tile("rr", [P, 2, HALF], F32, tag="w3_1_raw")
-        term[1] = tile("term1", [P, PACK, HALF], F32, tag="h_bf1")
-        for t in (2, 3, 0, 1):
+        late = tile("term1", [P, PACK, HALF], F32, tag="h_bf1")
+        for pair in range(2):
+            term[1, pair] = late[:, 2 * pair : 2 * pair + 2, :]
+        for t in (2, 3):
             form_term(1, t)
 
-        result = {}
+        result = tile("result", [P, PACK, S], F32)
 
-        def total(lo):
-            result[lo] = tile("result%d" % lo, [P, PACK, QUARTER], F32)
-            for pair in range(2):
-                bank = take_bank(EE_BANKS[2 * (lo // QUARTER) + pair], [P, 2, QUARTER])
-                moving = []
-                for g in range(PASSES):
-                    moving.append(tokens(g, lo, lo + QUARTER))
-                product("w3", moving, bank, 2 * pair, 2)
-                ts = slice(2 * pair, 2 * pair + 2)
-                scaled = term[lo // HALF][:, ts, lo % HALF : lo % HALF + QUARTER]
-                if lo == 0 and pair == 1:
-                    ee = tile("ee%d" % lo, [P, 2, QUARTER], F32)
-                    nc.scalar.copy(ee[:], bank[:])
-                    nc.gpsimd.tensor_tensor(result[lo][:, ts, :], ee[:], scaled, ADD)
-                else:
-                    nc.vector.tensor_tensor(result[lo][:, ts, :], bank[:], scaled, ADD)
-                nc.sync.dma_start(out_rows[:, ts, lo : lo + QUARTER], result[lo][:, ts, :])
+        def total(first, count, lo, number, on_gpsimd=False):
+            n = BANK // count
+            ts = slice(first, first + count)
+            bank = take_bank(number, [P, count, n])
+            product("w3", [tokens(g, lo, lo + n) for g in range(PASSES)], bank, first, count)
+            scaled = term[lo // HALF, first // 2][:, first % 2 : first % 2 + count, lo % HALF : lo % HALF + n]
+            if on_gpsimd:
+                ee = tile("ee%d" % lo, [P, count, n], F32)
+                nc.scalar.copy(ee[:], bank[:])
+                nc.gpsimd.tensor_tensor(result[:, ts, lo : lo + n], ee[:], scaled, ADD)
+            else:
+                nc.vector.tensor_tensor(result[:, ts, lo : lo + n], bank[:], scaled, ADD)
+            nc.sync.dma_start(out_rows[:, ts, lo : lo + n], result[:, ts, lo : lo + n])
 
         woven = {}
 
         def round_out(copy, lo, hi):
-            first = lo - lo % QUARTER
             woven[lo] = tile("o_bf%d" % lo, [P, (hi - lo) * PACK], BF16)
-            copy(as_woven(woven[lo][:]), as_planes(result[first][:, :, lo - first : hi - first]))
+            copy(as_woven(woven[lo][:]), as_planes(result[:, :, lo:hi]))
 
         def quantize_out(lo, hi):
             nc.vector.quantize_mx(out=out_codes[:, lo:hi].bitcast(FP8X4), scales=out_scales[:, lo:hi], in_=woven[lo][:])
@@ -302,13 +308,21 @@ def tile_picked_yvera_none_po_kernel(
             nc.sync.dma_start(out_words[:, lo:hi], out_codes[:, lo:hi].bitcast(I32))
 
         last = S - QUARTER
-        for lo in range(0, S, QUARTER):
-            total(lo)
-        for lo in (QUARTER, 0, HALF):
+        total(0, 1, 0, 0)
+        total(1, 1, 0, 1)
+        total(3, 1, 0, 3, on_gpsimd=True)
+        for t in (0, 1):
+            form_term(1, t)
+        total(2, 1, 0, 2)
+        total(2, 2, HALF, 6, on_gpsimd=True)
+        total(0, 2, HALF, 7)
+        total(0, 2, last, 4)
+        total(2, 2, last, 5)
+        for lo in (0, QUARTER, HALF):
             round_out(nc.scalar.copy, lo, lo + QUARTER)
         round_out(nc.vector.tensor_copy, last, S)
-        quantize_out(QUARTER, HALF)
         quantize_out(0, QUARTER)
+        quantize_out(QUARTER, HALF)
         store_words(0, HALF)
         quantize_out(last, S)
         quantize_out(HALF, last)

@@ -27,7 +27,9 @@ HALF = S // 2
 QUARTER = S // 4
 SPARE = 32
 WINDOW = R + SPARE
-H_ON_GPSIMD = 384
+H_ON_GPSIMD = 256
+Y_BANKS = (0, 1, 2, 3, 4, 0, 1, 2)
+RR_BANKS = ((5, 6, 7, 3), (1, 2, 4, 0))
 
 
 def tile_picked_yvera_none_po_kernel(
@@ -199,14 +201,18 @@ def tile_picked_yvera_none_po_kernel(
         gather_words(1, QUARTER, HALF)
         gather_words(1, HALF, S)
 
-        h_bf = [tile("h_bf%d" % u, [P, HALF * PACK], BF16, tag="h_bf%d" % u) for u in range(2)]
+        pieces = ((0, HALF), (HALF, S - QUARTER), (S - QUARTER, S))
+        h_bf = {}
         h_codes = [tile("h_codes%d" % u, [P, HALF], U32) for u in range(2)]
         h_scales = [tile("h_scales%d" % u, [P, HALF], U8) for u in range(2)]
 
         def form_h(at):
-            bank = take_bank(at // P, [P, PACK, P])
+            bank = take_bank(Y_BANKS[at // P], [P, PACK, P])
             product("w1", [tokens(g, at, at + P) for g in range(PASSES)], bank, 0, PACK)
             c = at % HALF
+            ((lo, hi),) = [(lo, hi) for lo, hi in pieces if lo <= at < hi]
+            if at == lo:
+                h_bf[lo] = tile("h_bf%d" % lo, [P, (hi - lo) * PACK], BF16, tag="h_bf%d" % (lo % (S - QUARTER)))
             if at < H_ON_GPSIMD:
                 y_woven = tile("y_woven%d" % at, [P, P * PACK], F32, tag="y_woven%d" % at)
                 nc.scalar.copy(y_woven[:].rearrange("p (n t) -> p n t", t=PACK), bank[:].rearrange("p t n -> p n t"))
@@ -215,91 +221,80 @@ def tile_picked_yvera_none_po_kernel(
                 )
                 return
             nc.vector.tensor_tensor(
-                as_woven(h_bf[at // HALF][:, c * PACK : (c + P) * PACK]),
+                as_woven(h_bf[lo][:, (at - lo) * PACK : (at - lo + P) * PACK]),
                 as_planes(bank[:]),
                 as_planes(picked["ld", at // HALF][:, :, c : c + P]),
                 MULT,
             )
 
-        def quantize_h(u):
-            nc.vector.quantize_mx(out=h_codes[u][:].bitcast(FP8X4), scales=h_scales[u][:], in_=h_bf[u][:])
+        def quantize_h(lo, hi):
+            u, columns = lo // HALF, slice(lo % HALF, lo % HALF + hi - lo)
+            nc.vector.quantize_mx(
+                out=h_codes[u][:, columns].bitcast(FP8X4), scales=h_scales[u][:, columns], in_=h_bf[lo][:]
+            )
 
         term = {}
 
-        def form_term(u, t):
-            bank = take_bank(PACK * u + t, [P, 1, HALF])
+        def form_term(u, t, rr=None):
+            bank = take_bank(RR_BANKS[u][t], [P, 1, HALF])
             product("w2", [(h_codes[u][:], h_scales[u][:])], bank, t, 1)
-            scaled = term[u, t // 2][:, t % 2, :]
-            if u == 1 and t >= 2:
-                nc.scalar.copy(rr[:, t % 2, :], bank[:, 0, :])
-                nc.gpsimd.tensor_tensor(scaled, rr[:, t % 2, :], picked["lb", u, t], MULT)
+            scaled = term[u, t]
+            if rr is not None:
+                nc.scalar.copy(rr, bank[:, 0, :])
+                nc.gpsimd.tensor_tensor(scaled, rr, picked["lb", u, t], MULT)
             else:
                 nc.vector.tensor_tensor(scaled, bank[:, 0, :], picked["lb", u, t], MULT)
 
         for at in range(0, H_ON_GPSIMD, P):
             form_h(at)
         round_weight(nc.scalar.copy, "w2", 0)
-        for at in range(H_ON_GPSIMD, S, P):
+        for at in range(H_ON_GPSIMD, S - QUARTER, P):
             form_h(at)
         quantize_weight("w2", 0, tag="y_woven%d" % (H_ON_GPSIMD - P))
-        quantize_h(0)
-        quantize_h(1)
+        quantize_h(*pieces[0])
+        for at in range(S - QUARTER, S, P):
+            form_h(at)
+        quantize_h(*pieces[1])
+        quantize_h(*pieces[2])
         round_weight(nc.scalar.copy, "w3", 0)
-        pairs = [tile("w3_1_low", [P, 2 * COLUMNS], BF16), tile("w3_1_bf", [P, 2 * COLUMNS], BF16, tag="h_bf1")]
-        nc.scalar.copy(
-            pairs[0][:].rearrange("p (u m j) -> p m j u", u=2, j=PACK),
-            raw["w3", 1][:].rearrange("p j (m h u) -> p h m j u", h=2, u=2)[:, 0],
-        )
-        for u in range(2):
-            nc.gpsimd.tensor_scalar(
-                pairs[1][:, u * COLUMNS : (u + 1) * COLUMNS].rearrange("p (m j) -> p m j", j=PACK),
-                raw["w3", 1][:].rearrange("p j (m t) -> p t m j", t=PACK)[:, 2 + u],
-                1.0,
-                0.0,
-                MULT,
-                ADD,
-            )
-        term[0, 0] = tile("term0_0", [P, 2, HALF], F32)
-        for t in range(2):
+        quantize_weight("w3", 0)
+        term[0, 3] = tile("term0_3", [P, HALF], F32, tag="w3_0_bf")[:]
+        rr_early = tile("rr_early", [P, HALF], F32, tag="w3_0_raw")
+        form_term(0, 3, rr_early[:])
+        for t in range(PACK - 1):
+            term[0, t] = tile("term0_%d" % t, [P, HALF], F32)[:]
             form_term(0, t)
-        quantize_weight("w3", 0, tag="lb_picked0_1")
-        codes = tile("w3_1_codes", [P, COLUMNS], U32)
-        scales = tile("w3_1_scales", [P, COLUMNS], U8)
-        for h in range(2):
-            columns = slice(h * 2 * P, (h + 1) * 2 * P)
-            nc.vector.quantize_mx(out=codes[:, columns].bitcast(FP8X4), scales=scales[:, columns], in_=pairs[h][:])
-        weight["w3", 1] = (codes, scales)
-        term[0, 1] = tile("term0_1", [P, 2, HALF], F32, tag="w3_0_bf")
-        for t in range(2, PACK):
-            form_term(0, t)
-        rr = tile("rr", [P, 2, HALF], F32, tag="w3_1_raw")
-        late = tile("term1", [P, PACK, HALF], F32, tag="h_bf1")
-        for pair in range(2):
-            term[1, pair] = late[:, 2 * pair : 2 * pair + 2, :]
-        for t in (2, 3):
-            form_term(1, t)
+        round_weight(nc.scalar.copy, "w3", 1)
+        quantize_weight("w3", 1, tag="lb_picked0_2")
+        rr_late = tile("rr_late", [P, 2, HALF], F32, tag="w3_1_raw")
+        late = tile("term1", [P, PACK - 1, HALF], F32, tag="w3_1_bf")
+        for t in range(PACK - 1):
+            term[1, t] = late[:, t, :]
+        form_term(1, 2, rr_late[:, 0, :])
+        form_term(1, 0)
 
-        result = tile("result", [P, PACK, S], F32)
+        result = [tile("result%d" % u, [P, PACK, HALF], F32) for u in range(2)]
 
-        def total(first, count, lo, number, on_gpsimd=False):
-            n = BANK // count
-            ts = slice(first, first + count)
-            bank = take_bank(number, [P, count, n])
-            product("w3", [tokens(g, lo, lo + n) for g in range(PASSES)], bank, first, count)
-            scaled = term[lo // HALF, first // 2][:, first % 2 : first % 2 + count, lo % HALF : lo % HALF + n]
-            if on_gpsimd:
-                ee = tile("ee%d" % lo, [P, count, n], F32)
-                nc.scalar.copy(ee[:], bank[:])
-                nc.gpsimd.tensor_tensor(result[:, ts, lo : lo + n], ee[:], scaled, ADD)
+        def total(u, t, number):
+            lo = u * HALF
+            bank = take_bank(number, [P, 1, HALF])
+            product("w3", [tokens(g, lo, lo + HALF) for g in range(PASSES)], bank, t, 1)
+            if t == PACK - 1:
+                ee = tile("ee%d" % u, [P, HALF], F32, tag="ee%d" % u)
+                nc.scalar.copy(ee[:], bank[:, 0, :])
+                nc.gpsimd.tensor_tensor(result[u][:, t, :], ee[:], term[u, t], ADD)
             else:
-                nc.vector.tensor_tensor(result[:, ts, lo : lo + n], bank[:], scaled, ADD)
-            nc.sync.dma_start(out_rows[:, ts, lo : lo + n], result[:, ts, lo : lo + n])
+                nc.vector.tensor_tensor(result[u][:, t, :], bank[:, 0, :], term[u, t], ADD)
+
+        def store(u, first, count):
+            ts, columns = slice(first, first + count), slice(u * HALF, (u + 1) * HALF)
+            nc.sync.dma_start(out_rows[:, ts, columns], result[u][:, ts, :])
 
         woven = {}
 
         def round_out(copy, lo, hi):
             woven[lo] = tile("o_bf%d" % lo, [P, (hi - lo) * PACK], BF16)
-            copy(as_woven(woven[lo][:]), as_planes(result[:, :, lo:hi]))
+            copy(as_woven(woven[lo][:]), as_planes(result[lo // HALF][:, :, lo % HALF : lo % HALF + hi - lo]))
 
         def quantize_out(lo, hi):
             nc.vector.quantize_mx(out=out_codes[:, lo:hi].bitcast(FP8X4), scales=out_scales[:, lo:hi], in_=woven[lo][:])
@@ -308,20 +303,25 @@ def tile_picked_yvera_none_po_kernel(
             nc.sync.dma_start(out_words[:, lo:hi], out_codes[:, lo:hi].bitcast(I32))
 
         last = S - QUARTER
-        total(0, 1, 0, 0)
-        total(1, 1, 0, 1)
-        total(3, 1, 0, 3, on_gpsimd=True)
-        for t in (0, 1):
-            form_term(1, t)
-        total(2, 1, 0, 2)
-        total(2, 2, HALF, 6, on_gpsimd=True)
-        total(0, 2, HALF, 7)
-        total(0, 2, last, 4)
-        total(2, 2, last, 5)
+        total(0, 3, 3)
+        for t in range(PACK - 1):
+            total(0, t, 5 + t)
+        store(0, 0, 1)
+        store(0, 1, 1)
+        store(0, 2, 2)
+        term[1, 3] = tile("term1_3", [P, HALF], F32, tag="ee0")[:]
+        form_term(1, 3, rr_late[:, 1, :])
+        form_term(1, 1)
+        total(1, 3, 4)
+        for t, number in enumerate((1, 0, 5)):
+            total(1, t, number)
+        store(1, 0, 1)
+        store(1, 1, 1)
+        store(1, 2, 2)
         for lo in (0, QUARTER, HALF):
             round_out(nc.scalar.copy, lo, lo + QUARTER)
-        round_out(nc.vector.tensor_copy, last, S)
         quantize_out(0, QUARTER)
+        round_out(nc.vector.tensor_copy, last, S)
         quantize_out(QUARTER, HALF)
         store_words(0, HALF)
         quantize_out(last, S)

@@ -29,7 +29,7 @@ SPARE = 32
 WINDOW = R + SPARE
 H_ON_GPSIMD = 256
 Y_BANKS = (0, 1, 2, 3, 4, 0, 1, 2)
-RR_BANKS = ((5, 6, 7, 3), (1, 2, 4, 0))
+RR_BANKS = ((5, 6, 7, 3), (1, 2, 3, 4))
 
 
 def tile_picked_yvera_none_po_kernel(
@@ -106,13 +106,13 @@ def tile_picked_yvera_none_po_kernel(
         load_scales(4, 8)
         load_weight(w1, 0, "w1")
         nc.sync.dma_start(offs_t[:], offs)
-        load_plane(lb, "lb", 0)
         load_plane(lb, "lb", 1)
         x_in = [load_words(0)]
         load_plane(lb, "lb", 2)
         load_weight(w1, 1, "w1")
         load_plane(lb, "lb", 3)
         x_in.append(load_words(1))
+        load_plane(lb, "lb", 0)
         load_weight(w2, 0, "w2")
         load_weight(w3, 0, "w3")
         load_weight(w3, 1, "w3")
@@ -124,11 +124,12 @@ def tile_picked_yvera_none_po_kernel(
             for t in range(PACK):
                 picked["ld", u, t] = whole[:, t, :]
                 label = "lb_picked%d_%d" % (u, t)
-                picked["lb", u, t] = tile(label, [P, HALF], F32, tag=label)[:]
+                if (u, t) != (1, 0):
+                    picked["lb", u, t] = tile(label, [P, HALF], F32, tag=label)[:]
 
         def look_up(name, t, lo, hi):
             columns = planes[name, t][:].indirect(entries(ad_t, lo, hi))
-            if name == "ld" and t % 2 == 1:
+            if (name, t) in (("ld", 1), ("ld", 3)):
                 nc.vector.tensor_copy(picked[name, lo // HALF, t], columns)
             else:
                 nc.scalar.activation(picked[name, lo // HALF, t], columns, COPY)
@@ -177,7 +178,19 @@ def tile_picked_yvera_none_po_kernel(
         for t in range(PACK):
             for lo in (0, HALF):
                 look_up("ld", t, lo, lo + HALF)
-        ld_woven = tile("ld_woven", [P, H_ON_GPSIMD * PACK], F32)
+        nc.vector.tensor_copy(x_sc[:], xs_in[:].indirect(offs_t[:]))
+        dealt["w1", 0] = tile("w1_0_bf", [P, PACK * COLUMNS], BF16, tag="w1_0_bf")
+        for t in range(PACK):
+            nc.gpsimd.tensor_scalar(
+                dealt["w1", 0][:, t * COLUMNS : (t + 1) * COLUMNS].rearrange("p (m j) -> p m j", j=PACK),
+                raw["w1", 0][:].rearrange("p j (m t) -> p t m j", t=PACK)[:, t],
+                1.0,
+                0.0,
+                MULT,
+                ADD,
+            )
+        quantize_weight("w1", 0)
+        ld_woven = tile("ld_woven", [P, H_ON_GPSIMD * PACK], F32, tag="w1_0_bf")
         for at in range(0, H_ON_GPSIMD, P):
             nc.gpsimd.tensor_scalar(
                 ld_woven[:, at * PACK : (at + P) * PACK].rearrange("p (n t) -> p n t", t=PACK),
@@ -187,18 +200,16 @@ def tile_picked_yvera_none_po_kernel(
                 MULT,
                 ADD,
             )
-        nc.vector.tensor_copy(x_sc[:], xs_in[:].indirect(offs_t[:]))
-        round_weight(nc.vector.tensor_copy, "w1", 0)
-        quantize_weight("w1", 0)
         gather_words(0, 0, HALF)
         gather_words(0, HALF, S)
         round_weight(nc.vector.tensor_copy, "w1", 1)
         quantize_weight("w1", 1)
-        for t in range(PACK):
+        for t in range(1, PACK):
             for lo in (0, HALF):
                 look_up("lb", t, lo, lo + HALF)
-        gather_words(1, 0, QUARTER)
-        gather_words(1, QUARTER, HALF)
+        look_up("lb", 0, 0, HALF)
+        gather_words(1, 0, P)
+        gather_words(1, P, HALF)
         gather_words(1, HALF, S)
 
         pieces = ((0, HALF), (HALF, S - QUARTER), (S - QUARTER, S))
@@ -212,7 +223,7 @@ def tile_picked_yvera_none_po_kernel(
             c = at % HALF
             ((lo, hi),) = [(lo, hi) for lo, hi in pieces if lo <= at < hi]
             if at == lo:
-                h_bf[lo] = tile("h_bf%d" % lo, [P, (hi - lo) * PACK], BF16, tag="h_bf%d" % (lo % (S - QUARTER)))
+                h_bf[lo] = tile("h_bf%d" % lo, [P, (hi - lo) * PACK], BF16, tag="w2_0_bf" if hi == S else "h_bf%d" % lo)
             if at < H_ON_GPSIMD:
                 y_woven = tile("y_woven%d" % at, [P, P * PACK], F32, tag="y_woven%d" % at)
                 nc.scalar.copy(y_woven[:].rearrange("p (n t) -> p n t", t=PACK), bank[:].rearrange("p t n -> p n t"))
@@ -264,27 +275,40 @@ def tile_picked_yvera_none_po_kernel(
         for t in range(PACK - 1):
             term[0, t] = tile("term0_%d" % t, [P, HALF], F32)[:]
             form_term(0, t)
-        round_weight(nc.scalar.copy, "w3", 1)
-        quantize_weight("w3", 1, tag="lb_picked0_2")
-        rr_late = tile("rr_late", [P, 2, HALF], F32, tag="w3_1_raw")
-        late = tile("term1", [P, PACK - 1, HALF], F32, tag="w3_1_bf")
-        for t in range(PACK - 1):
-            term[1, t] = late[:, t, :]
-        form_term(1, 2, rr_late[:, 0, :])
-        form_term(1, 0)
+        codes = tile("w3_1_codes", [P, COLUMNS], U32, tag="lb_picked0_1")
+        scales = tile("w3_1_scales", [P, COLUMNS], U8)
+        pairs = [tile("w3_1_pair%d" % h, [P, 2 * COLUMNS], BF16, tag="w3_1_pair%d" % h) for h in range(2)]
+        for h in (1, 0):
+            nc.scalar.copy(
+                pairs[h][:].rearrange("p (u m j) -> p m j u", u=2, j=PACK),
+                raw["w3", 1][:].rearrange("p j (m h u) -> p h m j u", h=2, u=2)[:, h],
+            )
+        for h in (1, 0):
+            columns = slice(h * 2 * P, (h + 1) * 2 * P)
+            nc.vector.quantize_mx(out=codes[:, columns].bitcast(FP8X4), scales=scales[:, columns], in_=pairs[h][:])
+        weight["w3", 1] = (codes, scales)
+        rr_late = tile("late_on_scalar", [P, 2, HALF], F32, tag="w3_1_raw")
+        on_vector = tile("terms_vector", [P, 2, HALF], F32, tag="w3_1_pair1")
+        on_gpsimd = tile("terms_gpsimd", [P, 2, HALF], F32, tag="w3_1_pair0")
+        for t in range(PACK):
+            term[1, t] = (on_vector, on_gpsimd)[t // 2][:, t % 2, :]
+        form_term(1, 3, rr_late[:, 1, :])
+        picked["lb", 1, 0] = rr_late[:, 0, :]
+        look_up("lb", 0, HALF, S)
+        form_term(1, 1)
 
         result = [tile("result%d" % u, [P, PACK, HALF], F32) for u in range(2)]
 
-        def total(u, t, number):
+        def total(u, t, number, a=0, b=HALF):
             lo = u * HALF
-            bank = take_bank(number, [P, 1, HALF])
-            product("w3", [tokens(g, lo, lo + HALF) for g in range(PASSES)], bank, t, 1)
-            if t == PACK - 1:
-                ee = tile("ee%d" % u, [P, HALF], F32, tag="ee%d" % u)
+            bank = take_bank(number, [P, 1, b - a])
+            product("w3", [tokens(g, lo + a, lo + b) for g in range(PASSES)], bank, t, 1)
+            if t == PACK - 1 and a == 0:
+                ee = tile("ee%d" % u, [P, b - a], F32)
                 nc.scalar.copy(ee[:], bank[:, 0, :])
-                nc.gpsimd.tensor_tensor(result[u][:, t, :], ee[:], term[u, t], ADD)
+                nc.gpsimd.tensor_tensor(result[u][:, t, a:b], ee[:], term[u, t][:, a:b], ADD)
             else:
-                nc.vector.tensor_tensor(result[u][:, t, :], bank[:, 0, :], term[u, t], ADD)
+                nc.vector.tensor_tensor(result[u][:, t, a:b], bank[:, 0, :], term[u, t][:, a:b], ADD)
 
         def store(u, first, count):
             ts, columns = slice(first, first + count), slice(u * HALF, (u + 1) * HALF)
@@ -309,14 +333,14 @@ def tile_picked_yvera_none_po_kernel(
         store(0, 0, 1)
         store(0, 1, 1)
         store(0, 2, 2)
-        term[1, 3] = tile("term1_3", [P, HALF], F32, tag="ee0")[:]
-        form_term(1, 3, rr_late[:, 1, :])
-        form_term(1, 1)
-        total(1, 3, 4)
-        for t, number in enumerate((1, 0, 5)):
+        form_term(1, 2, tile("rr1_2", [P, HALF], F32)[:])
+        form_term(1, 0)
+        total(1, 3, 4, 0, QUARTER)
+        total(1, 3, 5, QUARTER, HALF)
+        for t, number in ((1, 0), (0, 2), (2, 1)):
             total(1, t, number)
-        store(1, 0, 1)
         store(1, 1, 1)
+        store(1, 0, 1)
         store(1, 2, 2)
         for lo in (0, QUARTER, HALF):
             round_out(nc.scalar.copy, lo, lo + QUARTER)
@@ -325,8 +349,9 @@ def tile_picked_yvera_none_po_kernel(
         quantize_out(QUARTER, HALF)
         store_words(0, HALF)
         quantize_out(last, S)
+        store_words(last, S)
         quantize_out(HALF, last)
-        store_words(HALF, S)
+        store_words(HALF, last)
         for q in range(4):
             queue = nc.sync if q % 2 == 0 else nc.scalar
             queue.dma_start(

@@ -129,7 +129,7 @@ def tile_picked_yvera_none_po_kernel(
 
         def look_up(name, t, lo, hi):
             columns = planes[name, t][:].indirect(entries(ad_t, lo, hi))
-            if (name, t) in (("ld", 1), ("ld", 3)):
+            if (name, t) == ("ld", 1) or (name, t, lo) == ("ld", 3, 0):
                 nc.vector.tensor_copy(picked[name, lo // HALF, t], columns)
             else:
                 nc.scalar.activation(picked[name, lo // HALF, t], columns, COPY)
@@ -179,18 +179,9 @@ def tile_picked_yvera_none_po_kernel(
             for lo in (0, HALF):
                 look_up("ld", t, lo, lo + HALF)
         nc.vector.tensor_copy(x_sc[:], xs_in[:].indirect(offs_t[:]))
-        dealt["w1", 0] = tile("w1_0_bf", [P, PACK * COLUMNS], BF16, tag="w1_0_bf")
-        for t in range(PACK):
-            nc.gpsimd.tensor_scalar(
-                dealt["w1", 0][:, t * COLUMNS : (t + 1) * COLUMNS].rearrange("p (m j) -> p m j", j=PACK),
-                raw["w1", 0][:].rearrange("p j (m t) -> p t m j", t=PACK)[:, t],
-                1.0,
-                0.0,
-                MULT,
-                ADD,
-            )
+        round_weight(nc.vector.tensor_copy, "w1", 0)
         quantize_weight("w1", 0)
-        ld_woven = tile("ld_woven", [P, H_ON_GPSIMD * PACK], F32, tag="w1_0_bf")
+        ld_woven = tile("ld_woven", [P, H_ON_GPSIMD * PACK], F32)
         for at in range(0, H_ON_GPSIMD, P):
             nc.gpsimd.tensor_scalar(
                 ld_woven[:, at * PACK : (at + P) * PACK].rearrange("p (n t) -> p n t", t=PACK),

@@ -99,13 +99,13 @@ def tile_picked_yvera_none_po_kernel(
         load_plane(ld, "ld", 0)
         nc.sync.dma_start(ad_t[:], ad)
         load_plane(ld, "ld", 1)
+        nc.sync.dma_start(offs_t[:], offs)
         load_scales(0, 2)
         load_plane(ld, "ld", 2)
         load_scales(2, 4)
         load_plane(ld, "ld", 3)
         load_scales(4, 8)
         load_weight(w1, 0, "w1")
-        nc.sync.dma_start(offs_t[:], offs)
         load_plane(lb, "lb", 1)
         x_in = [load_words(0)]
         load_plane(lb, "lb", 2)
@@ -170,7 +170,6 @@ def tile_picked_yvera_none_po_kernel(
         def as_planes(ap):
             return ap.rearrange("p t (a i) -> p a t i", i=4)
 
-        out_codes = tile("out_codes", [P, S], U32)
         out_scales = tile("out_scales", [P, S], U8)
         out_rows = out_0.rearrange("(p t) s -> p t s", t=PACK)
         out_words = out_1[0].rearrange("p c r -> p (c r)").bitcast(I32)
@@ -203,9 +202,9 @@ def tile_picked_yvera_none_po_kernel(
         gather_words(1, P, HALF)
         gather_words(1, HALF, S)
 
-        pieces = ((0, HALF), (HALF, S - QUARTER), (S - QUARTER, S))
+        pieces = ((0, HALF), (HALF, S - P), (S - P, S))
         h_bf = {}
-        h_codes = [tile("h_codes%d" % u, [P, HALF], U32) for u in range(2)]
+        h_codes = [tile("h_codes0", [P, HALF], U32)]
         h_scales = [tile("h_scales%d" % u, [P, HALF], U8) for u in range(2)]
 
         def form_h(at):
@@ -250,21 +249,22 @@ def tile_picked_yvera_none_po_kernel(
         for at in range(0, H_ON_GPSIMD, P):
             form_h(at)
         round_weight(nc.scalar.copy, "w2", 0)
-        for at in range(H_ON_GPSIMD, S - QUARTER, P):
+        for at in range(H_ON_GPSIMD, S - P, P):
             form_h(at)
         quantize_weight("w2", 0, tag="y_woven%d" % (H_ON_GPSIMD - P))
         quantize_h(*pieces[0])
-        for at in range(S - QUARTER, S, P):
-            form_h(at)
+        form_h(S - P)
+        h_codes.append(tile("h_codes1", [P, HALF], U32, tag="w2_0_raw"))
         quantize_h(*pieces[1])
         quantize_h(*pieces[2])
         round_weight(nc.scalar.copy, "w3", 0)
         quantize_weight("w3", 0)
-        term[0, 3] = tile("term0_3", [P, HALF], F32, tag="w3_0_bf")[:]
+        early = tile("terms_early", [P, PACK, HALF], F32, tag="w3_0_bf")
+        for t in range(PACK):
+            term[0, t] = early[:, t, :]
         rr_early = tile("rr_early", [P, HALF], F32, tag="w3_0_raw")
         form_term(0, 3, rr_early[:])
         for t in range(PACK - 1):
-            term[0, t] = tile("term0_%d" % t, [P, HALF], F32)[:]
             form_term(0, t)
         codes = tile("w3_1_codes", [P, COLUMNS], U32, tag="lb_picked0_1")
         scales = tile("w3_1_scales", [P, COLUMNS], U8)
@@ -295,7 +295,7 @@ def tile_picked_yvera_none_po_kernel(
             bank = take_bank(number, [P, 1, b - a])
             product("w3", [tokens(g, lo + a, lo + b) for g in range(PASSES)], bank, t, 1)
             if t == PACK - 1 and a == 0:
-                ee = tile("ee%d" % u, [P, b - a], F32)
+                ee = tile("ee%d" % u, [P, b - a], F32, tag="ee%d" % u)
                 nc.scalar.copy(ee[:], bank[:, 0, :])
                 nc.gpsimd.tensor_tensor(result[u][:, t, a:b], ee[:], term[u, t][:, a:b], ADD)
             else:
@@ -319,11 +319,10 @@ def tile_picked_yvera_none_po_kernel(
 
         last = S - QUARTER
         total(0, 3, 3)
-        for t in range(PACK - 1):
+        for t in (2, 0, 1):
             total(0, t, 5 + t)
-        store(0, 0, 1)
-        store(0, 1, 1)
-        store(0, 2, 2)
+        for t in (2, 0, 1, 3):
+            store(0, t, 1)
         form_term(1, 2, tile("rr1_2", [P, HALF], F32)[:])
         form_term(1, 0)
         total(1, 3, 4, 0, QUARTER)
@@ -333,6 +332,7 @@ def tile_picked_yvera_none_po_kernel(
         store(1, 1, 1)
         store(1, 0, 1)
         store(1, 2, 2)
+        out_codes = tile("out_codes", [P, S], U32, tag="ee1")
         for lo in (0, QUARTER, HALF):
             round_out(nc.scalar.copy, lo, lo + QUARTER)
         quantize_out(0, QUARTER)

@@ -22,14 +22,23 @@ K_PASS = P * PACK
 PASSES = K // K_PASS
 COLUMNS = 512
 LIST_ROWS = 16
+QUADRANT = 32
+SCALE_ROWS = 4
 BANK = 512
 HALF = S // 2
 QUARTER = S // 4
+LAST = S - QUARTER
 SPARE = 32
 WINDOW = R + SPARE
 H_ON_GPSIMD = 256
+GPSIMD_PLANE = PACK - 1
+LATE_PLANE = 0
+H_PIECES = ((0, HALF), (HALF, S - P), (S - P, S))
+
 Y_BANKS = (0, 1, 2, 3, 4, 0, 1, 2)
 RR_BANKS = ((5, 6, 7, 3), (1, 2, 3, 4))
+EE_BANKS = ((5, 6, 7, 3), (2, 0, 1, 4))
+EE_LAST_BANK = 5
 
 
 def tile_picked_yvera_none_po_kernel(
@@ -49,6 +58,11 @@ def tile_picked_yvera_none_po_kernel(
         def tile(name, shape, dtype, **place):
             return keep.tile(shape, dtype, name=name, align_bytes=64, **place)
 
+        raw = {}
+        dealt = {}
+        weight = {}
+        table = {}
+
         def load_words(g):
             words = tile("x_in%d" % g, [P, T], I32)
             nc.sync.dma_start(words[:], x_words[g].rearrange("p c r -> p (c r)").bitcast(I32))
@@ -56,31 +70,26 @@ def tile_picked_yvera_none_po_kernel(
 
         def load_weight(w, g, name):
             label = "%s_%d_raw" % (name, g)
-            rows = tile(label, [P, PACK, COLUMNS], F32, tag=label)
-            nc.sync.dma_start(rows[:], w[g * K_PASS : (g + 1) * K_PASS, :].rearrange("(p j) c -> p j c", j=PACK))
-            raw[name, g] = rows
+            raw[name, g] = tile(label, [P, PACK, COLUMNS], F32, tag=label)
+            rows = w[g * K_PASS : (g + 1) * K_PASS, :]
+            nc.sync.dma_start(raw[name, g][:], rows.rearrange("(p j) c -> p j c", j=PACK))
 
-        def load_plane(table, name, t):
+        def load_plane(source, name, t):
             plane = tile("%s%d" % (name, t), [P, WINDOW], F32)
             if (name, t) == ("lb", PACK - 1):
-                nc.scalar.activation(plane[:, R:WINDOW], planes["ld", 0][:, R:WINDOW], COPY)
+                nc.scalar.activation(plane[:, R:WINDOW], table["ld", 0][:, R:WINDOW], COPY)
             else:
                 nc.gpsimd.memset(plane[:, R:WINDOW], 0.0)
-            nc.sync.dma_start(plane[:, 0:R], table.rearrange("(p t) r -> t p r", t=PACK)[t])
-            planes[name, t] = plane
+            nc.sync.dma_start(plane[:, 0:R], source.rearrange("(p t) r -> t p r", t=PACK)[t])
+            table[name, t] = plane
 
-        raw = {}
-        dealt = {}
-        weight = {}
-        planes = {}
+        def by_pairs(rows):
+            return rows[:].rearrange("p j (m h u) -> p h m j u", h=2, u=2)
 
         def round_weight(copy, name, g):
             label = "%s_%d_bf" % (name, g)
             dealt[name, g] = tile(label, [P, PACK * COLUMNS], BF16, tag=label)
-            copy(
-                dealt[name, g][:].rearrange("p (h u m j) -> p h m j u", h=2, u=2, j=PACK),
-                raw[name, g][:].rearrange("p j (m h u) -> p h m j u", h=2, u=2),
-            )
+            copy(dealt[name, g][:].rearrange("p (h u m j) -> p h m j u", h=2, u=2, j=PACK), by_pairs(raw[name, g]))
 
         def quantize_weight(name, g, **place):
             codes = tile("%s_%d_codes" % (name, g), [P, COLUMNS], U32, **place)
@@ -90,21 +99,24 @@ def tile_picked_yvera_none_po_kernel(
 
         xs_in = tile("xs_in", [P, T], U8)
         nc.vector.memset(xs_in[:].bitcast(I32), 0)
-        scale_rows = [(g, i) for i in range(4) for g in range(PASSES)]
 
-        def load_scales(lo, hi):
-            for g, i in scale_rows[lo:hi]:
-                nc.sync.dma_start(xs_in[4 * g + i : P : 32, :].bitcast(I32), x_scales[g, i:16:4, :].bitcast(I32))
+        def load_scales(*rows):
+            for i in rows:
+                for g in range(PASSES):
+                    nc.sync.dma_start(
+                        xs_in[SCALE_ROWS * g + i : P : QUADRANT, :].bitcast(I32),
+                        x_scales[g, i : SCALE_ROWS * P // QUADRANT : SCALE_ROWS, :].bitcast(I32),
+                    )
 
         load_plane(ld, "ld", 0)
         nc.sync.dma_start(ad_t[:], ad)
         load_plane(ld, "ld", 1)
         nc.sync.dma_start(offs_t[:], offs)
-        load_scales(0, 2)
+        load_scales(0)
         load_plane(ld, "ld", 2)
-        load_scales(2, 4)
+        load_scales(1)
         load_plane(ld, "ld", 3)
-        load_scales(4, 8)
+        load_scales(2, 3)
         load_weight(w1, 0, "w1")
         load_plane(lb, "lb", 1)
         x_in = [load_words(0)]
@@ -112,57 +124,54 @@ def tile_picked_yvera_none_po_kernel(
         load_weight(w1, 1, "w1")
         load_plane(lb, "lb", 3)
         x_in.append(load_words(1))
-        load_plane(lb, "lb", 0)
+        load_plane(lb, "lb", LATE_PLANE)
         load_weight(w2, 0, "w2")
         load_weight(w3, 0, "w3")
         load_weight(w3, 1, "w3")
 
         picked = {}
+        ld_picked = []
         for u in range(2):
-            whole = tile("ld_picked%d" % u, [P, PACK, HALF], F32)
-            picked["ld", u] = whole
+            ld_picked.append(tile("ld_picked%d" % u, [P, PACK, HALF], F32))
             for t in range(PACK):
-                picked["ld", u, t] = whole[:, t, :]
-                label = "lb_picked%d_%d" % (u, t)
-                if (u, t) != (1, 0):
+                picked["ld", u, t] = ld_picked[u][:, t, :]
+                if (u, t) != (1, LATE_PLANE):
+                    label = "lb_picked%d_%d" % (u, t)
                     picked["lb", u, t] = tile(label, [P, HALF], F32, tag=label)[:]
 
-        def look_up(name, t, lo, hi):
-            columns = planes[name, t][:].indirect(entries(ad_t, lo, hi))
-            if (name, t) == ("ld", 1) or (name, t, lo) == ("ld", 3, 0):
-                nc.vector.tensor_copy(picked[name, lo // HALF, t], columns)
+        def look_up(name, u, t):
+            columns = table[name, t][:].indirect(entries(ad_t, u * HALF, (u + 1) * HALF))
+            if (name, t) == ("ld", 1) or (name, u, t) == ("ld", 0, 3):
+                nc.vector.tensor_copy(picked[name, u, t], columns)
             else:
-                nc.scalar.activation(picked[name, lo // HALF, t], columns, COPY)
+                nc.scalar.activation(picked[name, u, t], columns, COPY)
 
         x_sc = tile("x_sc", [P, S], U8)
-        x_codes = {}
-
-        for g in range(PASSES):
-            x_codes[g] = tile("x%d_codes" % g, [P, S], U32)
+        x_codes = [tile("x%d_codes" % g, [P, S], U32) for g in range(PASSES)]
 
         def gather_words(g, lo, hi):
             nc.vector.tensor_copy(x_codes[g][:, lo:hi], x_in[g][:].bitcast(U32).indirect(entries(offs_t, lo, hi)))
 
-        def tokens(g, lo, hi):
-            return x_codes[g][:, lo:hi], x_sc[4 * g : P, lo:hi]
+        def tokens(lo, hi):
+            return [(x_codes[g][:, lo:hi], x_sc[SCALE_ROWS * g : P, lo:hi]) for g in range(PASSES)]
 
-        def take_bank(number, shape):
-            return psum.tile(shape, F32, name="bank%d" % number, tag="bank%d" % number, offset=number * BANK * 4)
-
-        def product(name, moving, bank, first, count):
+        def product(name, moving, number, planes, n):
+            bank = psum.tile(
+                [P, len(planes), n], F32, name="bank%d" % number, tag="bank%d" % number, offset=number * BANK * 4
+            )
             for g, (m_codes, m_scales) in enumerate(moving):
                 w_codes, w_scales = weight[name, g]
-                for u in range(count):
-                    t = first + u
+                for place, t in enumerate(planes):
                     nc.tensor.matmul_mx(
-                        out=bank[:, u, :],
+                        out=bank[:, place, :],
                         lhsT=w_codes[:, t * P : (t + 1) * P].bitcast(FP8X4),
                         lhsT_scale=w_scales[:, t * P : (t + 1) * P],
                         rhs=m_codes.bitcast(FP8X4),
                         rhs_scale=m_scales,
-                        start=(g == 0 and u == 0),
-                        stop=(g == len(moving) - 1 and u == count - 1),
+                        start=(g == 0 and place == 0),
+                        stop=(g == len(moving) - 1 and place == len(planes) - 1),
                     )
+            return bank
 
         def as_woven(ap):
             return ap.rearrange("p (a i t) -> p a t i", i=4, t=PACK)
@@ -175,16 +184,17 @@ def tile_picked_yvera_none_po_kernel(
         out_words = out_1[0].rearrange("p c r -> p (c r)").bitcast(I32)
 
         for t in range(PACK):
-            for lo in (0, HALF):
-                look_up("ld", t, lo, lo + HALF)
+            for u in range(2):
+                look_up("ld", u, t)
         nc.vector.tensor_copy(x_sc[:], xs_in[:].indirect(offs_t[:]))
         round_weight(nc.vector.tensor_copy, "w1", 0)
         quantize_weight("w1", 0)
-        ld_woven = tile("ld_woven", [P, H_ON_GPSIMD * PACK], F32)
+        ld_woven = {}
         for at in range(0, H_ON_GPSIMD, P):
+            ld_woven[at] = tile("ld_woven%d" % at, [P, P * PACK], F32, tag="w1_0_bf" if at > 0 else "ld_woven")
             nc.gpsimd.tensor_scalar(
-                ld_woven[:, at * PACK : (at + P) * PACK].rearrange("p (n t) -> p n t", t=PACK),
-                picked["ld", 0][:, :, at : at + P].rearrange("p t n -> p n t"),
+                ld_woven[at][:].rearrange("p (n t) -> p n t", t=PACK),
+                ld_picked[0][:, :, at : at + P].rearrange("p t n -> p n t"),
                 1.0,
                 0.0,
                 MULT,
@@ -195,38 +205,30 @@ def tile_picked_yvera_none_po_kernel(
         round_weight(nc.vector.tensor_copy, "w1", 1)
         quantize_weight("w1", 1)
         for t in range(1, PACK):
-            for lo in (0, HALF):
-                look_up("lb", t, lo, lo + HALF)
-        look_up("lb", 0, 0, HALF)
+            for u in range(2):
+                look_up("lb", u, t)
+        look_up("lb", 0, LATE_PLANE)
         gather_words(1, 0, P)
         gather_words(1, P, HALF)
         gather_words(1, HALF, S)
 
-        pieces = ((0, HALF), (HALF, S - P), (S - P, S))
         h_bf = {}
         h_codes = [tile("h_codes0", [P, HALF], U32)]
         h_scales = [tile("h_scales%d" % u, [P, HALF], U8) for u in range(2)]
 
         def form_h(at):
-            bank = take_bank(Y_BANKS[at // P], [P, PACK, P])
-            product("w1", [tokens(g, at, at + P) for g in range(PASSES)], bank, 0, PACK)
-            c = at % HALF
-            ((lo, hi),) = [(lo, hi) for lo, hi in pieces if lo <= at < hi]
+            bank = product("w1", tokens(at, at + P), Y_BANKS[at // P], range(PACK), P)
+            ((lo, hi),) = [(lo, hi) for lo, hi in H_PIECES if lo <= at < hi]
             if at == lo:
                 h_bf[lo] = tile("h_bf%d" % lo, [P, (hi - lo) * PACK], BF16, tag="w2_0_bf" if hi == S else "h_bf%d" % lo)
+            h = h_bf[lo][:, (at - lo) * PACK : (at - lo + P) * PACK]
             if at < H_ON_GPSIMD:
                 y_woven = tile("y_woven%d" % at, [P, P * PACK], F32, tag="y_woven%d" % at)
                 nc.scalar.copy(y_woven[:].rearrange("p (n t) -> p n t", t=PACK), bank[:].rearrange("p t n -> p n t"))
-                nc.gpsimd.tensor_tensor(
-                    h_bf[0][:, c * PACK : (c + P) * PACK], y_woven[:], ld_woven[:, c * PACK : (c + P) * PACK], MULT
-                )
-                return
-            nc.vector.tensor_tensor(
-                as_woven(h_bf[lo][:, (at - lo) * PACK : (at - lo + P) * PACK]),
-                as_planes(bank[:]),
-                as_planes(picked["ld", at // HALF][:, :, c : c + P]),
-                MULT,
-            )
+                nc.gpsimd.tensor_tensor(h, y_woven[:], ld_woven[at][:], MULT)
+            else:
+                scale = ld_picked[at // HALF][:, :, at % HALF : at % HALF + P]
+                nc.vector.tensor_tensor(as_woven(h), as_planes(bank[:]), as_planes(scale), MULT)
 
         def quantize_h(lo, hi):
             u, columns = lo // HALF, slice(lo % HALF, lo % HALF + hi - lo)
@@ -237,14 +239,12 @@ def tile_picked_yvera_none_po_kernel(
         term = {}
 
         def form_term(u, t, rr=None):
-            bank = take_bank(RR_BANKS[u][t], [P, 1, HALF])
-            product("w2", [(h_codes[u][:], h_scales[u][:])], bank, t, 1)
-            scaled = term[u, t]
+            bank = product("w2", [(h_codes[u][:], h_scales[u][:])], RR_BANKS[u][t], [t], HALF)
             if rr is not None:
                 nc.scalar.copy(rr, bank[:, 0, :])
-                nc.gpsimd.tensor_tensor(scaled, rr, picked["lb", u, t], MULT)
+                nc.gpsimd.tensor_tensor(term[u, t], rr, picked["lb", u, t], MULT)
             else:
-                nc.vector.tensor_tensor(scaled, bank[:, 0, :], picked["lb", u, t], MULT)
+                nc.vector.tensor_tensor(term[u, t], bank[:, 0, :], picked["lb", u, t], MULT)
 
         for at in range(0, H_ON_GPSIMD, P):
             form_h(at)
@@ -252,99 +252,95 @@ def tile_picked_yvera_none_po_kernel(
         for at in range(H_ON_GPSIMD, S - P, P):
             form_h(at)
         quantize_weight("w2", 0, tag="y_woven%d" % (H_ON_GPSIMD - P))
-        quantize_h(*pieces[0])
+        quantize_h(*H_PIECES[0])
         form_h(S - P)
         h_codes.append(tile("h_codes1", [P, HALF], U32, tag="w2_0_raw"))
-        quantize_h(*pieces[1])
-        quantize_h(*pieces[2])
+        quantize_h(*H_PIECES[1])
+        quantize_h(*H_PIECES[2])
+
         round_weight(nc.scalar.copy, "w3", 0)
         quantize_weight("w3", 0)
         early = tile("terms_early", [P, PACK, HALF], F32, tag="w3_0_bf")
         for t in range(PACK):
             term[0, t] = early[:, t, :]
-        rr_early = tile("rr_early", [P, HALF], F32, tag="w3_0_raw")
-        form_term(0, 3, rr_early[:])
-        for t in range(PACK - 1):
+        form_term(0, GPSIMD_PLANE, tile("rr_early", [P, HALF], F32, tag="w3_0_raw")[:])
+        for t in range(GPSIMD_PLANE):
             form_term(0, t)
         codes = tile("w3_1_codes", [P, COLUMNS], U32, tag="lb_picked0_1")
         scales = tile("w3_1_scales", [P, COLUMNS], U8)
         pairs = [tile("w3_1_pair%d" % h, [P, 2 * COLUMNS], BF16, tag="w3_1_pair%d" % h) for h in range(2)]
         for h in (1, 0):
-            nc.scalar.copy(
-                pairs[h][:].rearrange("p (u m j) -> p m j u", u=2, j=PACK),
-                raw["w3", 1][:].rearrange("p j (m h u) -> p h m j u", h=2, u=2)[:, h],
-            )
+            nc.scalar.copy(pairs[h][:].rearrange("p (u m j) -> p m j u", u=2, j=PACK), by_pairs(raw["w3", 1])[:, h])
         for h in (1, 0):
             columns = slice(h * 2 * P, (h + 1) * 2 * P)
             nc.vector.quantize_mx(out=codes[:, columns].bitcast(FP8X4), scales=scales[:, columns], in_=pairs[h][:])
         weight["w3", 1] = (codes, scales)
-        rr_late = tile("late_on_scalar", [P, 2, HALF], F32, tag="w3_1_raw")
+
         on_vector = tile("terms_vector", [P, 2, HALF], F32, tag="w3_1_pair1")
-        on_gpsimd = tile("terms_gpsimd", [P, 2, HALF], F32, tag="w3_1_pair0")
+        behind_codes = tile("behind_codes", [P, 3, HALF], F32, tag="w3_1_pair0")
         for t in range(PACK):
-            term[1, t] = (on_vector, on_gpsimd)[t // 2][:, t % 2, :]
-        form_term(1, 3, rr_late[:, 1, :])
-        picked["lb", 1, 0] = rr_late[:, 0, :]
-        look_up("lb", 0, HALF, S)
+            term[1, t] = (on_vector, behind_codes)[t // 2][:, t % 2, :]
+        picked["lb", 1, LATE_PLANE] = behind_codes[:, 2, :]
+        form_term(1, GPSIMD_PLANE, tile("rr_late", [P, HALF], F32, tag="w3_1_raw")[:])
         form_term(1, 1)
 
         result = [tile("result%d" % u, [P, PACK, HALF], F32) for u in range(2)]
 
-        def total(u, t, number, a=0, b=HALF):
-            lo = u * HALF
-            bank = take_bank(number, [P, 1, b - a])
-            product("w3", [tokens(g, lo + a, lo + b) for g in range(PASSES)], bank, t, 1)
-            if t == PACK - 1 and a == 0:
+        def total(u, t, number, a=0, b=HALF, on_gpsimd=False):
+            bank = product("w3", tokens(u * HALF + a, u * HALF + b), number, [t], b - a)
+            if on_gpsimd:
                 ee = tile("ee%d" % u, [P, b - a], F32, tag="ee%d" % u)
                 nc.scalar.copy(ee[:], bank[:, 0, :])
                 nc.gpsimd.tensor_tensor(result[u][:, t, a:b], ee[:], term[u, t][:, a:b], ADD)
             else:
                 nc.vector.tensor_tensor(result[u][:, t, a:b], bank[:, 0, :], term[u, t][:, a:b], ADD)
 
-        def store(u, first, count):
-            ts, columns = slice(first, first + count), slice(u * HALF, (u + 1) * HALF)
-            nc.sync.dma_start(out_rows[:, ts, columns], result[u][:, ts, :])
+        def store(u, first, count=1):
+            ts = slice(first, first + count)
+            nc.sync.dma_start(out_rows[:, ts, u * HALF : (u + 1) * HALF], result[u][:, ts, :])
 
         woven = {}
 
-        def round_out(copy, lo, hi):
-            woven[lo] = tile("o_bf%d" % lo, [P, (hi - lo) * PACK], BF16)
-            copy(as_woven(woven[lo][:]), as_planes(result[lo // HALF][:, :, lo % HALF : lo % HALF + hi - lo]))
+        def round_out(copy, lo):
+            woven[lo] = tile("o_bf%d" % lo, [P, QUARTER * PACK], BF16)
+            copy(as_woven(woven[lo][:]), as_planes(result[lo // HALF][:, :, lo % HALF : lo % HALF + QUARTER]))
 
-        def quantize_out(lo, hi):
-            nc.vector.quantize_mx(out=out_codes[:, lo:hi].bitcast(FP8X4), scales=out_scales[:, lo:hi], in_=woven[lo][:])
+        def quantize_out(lo):
+            columns = slice(lo, lo + QUARTER)
+            nc.vector.quantize_mx(out=out_codes[:, columns].bitcast(FP8X4), scales=out_scales[:, columns], in_=woven[lo][:])
 
         def store_words(lo, hi):
             nc.sync.dma_start(out_words[:, lo:hi], out_codes[:, lo:hi].bitcast(I32))
 
-        last = S - QUARTER
-        total(0, 3, 3)
+        total(0, GPSIMD_PLANE, EE_BANKS[0][GPSIMD_PLANE], on_gpsimd=True)
+        look_up("lb", 1, LATE_PLANE)
         for t in (2, 0, 1):
-            total(0, t, 5 + t)
-        for t in (2, 0, 1, 3):
-            store(0, t, 1)
-        form_term(1, 2, tile("rr1_2", [P, HALF], F32)[:])
-        form_term(1, 0)
-        total(1, 3, 4, 0, QUARTER)
-        total(1, 3, 5, QUARTER, HALF)
-        for t, number in ((1, 0), (0, 2), (2, 1)):
-            total(1, t, number)
-        store(1, 1, 1)
-        store(1, 0, 1)
+            total(0, t, EE_BANKS[0][t])
+        for t in (2, 0, 1, GPSIMD_PLANE):
+            store(0, t)
+        form_term(1, 2, tile("rr_last", [P, HALF], F32)[:])
+        form_term(1, LATE_PLANE)
+        total(1, GPSIMD_PLANE, EE_BANKS[1][GPSIMD_PLANE], 0, QUARTER, on_gpsimd=True)
+        total(1, GPSIMD_PLANE, EE_LAST_BANK, QUARTER, HALF)
+        for t in (1, 0, 2):
+            total(1, t, EE_BANKS[1][t])
+        store(1, 1)
+        store(1, 0)
         store(1, 2, 2)
+
         out_codes = tile("out_codes", [P, S], U32, tag="ee1")
         for lo in (0, QUARTER, HALF):
-            round_out(nc.scalar.copy, lo, lo + QUARTER)
-        quantize_out(0, QUARTER)
-        round_out(nc.vector.tensor_copy, last, S)
-        quantize_out(QUARTER, HALF)
+            round_out(nc.scalar.copy, lo)
+        quantize_out(0)
+        round_out(nc.vector.tensor_copy, LAST)
+        quantize_out(QUARTER)
         store_words(0, HALF)
-        quantize_out(last, S)
-        store_words(last, S)
-        quantize_out(HALF, last)
-        store_words(HALF, last)
-        for q in range(4):
+        for lo in (LAST, HALF):
+            quantize_out(lo)
+            store_words(lo, lo + QUARTER)
+        for q in range(P // QUADRANT):
             queue = nc.sync if q % 2 == 0 else nc.scalar
             queue.dma_start(
-                out_2[0, 4 * q : 4 * q + 4, :].bitcast(I32), out_scales[32 * q : 32 * q + 4, :].bitcast(I32)
+                out_2[0, SCALE_ROWS * q : SCALE_ROWS * (q + 1), :].bitcast(I32),
+                out_scales[QUADRANT * q : QUADRANT * q + SCALE_ROWS, :].bitcast(I32),
             )

@@ -47,6 +47,7 @@ def tile_picked_yvera_none_po_kernel(
     nc = tc.nc
     with ExitStack() as ctx:
         keep = ctx.enter_context(tc.tile_pool(name="keep", bufs=1))
+        reuse = ctx.enter_context(tc.tile_pool(name="reuse", bufs=1))
         psum = ctx.enter_context(tc.psum_pool(name="psum", bufs=1))
 
         offs_t = keep.tile([P, S // LIST_ROWS], U16, name="offs_t")
@@ -98,26 +99,23 @@ def tile_picked_yvera_none_po_kernel(
             weight[name, g] = (codes, scales)
 
         xs_in = tile("xs_in", [P, T], U8)
-        nc.vector.memset(xs_in[:].bitcast(I32), 0)
+        nc.gpsimd.memset(xs_in[:].bitcast(I32), 0)
 
-        def load_scales(*rows):
-            for i in rows:
-                for g in range(PASSES):
-                    nc.sync.dma_start(
-                        xs_in[SCALE_ROWS * g + i : P : QUADRANT, :].bitcast(I32),
-                        x_scales[g, i : SCALE_ROWS * P // QUADRANT : SCALE_ROWS, :].bitcast(I32),
-                    )
+        def load_scales(q):
+            nc.sync.dma_start(
+                xs_in[QUADRANT * q : QUADRANT * q + PASSES * SCALE_ROWS, :].bitcast(I32),
+                x_scales[:, SCALE_ROWS * q : SCALE_ROWS * (q + 1), :].bitcast(I32),
+            )
 
         load_plane(ld, "ld", 0)
         nc.sync.dma_start(ad_t[:], ad)
         load_plane(ld, "ld", 1)
-        nc.sync.dma_start(offs_t[:], offs)
-        load_scales(0)
         load_plane(ld, "ld", 2)
-        load_scales(1)
-        load_plane(ld, "ld", 3)
-        load_scales(2, 3)
+        for q in range(P // QUADRANT):
+            load_scales(q)
+        nc.sync.dma_start(offs_t[:], offs)
         load_weight(w1, 0, "w1")
+        load_plane(ld, "ld", 3)
         load_plane(lb, "lb", 1)
         x_in = [load_words(0)]
         load_plane(lb, "lb", 2)
@@ -141,13 +139,13 @@ def tile_picked_yvera_none_po_kernel(
 
         def look_up(name, u, t):
             columns = table[name, t][:].indirect(entries(ad_t, u * HALF, (u + 1) * HALF))
-            if (name, t) == ("ld", 1) or (name, u, t) == ("ld", 0, 3):
+            if (name, u) == ("ld", 1):
                 nc.vector.tensor_copy(picked[name, u, t], columns)
             else:
                 nc.scalar.activation(picked[name, u, t], columns, COPY)
 
         x_sc = tile("x_sc", [P, S], U8)
-        x_codes = [tile("x%d_codes" % g, [P, S], U32) for g in range(PASSES)]
+        x_codes = {1: tile("x1_codes", [P, S], U32)}
 
         def gather_words(g, lo, hi):
             nc.vector.tensor_copy(x_codes[g][:, lo:hi], x_in[g][:].bitcast(U32).indirect(entries(offs_t, lo, hi)))
@@ -187,19 +185,27 @@ def tile_picked_yvera_none_po_kernel(
             for u in range(2):
                 look_up("ld", u, t)
         nc.vector.tensor_copy(x_sc[:], xs_in[:].indirect(offs_t[:]))
-        round_weight(nc.vector.tensor_copy, "w1", 0)
+        dealt["w1", 0] = reuse.tile([P, PACK * COLUMNS], BF16, name="w1_0_bf", offset=2048, align_bytes=64)
+        nc.gpsimd.tensor_scalar(
+            dealt["w1", 0][:].rearrange("p (t m j) -> p m t j", t=PACK, j=PACK),
+            raw["w1", 0][:].rearrange("p j (m t) -> p m t j", t=PACK),
+            1.0,
+            0.0,
+            MULT,
+            ADD,
+        )
         quantize_weight("w1", 0)
-        ld_woven = {}
-        for at in range(0, H_ON_GPSIMD, P):
-            ld_woven[at] = tile("ld_woven%d" % at, [P, P * PACK], F32, tag="w1_0_bf" if at > 0 else "ld_woven")
-            nc.gpsimd.tensor_scalar(
-                ld_woven[at][:].rearrange("p (n t) -> p n t", t=PACK),
-                ld_picked[0][:, :, at : at + P].rearrange("p t n -> p n t"),
-                1.0,
-                0.0,
-                MULT,
-                ADD,
-            )
+        x_codes[0] = reuse.tile([P, S], U32, name="x0_codes", offset=0, align_bytes=64)
+        woven_ld = reuse.tile([P, H_ON_GPSIMD * PACK], F32, name="ld_woven", offset=4096, align_bytes=64)
+        nc.gpsimd.tensor_scalar(
+            woven_ld[:].rearrange("p (n t) -> p n t", t=PACK),
+            ld_picked[0][:, :, 0:H_ON_GPSIMD].rearrange("p t n -> p n t"),
+            1.0,
+            0.0,
+            MULT,
+            ADD,
+        )
+        ld_woven = {at: woven_ld[:, at * PACK : (at + P) * PACK] for at in range(0, H_ON_GPSIMD, P)}
         gather_words(0, 0, HALF)
         gather_words(0, HALF, S)
         round_weight(nc.vector.tensor_copy, "w1", 1)
@@ -225,7 +231,7 @@ def tile_picked_yvera_none_po_kernel(
             if at < H_ON_GPSIMD:
                 y_woven = tile("y_woven%d" % at, [P, P * PACK], F32, tag="y_woven%d" % at)
                 nc.scalar.copy(y_woven[:].rearrange("p (n t) -> p n t", t=PACK), bank[:].rearrange("p t n -> p n t"))
-                nc.gpsimd.tensor_tensor(h, y_woven[:], ld_woven[at][:], MULT)
+                nc.gpsimd.tensor_tensor(h, y_woven[:], ld_woven[at], MULT)
             else:
                 scale = ld_picked[at // HALF][:, :, at % HALF : at % HALF + P]
                 nc.vector.tensor_tensor(as_woven(h), as_planes(bank[:]), as_planes(scale), MULT)

from contextlib import ExitStack

import concourse.mybir as mybir

K, T, S, H, N, R = 1024, 2048, 1024, 512, 512, 512
FLOPS = 2 * S * (K * H + K * N + H * N)

F32 = mybir.dt.float32
BF16 = mybir.dt.bfloat16
I32 = mybir.dt.int32
U32 = mybir.dt.uint32
U16 = mybir.dt.uint16
U8 = mybir.dt.uint8
FP8X4 = mybir.dt.float8_e4m3fn_x4
MULT = mybir.AluOpType.mult
ADD = mybir.AluOpType.add
COPY = mybir.ActivationFunctionType.Copy

P = 128
PACK = 4
K_PASS = P * PACK
PASSES = K // K_PASS
COLUMNS = 512
LIST_ROWS = 16
QUADRANT = 32
SCALE_ROWS = 4
BANK = 512
HALF = S // 2
QUARTER = S // 4
LAST = S - QUARTER
SPARE = 32
WINDOW = R + SPARE
H_ON_GPSIMD = 256
GPSIMD_PLANE = PACK - 1
LATE_PLANE = 0
H_PIECES = ((0, HALF), (HALF, S - P), (S - P, S))

Y_BANKS = (0, 1, 2, 3, 4, 0, 1, 2)
RR_BANKS = ((5, 6, 7, 3), (1, 2, 3, 4))
EE_BANKS = ((5, 6, 7, 3), (2, 0, 1, 4))
EE_LAST_BANK = 5


def tile_picked_yvera_none_po_kernel(
    tc, x_words, x_scales, w1, w2, w3, ld, lb, offs, ad, out_0, out_1, out_2
):
    nc = tc.nc
    with ExitStack() as ctx:
        keep = ctx.enter_context(tc.tile_pool(name="keep", bufs=1))
        reuse = ctx.enter_context(tc.tile_pool(name="reuse", bufs=1))
        psum = ctx.enter_context(tc.psum_pool(name="psum", bufs=1))

        offs_t = keep.tile([P, S // LIST_ROWS], U16, name="offs_t")
        ad_t = keep.tile([P, S // LIST_ROWS], U16, name="ad_t")

        def entries(list_tile, lo, hi):
            return list_tile[:, lo // LIST_ROWS : hi // LIST_ROWS]

        def tile(name, shape, dtype, **place):
            return keep.tile(shape, dtype, name=name, align_bytes=64, **place)

        raw = {}
        dealt = {}
        weight = {}
        table = {}

        def load_words(g):
            words = tile("x_in%d" % g, [P, T], I32)
            nc.sync.dma_start(words[:], x_words[g].rearrange("p c r -> p (c r)").bitcast(I32))
            return words

        def load_weight(w, g, name):
            label = "%s_%d_raw" % (name, g)
            raw[name, g] = tile(label, [P, PACK, COLUMNS], F32, tag=label)
            rows = w[g * K_PASS : (g + 1) * K_PASS, :]
            nc.sync.dma_start(raw[name, g][:], rows.rearrange("(p j) c -> p j c", j=PACK))

        def load_plane(source, name, t):
            plane = tile("%s%d" % (name, t), [P, WINDOW], F32)
            if (name, t) == ("lb", PACK - 1):
                nc.scalar.activation(plane[:, R:WINDOW], table["ld", 0][:, R:WINDOW], COPY)
            else:
                nc.gpsimd.memset(plane[:, R:WINDOW], 0.0)
            nc.sync.dma_start(plane[:, 0:R], source.rearrange("(p t) r -> t p r", t=PACK)[t])
            table[name, t] = plane

        def by_pairs(rows):
            return rows[:].rearrange("p j (m h u) -> p h m j u", h=2, u=2)

        def round_weight(copy, name, g):
            label = "%s_%d_bf" % (name, g)
            dealt[name, g] = tile(label, [P, PACK * COLUMNS], BF16, tag=label)
            copy(dealt[name, g][:].rearrange("p (h u m j) -> p h m j u", h=2, u=2, j=PACK), by_pairs(raw[name, g]))

        def quantize_weight(name, g, **place):
            codes = tile("%s_%d_codes" % (name, g), [P, COLUMNS], U32, **place)
            scales = tile("%s_%d_scales" % (name, g), [P, COLUMNS], U8)
            nc.vector.quantize_mx(out=codes[:].bitcast(FP8X4), scales=scales[:], in_=dealt[name, g][:])
            weight[name, g] = (codes, scales)

        xs_in = tile("xs_in", [P, T], U8)
        nc.gpsimd.memset(xs_in[:].bitcast(I32), 0)

        def load_scales(q):
            nc.sync.dma_start(
                xs_in[QUADRANT * q : QUADRANT * q + PASSES * SCALE_ROWS, :].bitcast(I32),
                x_scales[:, SCALE_ROWS * q : SCALE_ROWS * (q + 1), :].bitcast(I32),
            )

        load_plane(ld, "ld", 0)
        nc.sync.dma_start(ad_t[:], ad)
        load_plane(ld, "ld", 1)
        load_plane(ld, "ld", 2)
        for q in range(P // QUADRANT):
            load_scales(q)
        nc.sync.dma_start(offs_t[:], offs)
        load_weight(w1, 0, "w1")
        load_plane(ld, "ld", 3)
        load_plane(lb, "lb", 1)
        x_in = [load_words(0)]
        load_plane(lb, "lb", 2)
        load_weight(w1, 1, "w1")
        load_plane(lb, "lb", 3)
        x_in.append(load_words(1))
        load_plane(lb, "lb", LATE_PLANE)
        load_weight(w2, 0, "w2")
        load_weight(w3, 0, "w3")
        load_weight(w3, 1, "w3")

        picked = {}
        ld_picked = []
        for u in range(2):
            ld_picked.append(tile("ld_picked%d" % u, [P, PACK, HALF], F32))
            for t in range(PACK):
                picked["ld", u, t] = ld_picked[u][:, t, :]
                if (u, t) != (1, LATE_PLANE):
                    label = "lb_picked%d_%d" % (u, t)
                    picked["lb", u, t] = tile(label, [P, HALF], F32, tag=label)[:]

        def look_up(name, u, t):
            columns = table[name, t][:].indirect(entries(ad_t, u * HALF, (u + 1) * HALF))
            if (name, u) == ("ld", 1):
                nc.vector.tensor_copy(picked[name, u, t], columns)
            else:
                nc.scalar.activation(picked[name, u, t], columns, COPY)

        x_sc = tile("x_sc", [P, S], U8)
        x_codes = {1: tile("x1_codes", [P, S], U32)}

        def gather_words(g, lo, hi):
            nc.vector.tensor_copy(x_codes[g][:, lo:hi], x_in[g][:].bitcast(U32).indirect(entries(offs_t, lo, hi)))

        def tokens(lo, hi):
            return [(x_codes[g][:, lo:hi], x_sc[SCALE_ROWS * g : P, lo:hi]) for g in range(PASSES)]

        def product(name, moving, number, planes, n):
            bank = psum.tile(
                [P, len(planes), n], F32, name="bank%d" % number, tag="bank%d" % number, offset=number * BANK * 4
            )
            for g, (m_codes, m_scales) in enumerate(moving):
                w_codes, w_scales = weight[name, g]
                for place, t in enumerate(planes):
                    nc.tensor.matmul_mx(
                        out=bank[:, place, :],
                        lhsT=w_codes[:, t * P : (t + 1) * P].bitcast(FP8X4),
                        lhsT_scale=w_scales[:, t * P : (t + 1) * P],
                        rhs=m_codes.bitcast(FP8X4),
                        rhs_scale=m_scales,
                        start=(g == 0 and place == 0),
                        stop=(g == len(moving) - 1 and place == len(planes) - 1),
                    )
            return bank

        def as_woven(ap):
            return ap.rearrange("p (a i t) -> p a t i", i=4, t=PACK)

        def as_planes(ap):
            return ap.rearrange("p t (a i) -> p a t i", i=4)

        out_scales = tile("out_scales", [P, S], U8)
        out_rows = out_0.rearrange("(p t) s -> p t s", t=PACK)
        out_words = out_1[0].rearrange("p c r -> p (c r)").bitcast(I32)

        for t in range(PACK):
            for u in range(2):
                look_up("ld", u, t)
        nc.vector.tensor_copy(x_sc[:], xs_in[:].indirect(offs_t[:]))
        dealt["w1", 0] = reuse.tile([P, PACK * COLUMNS], BF16, name="w1_0_bf", offset=2048, align_bytes=64)
        nc.gpsimd.tensor_scalar(
            dealt["w1", 0][:].rearrange("p (t m j) -> p m t j", t=PACK, j=PACK),
            raw["w1", 0][:].rearrange("p j (m t) -> p m t j", t=PACK),
            1.0,
            0.0,
            MULT,
            ADD,
        )
        quantize_weight("w1", 0)
        x_codes[0] = reuse.tile([P, S], U32, name="x0_codes", offset=0, align_bytes=64)
        woven_ld = reuse.tile([P, H_ON_GPSIMD * PACK], F32, name="ld_woven", offset=4096, align_bytes=64)
        nc.gpsimd.tensor_scalar(
            woven_ld[:].rearrange("p (n t) -> p n t", t=PACK),
            ld_picked[0][:, :, 0:H_ON_GPSIMD].rearrange("p t n -> p n t"),
            1.0,
            0.0,
            MULT,
            ADD,
        )
        ld_woven = {at: woven_ld[:, at * PACK : (at + P) * PACK] for at in range(0, H_ON_GPSIMD, P)}
        gather_words(0, 0, HALF)
        gather_words(0, HALF, S)
        round_weight(nc.vector.tensor_copy, "w1", 1)
        quantize_weight("w1", 1)
        for t in range(1, PACK):
            for u in range(2):
                look_up("lb", u, t)
        look_up("lb", 0, LATE_PLANE)
        gather_words(1, 0, P)
        gather_words(1, P, HALF)
        gather_words(1, HALF, S)

        h_bf = {}
        h_codes = [tile("h_codes0", [P, HALF], U32)]
        h_scales = [tile("h_scales%d" % u, [P, HALF], U8) for u in range(2)]

        def form_h(at):
            bank = product("w1", tokens(at, at + P), Y_BANKS[at // P], range(PACK), P)
            ((lo, hi),) = [(lo, hi) for lo, hi in H_PIECES if lo <= at < hi]
            if at == lo:
                h_bf[lo] = tile("h_bf%d" % lo, [P, (hi - lo) * PACK], BF16, tag="w2_0_bf" if hi == S else "h_bf%d" % lo)
            h = h_bf[lo][:, (at - lo) * PACK : (at - lo + P) * PACK]
            if at < H_ON_GPSIMD:
                y_woven = tile("y_woven%d" % at, [P, P * PACK], F32, tag="y_woven%d" % at)
                nc.scalar.copy(y_woven[:].rearrange("p (n t) -> p n t", t=PACK), bank[:].rearrange("p t n -> p n t"))
                nc.gpsimd.tensor_tensor(h, y_woven[:], ld_woven[at], MULT)
            else:
                scale = ld_picked[at // HALF][:, :, at % HALF : at % HALF + P]
                nc.vector.tensor_tensor(as_woven(h), as_planes(bank[:]), as_planes(scale), MULT)

        def quantize_h(lo, hi):
            u, columns = lo // HALF, slice(lo % HALF, lo % HALF + hi - lo)
            nc.vector.quantize_mx(
                out=h_codes[u][:, columns].bitcast(FP8X4), scales=h_scales[u][:, columns], in_=h_bf[lo][:]
            )

        term = {}

        def form_term(u, t, rr=None):
            bank = product("w2", [(h_codes[u][:], h_scales[u][:])], RR_BANKS[u][t], [t], HALF)
            if rr is not None:
                nc.scalar.copy(rr, bank[:, 0, :])
                nc.gpsimd.tensor_tensor(term[u, t], rr, picked["lb", u, t], MULT)
            else:
                nc.vector.tensor_tensor(term[u, t], bank[:, 0, :], picked["lb", u, t], MULT)

        for at in range(0, H_ON_GPSIMD, P):
            form_h(at)
        round_weight(nc.scalar.copy, "w2", 0)
        for at in range(H_ON_GPSIMD, S - P, P):
            form_h(at)
        quantize_weight("w2", 0, tag="y_woven%d" % (H_ON_GPSIMD - P))
        quantize_h(*H_PIECES[0])
        form_h(S - P)
        h_codes.append(tile("h_codes1", [P, HALF], U32, tag="w2_0_raw"))
        quantize_h(*H_PIECES[1])
        quantize_h(*H_PIECES[2])

        round_weight(nc.scalar.copy, "w3", 0)
        quantize_weight("w3", 0)
        early = tile("terms_early", [P, PACK, HALF], F32, tag="w3_0_bf")
        for t in range(PACK):
            term[0, t] = early[:, t, :]
        form_term(0, GPSIMD_PLANE, tile("rr_early", [P, HALF], F32, tag="w3_0_raw")[:])
        for t in range(GPSIMD_PLANE):
            form_term(0, t)
        codes = tile("w3_1_codes", [P, COLUMNS], U32, tag="lb_picked0_1")
        scales = tile("w3_1_scales", [P, COLUMNS], U8)
        pairs = [tile("w3_1_pair%d" % h, [P, 2 * COLUMNS], BF16, tag="w3_1_pair%d" % h) for h in range(2)]
        for h in (1, 0):
            nc.scalar.copy(pairs[h][:].rearrange("p (u m j) -> p m j u", u=2, j=PACK), by_pairs(raw["w3", 1])[:, h])
        for h in (1, 0):
            columns = slice(h * 2 * P, (h + 1) * 2 * P)
            nc.vector.quantize_mx(out=codes[:, columns].bitcast(FP8X4), scales=scales[:, columns], in_=pairs[h][:])
        weight["w3", 1] = (codes, scales)

        on_vector = tile("terms_vector", [P, 2, HALF], F32, tag="w3_1_pair1")
        behind_codes = tile("behind_codes", [P, 3, HALF], F32, tag="w3_1_pair0")
        for t in range(PACK):
            term[1, t] = (on_vector, behind_codes)[t // 2][:, t % 2, :]
        picked["lb", 1, LATE_PLANE] = behind_codes[:, 2, :]
        form_term(1, GPSIMD_PLANE, tile("rr_late", [P, HALF], F32, tag="w3_1_raw")[:])
        form_term(1, 1)

        result = [tile("result%d" % u, [P, PACK, HALF], F32) for u in range(2)]

        def total(u, t, number, a=0, b=HALF, on_gpsimd=False):
            bank = product("w3", tokens(u * HALF + a, u * HALF + b), number, [t], b - a)
            if on_gpsimd:
                ee = tile("ee%d" % u, [P, b - a], F32, tag="ee%d" % u)
                nc.scalar.copy(ee[:], bank[:, 0, :])
                nc.gpsimd.tensor_tensor(result[u][:, t, a:b], ee[:], term[u, t][:, a:b], ADD)
            else:
                nc.vector.tensor_tensor(result[u][:, t, a:b], bank[:, 0, :], term[u, t][:, a:b], ADD)

        def store(u, first, count=1):
            ts = slice(first, first + count)
            nc.sync.dma_start(out_rows[:, ts, u * HALF : (u + 1) * HALF], result[u][:, ts, :])

        woven = {}

        def round_out(copy, lo):
            woven[lo] = tile("o_bf%d" % lo, [P, QUARTER * PACK], BF16)
            copy(as_woven(woven[lo][:]), as_planes(result[lo // HALF][:, :, lo % HALF : lo % HALF + QUARTER]))

        def quantize_out(lo):
            columns = slice(lo, lo + QUARTER)
            nc.vector.quantize_mx(out=out_codes[:, columns].bitcast(FP8X4), scales=out_scales[:, columns], in_=woven[lo][:])

        def store_words(lo, hi):
            nc.sync.dma_start(out_words[:, lo:hi], out_codes[:, lo:hi].bitcast(I32))

        total(0, GPSIMD_PLANE, EE_BANKS[0][GPSIMD_PLANE], on_gpsimd=True)
        look_up("lb", 1, LATE_PLANE)
        for t in (2, 0, 1):
            total(0, t, EE_BANKS[0][t])
        for t in (2, 0, 1, GPSIMD_PLANE):
            store(0, t)
        form_term(1, 2, tile("rr_last", [P, HALF], F32)[:])
        form_term(1, LATE_PLANE)
        total(1, GPSIMD_PLANE, EE_BANKS[1][GPSIMD_PLANE], 0, QUARTER, on_gpsimd=True)
        total(1, GPSIMD_PLANE, EE_LAST_BANK, QUARTER, HALF)
        for t in (1, 0, 2):
            total(1, t, EE_BANKS[1][t])
        store(1, 1)
        store(1, 0)
        store(1, 2, 2)

        out_codes = tile("out_codes", [P, S], U32, tag="ee1")
        for lo in (0, QUARTER, HALF):
            round_out(nc.scalar.copy, lo)
        quantize_out(0)
        round_out(nc.vector.tensor_copy, LAST)
        quantize_out(QUARTER)
        store_words(0, HALF)
        for lo in (LAST, HALF):
            quantize_out(lo)
            store_words(lo, lo + QUARTER)
        for q in range(P // QUADRANT):
            queue = nc.sync if q % 2 == 0 else nc.scalar
            queue.dma_start(
                out_2[0, SCALE_ROWS * q : SCALE_ROWS * (q + 1), :].bitcast(I32),
                out_scales[QUADRANT * q : QUADRANT * q + SCALE_ROWS, :].bitcast(I32),
            )
